import numpy as np, ml_dtypes
CORES = [35,38,43,46]
N = 4
import mx_ref
BF = ml_dtypes.bfloat16
def entries(a):
    return np.ascontiguousarray(a.T).reshape(-1)
def table(e):
    return np.ascontiguousarray(np.reshape(e, (-1, 16)).T).astype(np.int32)
def pick(q, e):
    c = np.concatenate([q[0].reshape(128, -1, 4), np.zeros((128, 1, 4), np.uint8)], axis=1); s = np.concatenate([q[1], np.ones((16, 1), np.uint8)], axis=1)
    return (np.ascontiguousarray(c[:, e].reshape(128, -1)), np.ascontiguousarray(s[:, e]))
def join(*qs):
    return (np.concatenate([q[0] for q in qs], axis=1), np.concatenate([q[1] for q in qs], axis=1))
def put(q, e, v):
    c, s = q[0].reshape(128, -1, 4).copy(), q[1].copy(); c[:, e] = v[0].reshape(128, -1, 4); s[:, e] = v[1]
    return (c.reshape(128, -1), s)
def pk(c, s):
    return (np.ascontiguousarray(c), mx_ref.live(s))
def emit(q):
    return q[0], q[1]
def cut(t, i, w=512):
    return t[:, w * i:w * i + w]
def f(rng, *shape):
    return mx_ref.flush((rng.standard_normal(shape, dtype=np.float32) * np.exp2(rng.integers(-2, 3, shape[:-1] + (1,)))).astype(BF))
def wide(rng, *shape, cols=0):
    v = rng.standard_normal(shape, dtype=np.float32) * np.exp2(rng.integers(-12, 13, shape)).astype(np.float32)
    if cols: v *= np.repeat(np.exp2(rng.integers(-cols, cols + 1, shape[:-2] + (1, shape[-1] // 4))) * (rng.random(shape[:-2] + (1, shape[-1] // 4)) > 0.0625), 4, axis=-1).astype(np.float32)
    return mx_ref.flush(v.astype(BF))
P, K, R, LC = 256, 48, 3, 96
def near(nb):
    return np.stack([entries(nb[r]).reshape(P, 3) for r in range(N)]).astype(np.int64)
def play(x, bb, nb, u, v, a):
    n = near(nb)
    X = join(*[mx_ref.quantize(np.ascontiguousarray(x[r])) for r in range(N)])
    qu, qv = mx_ref.quantize(np.ascontiguousarray(u[0])), mx_ref.quantize(np.ascontiguousarray(v[0]))
    qa = [[mx_ref.quantize(np.ascontiguousarray(cut(a[r], i))) for i in range(4)] for r in range(N)]
    fixed = [mx_ref.matmul(qv, mx_ref.quantize(np.ascontiguousarray(bb[r])))[0] for r in range(N)]
    b = bb.astype(np.float32).reshape(N, 128, P, 4)
    done, res, made = np.zeros((N, R, K), np.int64), [], []
    for t in range(R):
        e = mx_ref.matmul(qu, X)[0]
        new = []
        for r in range(N):
            z = ((e[n[r, :, 0]] + e[n[r, :, 1]]) + e[n[r, :, 2]]) - fixed[r]
            j = np.argsort(-np.abs(z), kind="stable")[:K]
            nbs = pick(X, n[r, j].T.reshape(-1))
            s = []
            for i in range(4):
                m = mx_ref.matmul(qa[r][i], nbs)
                s.append((m[:, :K] + m[:, K:2 * K]) + m[:, 2 * K:])
            g = np.float32(0.05) * np.stack(s, axis=2) + b[r][:, j]
            new.append(mx_ref.quantize(np.ascontiguousarray(g.reshape(128, -1).astype(BF))))
            done[r, t] = j
            res.append(z)
            made.append(g)
        X = put(X, np.concatenate([P * r + done[r, t] for r in range(N)]), join(*new))
    return X, done, np.stack(res), np.stack(made)
def fit(z, g):
    top = np.abs(g.astype(BF).astype(np.float32)).reshape(-1, 16, 8, K, 4).max(axis=(2, 4))
    g = np.abs(g)
    return bool(np.isfinite(z).all() and np.isfinite(g).all() and ((g == 0) | (g >= 2.0 ** -60) & (g <= 2.0 ** 60)).all() and ((top == 0) | (top >= 2.0 ** -30) & (top <= 2.0 ** 30)).all())
def bf(v):
    return mx_ref.flush(np.asarray(v, np.float32).astype(BF))
def lone(c):
    t = np.zeros((N, 128, 512), BF)
    t[:, :, :4] = c
    return t
def few(rng, q, n, free, most):
    p = rng.permutation(free)[:most]
    return q * P + rng.permutation(np.concatenate([p, p[rng.integers(0, p.size, P)]])[:n])
def graph(rng, src=None, free=None, most=LC):
    n = np.zeros((N, P, 3), np.int64)
    if free is None: free = [np.arange(P)] * N
    for r in range(N):
        n[r, :, :2] = r * P + rng.choice(free[r], (P, 2))
        s = (r + rng.integers(1, N, P)) % N if src is None else np.full(P, src[r])
        for q in range(N):
            i = np.flatnonzero(s == q)
            n[r, i, 2] = few(rng, q, i.size, free[q], most)
    return n
def stored(n):
    return np.stack([table(n[r].reshape(-1)) for r in range(N)])
def setup_inputs(rng):
    return {"x": f(rng, N, 128, 4 * P), "bb": f(rng, N, 128, 4 * P), "nb": stored(graph(rng)), "u": lone(f(rng, 128, 4)), "v": lone(f(rng, 128, 4)),
            "a": bf(f(rng, N, 128, 2048).astype(np.float32) * np.float32(2.0 ** -4)), "w": f(rng, N, 128, 512)}
def signs(rng):
    return 1.0 - 2.0 * rng.integers(0, 2, (128, 4))
def signed(rng, sg, size):
    return bf(((1 + rng.random((N, 128, P, 4))) * size[:, None, :, None] * sg[:, None, :] + 0.0).reshape(N, 128, 4 * P))
def single(rng, sg, size):
    return lone(bf((1 + rng.random((128, 4))) * sg * size))
def setup_inputs_again(rng):
    d, sg, size, m = setup_inputs(rng), signs(rng), np.zeros((N, P)), K // 8
    o = np.stack([rng.permutation(P) for r in range(N)])
    rest = np.sort(o[:, 7 * m:], axis=1)
    hold = np.stack([rng.permutation(rest[r, -5:]) for r in range(N)])
    n = graph(rng, free=rest[:, :-5], most=LC - 2)
    large, small = (1 + rng.random((128, 4))) * sg * 2.0 ** 20, (1 + rng.random((128, 4))) * sg * 2.0 ** -8
    top = np.arange(128)[:, None] < 64
    five = np.stack([large * top, large * ~top, -large, large, small], axis=1) + 0.0
    x = np.zeros((N, 128, P, 4))
    for r in range(N):
        x[r][:, hold[r]] = five
        h, left, both, alone = o[r, :4 * m], o[r, 4 * m:5 * m], o[r, 5 * m:6 * m], o[r, 6 * m:7 * m]
        size[r, h] = 64
        size[r, left] = 64
        n[r, h, 0] = r * P + rng.permutation(h)
        n[r, left, 0], n[r, left, 1] = r * P + hold[r, 0], r * P + hold[r, 1]
        n[r, both, 0], n[r, both, 1] = r * P + hold[r, 3], r * P + hold[r, 2]
        for i, k in ((left, 2), (both, 4), (alone, 4)):
            q = n[r, i, 2] // P
            n[r, i, 2] = q * P + hold[q, k]
    bb = signed(rng, sg, size).reshape(N, 128, P, 4)
    for r in range(N): bb[r][8:, o[r, 4 * m:5 * m]] = 0
    d.update(x=bf(x.reshape(N, 128, 4 * P)), bb=bb.reshape(N, 128, 4 * P), nb=stored(n), u=single(rng, sg, 1.0), v=single(rng, sg, 4.0))
    return d
def setup_inputs_far(rng):
    h = int(rng.integers(0, N))
    src = np.full(N, h)
    src[h] = (h + int(rng.integers(1, N))) % N
    d, n, sg, size = setup_inputs(rng), graph(rng, src), signs(rng), np.full((N, P), 2.0 ** 20)
    for r in range(N):
        first = np.unique(n[r, :, 2], return_index=True)[1]
        size[r, rng.permutation(first)[:K]] = 2.0 ** 26
    d.update(x=signed(rng, sg, np.full((N, P), 2.0 ** 20)), bb=signed(rng, sg, size), nb=stored(n), u=single(rng, sg, 2.0 ** 23), v=single(rng, sg, 2.0 ** 29))
    return d
def setup_inputs_moved(rng):
    d, n, sg, size = setup_inputs(rng), np.zeros((N, P, 3), np.int64), signs(rng), np.full((N, P), 2.0 ** -4)
    o = [rng.permutation(P) for r in range(N)]
    for r in range(N):
        size[r, o[r][:K]] = 64
        n[r, :, :2] = r * P + rng.choice(o[r][K:], (P, 2))
        m = np.zeros(P, bool)
        m[rng.permutation(P)[:K + K // 2]] = True
        s = (r + rng.integers(1, N, P)) % N
        for q in range(N):
            hot, cold = rng.permutation(o[q][:K])[:LC // 2], rng.permutation(o[q][K:])[:LC - LC // 2]
            i, k = np.flatnonzero((s == q) & m), np.flatnonzero((s == q) & ~m)
            n[r, i, 2] = q * P + rng.choice(hot, i.size)
            n[r, k, 2] = q * P + rng.choice(cold, k.size)
    d.update(x=signed(rng, sg, np.full((N, P), 2.0 ** -6)), bb=signed(rng, sg, size), nb=stored(n), u=single(rng, sg, 16.0), v=single(rng, sg, 1.0))
    return d
def setup_inputs_spread(rng):
    d = setup_inputs(rng)
    d["x"] = wide(rng, N, 128, 4 * P, cols=4)
    d["bb"] = wide(rng, N, 128, 4 * P, cols=4)
    return d
def setup_inputs_ties(rng):
    d, n = setup_inputs(rng), np.zeros((N, P, 3), np.int64)
    kind = np.stack([rng.permutation(np.arange(P) % 4) for r in range(N)])
    for k in ("x", "bb"):
        c = f(rng, 128, 8).astype(np.float32).reshape(128, 2, 4)
        d[k] = np.stack([bf((c[:, kind[r] >> 1] * (1 - 2 * (kind[r] & 1))[None, :, None]).reshape(128, -1)) for r in range(N)])
    for r in range(N):
        s = (r + rng.integers(1, N, P)) % N
        for k in range(4):
            i = np.flatnonzero(kind[r] == k)
            n[r, i, 0] = r * P + rng.choice(i, i.size)
            n[r, i, 1] = r * P + rng.choice(np.flatnonzero(kind[r] == (k ^ 2)), i.size)
            for q in range(N):
                j = i[s[i] == q]
                n[r, j, 2] = q * P + rng.choice(rng.permutation(np.flatnonzero(kind[q] == k))[:LC // 4], j.size)
    d["nb"] = stored(n)
    return d
def check_inputs(d):
    b = []
    for k in ("x", "bb", "u", "v", "a", "w"):
        t = np.abs(d[k].astype(np.float32))
        if not (np.isfinite(t).all() and ((t == 0) | (t >= 2.0 ** -30) & (t <= 2.0 ** 30)).all()): b.append("a value of " + k)
    for k in ("u", "v"):
        t = d[k].astype(np.float32)
        if (t[:, :, 4:] != 0).any(): b.append(k + " has numbers behind its column 0")
        if (t != t[:1]).any(): b.append(k + " isn't the same on all ranks")
    n = near(d["nb"])
    at, own = n // P, np.arange(N)[:, None, None]
    if n.min() < 0 or n.max() >= N * P or (at[:, :, :2] != own).any() or (at[:, :, 2] == own[:, :, 0]).any(): b.append("nb")
    elif any(np.unique(n[r, :, 2][at[r, :, 2] == q]).size > LC for r in range(N) for q in range(N)): b.append("nb names too many columns of one rank")
    if not b:
        try:
            with np.errstate(all="ignore"):
                X, done, z, g = play(d["x"], d["bb"], d["nb"], d["u"], d["v"], d["a"])
                good = fit(z, g)
        except Exception:
            good = False
        if not good: b.append("a number that the rounds make")
    return b
def reference(x, bb, nb, u, v, a, w):
    X, done, z, g = play(x, bb, nb, u, v, a)
    oc, osc, y = np.zeros((N, 128, 4 * P), np.uint8), np.zeros((N, 16, P), np.uint8), np.zeros((N, 128, P), np.float32)
    for r in range(N):
        q = pick(X, np.arange(P * r, P * r + P))
        oc[r], osc[r] = emit(q)
        y[r] = mx_ref.matmul(mx_ref.quantize(np.ascontiguousarray(w[r])), q)
    return {"oc": oc, "osc": osc, "nd": done.astype(np.float32), "y": y}

@@ -1,0 +1,442 @@
+from concourse.bass import DstId, RemoteDMATransfer
+from concourse.mybir import AluOpType as OP, AxisListType, ActivationFunctionType as AF, dt
+
+P, K, R, LC = 256, 48, 3, 96
+FAR = P
+ARR = [FAR + 3 * LC, FAR + 3 * LC + 3 * K + 128]
+OWN = [ARR[0] + 3 * K, ARR[1] + 3 * K, ARR[1] + 3 * K + 128]
+WC = OWN[2] + 128
+TINY = 2.0 ** -120
+PRED = 1.0 - 2.0 ** -24
+STEP = 4096.0
+
+BUF = {
+    "float32": "ID:%d C32:8 C16:16 tf:8 GCOL:8 JROW:64 IC:16 ICS:8 TB:4 Fm:128 Ft:128 CK:32 C1:32 PADD:1 SLf:256 LJ:512 LS:2 M:1024 ec:2 E0:1024 E1:%d fb:64 PC:192 PJ:192 PD:384 PT:384 EG:192 z1:64 z2:64 z3:64 z4:64 zr:64 ZT:64 zB:64 zr0:64 Zc:320 KB:64 KEY:256 DK:768 R0:14 RX:14 R1:14 RY:14 Rf0:14 Rf1:14 Rf2:14 S0:192 S1:192 S2:192 S3:192 FD:512 FT:512 ys:256" % (WC, OWN[2]),
+    "bfloat16": "JCOL:2 ZB:256 xt:1024 bt:1024 at:2048 wt:512 uvt:512 bbT:1024 EQ:2048 SC:1024 PB:256 PR:256 SCN:256 LE:1024 LC2:512 MK:512 RS:256 BS:192 H:512",
+    "int32": "pI:2 ti:8 nbt:12",
+    "uint16": "UL:16 DL:32 nbo:12 nbo2:24 FR:192 FA:256 LST:6 LA:18 LO:18 EO:12 PO0:14 PO1:14 PO2:14 SL0:4 SL1:4 SR0:9 SR1:9 FO:16",
+}
+QBUF = "Q0:256 Qb:256 Qa:512 Qw:128 UVq:128 UV2:256 SND:288 W:%d PK0:144 PK1:144 PK2:144 FIN:256" % WC
+SCRATCH = {"eld": ("dram", [6, 128, 1], "float32"), "ps": ("psum", [128, 4096], "float32")}
+for _d, _s in BUF.items():
+    for _b in _s.split():
+        SCRATCH[_b.split(":")[0]] = ("sbuf", [128, int(_b.split(":")[1])], _d)
+for _b in QBUF.split():
+    SCRATCH[_b.split(":")[0]] = ("sbuf", [128, int(_b.split(":")[1])], "float8_e4m3fn_x4")
+    SCRATCH[_b.split(":")[0] + "s"] = ("sbuf", [128, int(_b.split(":")[1])], "uint8")
+SEMAPHORES = "v s p gq d_nb d_x d_uv d_bb d_a d_w d_q d_m d_e d_nd d_out r_e r_l r_c r_s0 r_s1 r_n0 r_n1 loc".split()
+
+
+def rank_program(g, core, T, topo):
+    rank = T.rank_of(core)
+    if rank is None:
+        return
+    V, S, PE, Y = g.vector, g.scalar, g.tensor, g.sync
+    queue = {"V": V, "S": S, "P": PE, "G": g, "Y": Y}
+    sem_of = {"V": "v", "S": "s", "P": "p", "G": "gq"}
+    count = {s: 0 for s in SEMAPHORES}
+    know = {q: {} for q in queue}
+    snaps, touched = {}, {}
+
+    def reg(name, c0, c1, p0=0, p1=128, st=1):
+        return (name, p0, p1, c0, c1, st)
+
+    def ap(r):
+        n, p0, p1, c0, c1, st = r
+        return T[n][p0:p1, c0:c1:st] if st > 1 else T[n][p0:p1, c0:c1]
+
+    def meet(a, b):
+        if a[0] == "ps":
+            return a[3] // 512 == b[3] // 512
+        if a[2] <= b[1] or b[2] <= a[1] or a[4] <= b[3] or b[4] <= a[3]:
+            return False
+        return not (a[5] == b[5] > 1 and a[3] % a[5] != b[3] % b[5])
+
+    def order(q, reads, writes):
+        want = {}
+        for r, w in [(r, False) for r in reads] + [(r, True) for r in writes]:
+            for (o, ow, oq, sem, val) in touched.get(r[0], []):
+                if meet(r, o) and (ow or ((w or r[0] == "ps") and oq != q)):
+                    val = count[sem] if val is None else val
+                    if know[q].get(sem, 0) < val:
+                        want[sem] = max(want.get(sem, 0), val)
+        for s in sorted(want):
+            if any(o != s and snaps.get((o, want[o]), {}).get(s, 0) >= want[s] for o in want):
+                del want[s]
+        for s, val in want.items():
+            queue[q].wait_ge(T.sem[s], val)
+            know[q][s] = max(know[q].get(s, 0), val)
+            for k, x in snaps.get((s, val), {}).items():
+                know[q][k] = max(know[q].get(k, 0), x)
+
+    def note(reads, writes, q, sem, val):
+        for r in reads:
+            touched.setdefault(r[0], []).append((r, False, q, sem, val))
+        for r in writes:
+            touched.setdefault(r[0], []).append((r, True, q, sem, val))
+
+    def op(q, fn, reads, writes):
+        order(q, reads, writes)
+        s = sem_of[q]
+        count[s] += 1
+        fn().then_inc(T.sem[s], 1)
+        snaps[(s, count[s])] = dict(know[q])
+        note(reads, writes, q, s, count[s])
+
+    def dma(q, sem, out, in_, reads, writes):
+        order(q, reads, writes)
+        count[sem] += 16
+        queue[q].dma_start(out, in_).then_inc(T.sem[sem], 16)
+        note(reads, writes, "dma", sem, None)
+
+    def arrive(sem, total, *writes):
+        note([], writes, "far", sem, total)
+
+    def sc(x):
+        return ap(x) if isinstance(x, tuple) else x
+
+    def copy(out, in_, q="V"):
+        if q == "V":
+            op("V", lambda: V.tensor_copy(ap(out), ap(in_)), [in_], [out])
+        else:
+            op("S", lambda: S.activation(ap(out), ap(in_), AF.Copy), [in_], [out])
+
+    def ts(out, in_, s1, op0, s2=None, op1=None):
+        rd = [in_] + [x for x in (s1, s2) if isinstance(x, tuple)]
+        if op1 is None:
+            op("V", lambda: V.tensor_scalar(ap(out), ap(in_), sc(s1), None, op0), rd, [out])
+        else:
+            op("V", lambda: V.tensor_scalar(ap(out), ap(in_), sc(s1), sc(s2), op0, op1), rd, [out])
+
+    def tt(out, a, b, o):
+        op("V", lambda: V.tensor_tensor(ap(out), ap(a), ap(b), o), [a, b], [out])
+
+    def scan(out, a, b):
+        op("V", lambda: V.tensor_tensor_scan(ap(out), ap(a), ap(b), 0.0, OP.add, OP.add), [a, b], [out])
+
+    def turn(out, in_):
+        op("V", lambda: V.transpose(ap(out), ap(in_)), [in_], [out])
+
+    def fill(out, x):
+        op("V", lambda: V.memset(ap(out), x), [], [out])
+
+    def act(out, in_, f, bias=None, scale=None, accum=None):
+        kw = {}
+        if bias is not None: kw["bias"] = sc(bias)
+        if scale is not None: kw["scale"] = sc(scale)
+        if accum is not None: kw["accum_out"] = ap(accum)
+        op("S", lambda: S.activation(ap(out), ap(in_), f, **kw), [in_] + [x for x in (bias, scale) if isinstance(x, tuple)], [out] + ([accum] if accum else []))
+
+    def gather(out, win, off, q="V"):
+        if q == "V":
+            op("V", lambda: V.tensor_copy(ap(out), ap(win).indirect(ap(off))), [win, off], [out])
+        else:
+            op("S", lambda: S.activation(ap(out), ap(win).indirect(ap(off)), AF.Copy), [win, off], [out])
+
+    def scatter(win, off, in_):
+        op("V", lambda: V.tensor_copy(ap(win).indirect(ap(off)), ap(in_)), [in_, off], [win])
+
+    def pick(dst, c1, src, w1, off):
+        a, b = reg(dst, 0, c1), reg(src, 0, w1)
+        op("V", lambda: V.tensor_copy(ap(a).bitcast(dt.uint32), ap(b).bitcast(dt.uint32).indirect(ap(off))), [b, off], [a])
+        gather(reg(dst + "s", 0, c1), reg(src + "s", 0, w1), off, "S")
+
+    def both(q, c0, c1):
+        return [reg(q, c0, c1), reg(q + "s", c0, c1)]
+
+    def quant(q, c0, c1, t):
+        n = 4 * (c1 - c0)
+        op("V", lambda: V.quantize_mx(T[q][:, c0:c1], T[q + "s"][:, c0:c1], T[t][:, 0:n]), [reg(t, 0, n)], both(q, c0, c1))
+
+    def mm(bank, a, a0, b, b0, n):
+        o = reg("ps", 512 * bank, 512 * bank + n)
+        op("P", lambda: PE.matmul_mx(ap(o), T[a][:, a0:a0 + 128], T[a + "s"][:, a0:a0 + 128], T[b][:, b0:b0 + n], T[b + "s"][:, b0:b0 + n], True, True), both(a, a0, a0 + 128) + both(b, b0, b0 + n), [o])
+
+    def ps(bank, c0, c1, p0=0, p1=128):
+        return reg("ps", 512 * bank + c0, 512 * bank + c1, p0, p1)
+
+    def lanes(src):
+        others = [c for c in T.cores if c != src]
+        off = [c for c in others if topo.chip(c) != topo.chip(src)]
+        on = [c for c in others if topo.chip(c) == topo.chip(src)]
+        out = topo.engines(src, off[0])
+        inn = [e for e in topo.engines(src, on[0]) if e not in out]
+        m = {}
+        for i, c in enumerate(off): m[c] = out[i * (len(out) // len(off)):(i + 1) * (len(out) // len(off))]
+        for i, c in enumerate(on): m[c] = inn[i * (len(inn) // len(on)):(i + 1) * (len(inn) // len(on))]
+        return m
+
+    mine = lanes(core)
+    sources = [T.cores[(rank + 1 + i) % 4] for i in range(3)]
+
+    def slot(dst):
+        return (rank - T.rank_of(dst) - 1) % 4
+
+    def send(sem, pairs, reads):
+        order("G", reads, [])
+        tr = []
+        for c in mine:
+            rid, pid, _ = topo.addr(c)
+            pr = pairs(c)
+            w = len(mine[c]) // len(pr)
+            for i, (s, d) in enumerate(pr):
+                es = mine[c][i * w:(i + 1) * w]
+                tr.append(RemoteDMATransfer(dst_ids=[DstId(rid=rid, pnc=pid)], dma_engine_mask=sum(1 << e for e in es), remote_sem=T.sem[sem], src=s, dst=d))
+                count["loc"] += len(es)
+        g.remote_dma_fused(tr, local_sem=T.sem.loc)
+
+    incoming = sum(len(lanes(c)[core]) for c in sources)
+
+    def cb(name, c0, c1):
+        return T[name][:, c0:c1].bitcast(dt.uint8)
+
+    def ship(sem, q, src, dst):
+        s0, s1 = src
+        send(sem, lambda c: [(cb(q, s0(c), s1(c)), cb("W", dst(c), dst(c) + s1(c) - s0(c)))], [reg(q, 0, s1(None))] if q == "SND" else [reg(q, s0(None), s1(None))])
+        send(sem, lambda c: [(T[q + "s"][:, s0(c):s1(c)], T.Ws[:, dst(c):dst(c) + s1(c) - s0(c)])], [reg(q + "s", 0, s1(None))] if q == "SND" else [reg(q + "s", s0(None), s1(None))])
+
+    flag = dict(allow_small_or_imprecise_dtypes=True)
+    op("G", lambda: g.iota(T.pI[:, 0:1], [[0, 1]], 0, 1), [], [reg("pI", 0, 1)])
+    op("G", lambda: g.iota(T.C32[:], [[32, 8]], 0, 0, **flag), [], [reg("C32", 0, 8)])
+    op("G", lambda: g.iota(T.ID[:], [[1, WC]], 0, 0, **flag), [], [reg("ID", 0, WC)])
+    op("G", lambda: g.iota(T.C16[:], [[16, 16]], 0, 0, **flag), [], [reg("C16", 0, 16)])
+    fill(reg("uvt", 0, 512), 0.0)
+    for h in range(2):
+        for a in range(4):
+            p0 = 32 * a + 16 * h
+            dma("YS"[h], "d_nb", T.nbt[p0:p0 + 16, :], T.nb[:, 12 * a:12 * a + 12], [], [reg("nbt", 0, 12, p0, p0 + 16)])
+    dma("Y", "d_x", T.xt[:], T.x[:], [], [reg("xt", 0, 1024)])
+    dma("Y", "d_uv", T.uvt[:, 0:4], T.u[:, 0:4], [], [reg("uvt", 0, 4)])
+    dma("Y", "d_uv", T.uvt[:, 8:12], T.v[:, 0:4], [], [reg("uvt", 8, 12)])
+    dma("S", "d_bb", T.bt[:], T.bb[:], [], [reg("bt", 0, 1024)])
+    dma("Y", "d_a", T.at[:], T.a[:], [], [reg("at", 0, 2048)])
+    dma("Y", "d_w", T.wt[:], T.w[:], [], [reg("wt", 0, 512)])
+    fill(reg("ZB", 0, 256), 0.0)
+    pI = reg("pI", 0, 1)
+
+    def ti(i):
+        return reg("ti", i, i + 1)
+
+    def tf(i):
+        return reg("tf", i, i + 1)
+
+    ts(ti(0), pI, 96, OP.bitwise_and)
+    ts(ti(1), pI, 31, OP.bitwise_and)
+    ts(ti(2), pI, 15, OP.bitwise_and)
+    ts(tf(4), ti(0), 7.0, OP.mult)
+    tt(tf(0), tf(4), pI, OP.add)
+    tt(tf(1), ti(0), pI, OP.add)
+    ts(tf(2), ti(0), 2.0, OP.mult)
+    copy(tf(3), ti(2))
+    copy(tf(5), ti(1))
+    ts(tf(6), ti(1), 32.0, OP.add)
+    ts(reg("GCOL", 0, 8), reg("C32", 0, 8), tf(0), OP.add)
+    ts(reg("JCOL", 0, 2), reg("C32", 0, 2), tf(1), OP.add)
+    fill(reg("CK", 0, 32), STEP)
+    fill(reg("C1", 0, 32), 1.0)
+    fill(reg("UL", 0, 8), 0)
+    fill(reg("UL", 8, 16), 2)
+    for a in range(4):
+        fill(reg("PADD", 0, 1, 32 * a, 32 * a + 32), float(FAR + LC * ((a - rank - 1) % 4 % 3) - 1))
+    fill(reg("R0", 0, 14), 0.0)
+    fill(reg("H", 0, 512), 0.0)
+    ts(reg("IC", 0, 16), reg("C16", 0, 16), tf(3), OP.add)
+    ts(reg("ICS", 0, 8), reg("IC", 0, 8), -1.0, OP.mult, -0.5, OP.add)
+    ts(reg("TB", 0, 4), reg("IC", 0, 4), -STEP, OP.mult)
+    copy(reg("nbo", 0, 12), reg("nbt", 0, 12))
+    gather(reg("FR", 0, 192), reg("ID", 0, 1024), reg("nbo", 0, 12))
+    copy(reg("FA", 0, 64), reg("FR", 2, 192, st=3))
+    for d in range(4):
+        s = d ^ 1
+        copy(reg("FA", 64, 128, 32 * d, 32 * d + 32), reg("FA", 0, 64, 32 * s, 32 * s + 32))
+    copy(reg("FA", 128, 256, 0, 64), reg("FA", 0, 128, 64, 128))
+    copy(reg("FA", 128, 256, 64, 128), reg("FA", 0, 128, 0, 64))
+    quant("Q0", 0, 256, "xt")
+    quant("UVq", 0, 128, "uvt")
+    for c in range(2):
+        mm(c, "Q0", 128 * c, "UVq", 0, 128)
+    for c in range(2):
+        copy(reg("ec", c, c + 1), ps(c, 0, 1), "S")
+    send("r_e", lambda c: [(T.ec[:, i:i + 1], T.eld[2 * slot(c) + i]) for i in range(2)], [reg("ec", 0, 2)])
+    arrive("r_e", incoming, reg("eld", 0, 6))
+    dma("Y", "d_q", cb("W", 0, 256), cb("Q0", 0, 256), [reg("Q0", 0, 256)], [reg("W", 0, 256)])
+    dma("Y", "d_q", T.Ws[:, 0:256], T.Q0s[:, 0:256], [reg("Q0s", 0, 256)], [reg("Ws", 0, 256)])
+    copy(reg("E0", 0, 1024), reg("ID", 0, 1024), "S")
+    for c in range(8):
+        ts(reg("EQ", 256 * c, 256 * c + 256), reg("FA", 0, 256), reg("GCOL", c, c + 1), OP.is_equal)
+        scan(reg("SC", 128 * c, 128 * c + 128), reg("EQ", 256 * c, 256 * c + 128), reg("EQ", 256 * c + 128, 256 * c + 256))
+        act(reg("PB", 32 * c, 32 * c + 32), reg("ZB", 0, 32), AF.Sign, bias=reg("SC", 128 * c + 127, 128 * c + 128))
+    turn(reg("PR", 0, 256), reg("PB", 0, 256))
+    scan(reg("SCN", 0, 256), reg("PR", 0, 256), reg("ZB", 0, 256))
+    for c in range(4):
+        ts(reg("LE", 256 * c, 256 * c + 256), reg("SCN", 0, 256), reg("IC", c, c + 1), OP.is_le)
+        scan(reg("LC2", 128 * c, 128 * c + 128), reg("LE", 256 * c, 256 * c + 128), reg("LE", 256 * c + 128, 256 * c + 256))
+    for c in range(2):
+        act(reg("LJ", 256 * c, 256 * c + 255), reg("SCN", 0, 255), AF.Sign, bias=reg("ICS", 4 + c, 5 + c), accum=reg("LS", c, c + 1))
+    ts(reg("LST", 0, 4), reg("LC2", 127, 512, st=128), 255.0, OP.min)
+    ts(reg("LST", 4, 6), reg("LS", 0, 2), -0.5, OP.mult, 127.5, OP.add)
+    send("r_l", lambda c: [(T.LST[:, 0:6], T.LA[:, 6 * slot(c):6 * slot(c) + 6])], [reg("LST", 0, 6)])
+    arrive("r_l", incoming, reg("LA", 0, 18))
+    act(reg("SLf", 0, 256), reg("SCN", 0, 256), AF.Identity, bias=reg("PADD", 0, 1))
+    for q in range(4):
+        if q != rank:
+            for d in range(4):
+                dma("Y", "d_m", T.M[32 * d:32 * d + 32, 256 * q:256 * q + 256], T.SLf[32 * q:32 * q + 32, :], [reg("SLf", 0, 256, 32 * q, 32 * q + 32)], [reg("M", 256 * q, 256 * q + 256, 32 * d, 32 * d + 32)])
+    copy(reg("M", 256 * rank, 256 * rank + 256), reg("ID", 0, 256), "S")
+    for d in range(4):
+        i = 0
+        while i < 3:
+            q = (rank + 1 + i) % 4
+            n = min(3 - i, 4 - q)
+            dma("Y", "d_e", T.E0[32 * d:32 * d + 1, 256 * q:256 * (q + n)], T.eld[2 * i:2 * (i + n)], [reg("eld", 2 * i, 2 * (i + n))], [reg("E0", 256 * q, 256 * (q + n), 32 * d, 32 * d + 1)])
+            i += n
+    pick("UV2", 256, "UVq", 128, reg("UL", 0, 16))
+    quant("Qb", 0, 256, "bt")
+    mm(5, "UV2", 0, "Q0", 0, 256)
+    mm(4, "UV2", 128, "Qb", 0, 256)
+    copy(reg("E0", 256 * rank, 256 * rank + 256), ps(5, 0, 256), "S")
+    copy(reg("E1", 0, 256), ps(5, 0, 256), "S")
+    for a in range(4):
+        copy(reg("fb", 0, 64, 32 * a, 32 * a + 32), ps(4, 64 * a, 64 * a + 64, 32 * a, 32 * a + 32), "S")
+    quant("Qa", 0, 512, "at")
+    for h in range(2):
+        copy(reg("nbo2", h, 24, st=2), reg("nbt", 0, 12))
+        copy(reg("DL", h, 32, st=2), reg("IC", 0, 16))
+    ts(reg("JROW", 0, 64), reg("ID", 0, 64), tf(2), OP.add)
+    for b in range(2):
+        ts(reg("Ft", 64 * b, 64 * b + 64), reg("ID", 0, 64), tf(5 + b), OP.is_lt, 2.0 ** -24, OP.mult)
+        ts(reg("Fm", 64 * b, 64 * b + 64), reg("Ft", 64 * b, 64 * b + 64), PRED, OP.add)
+    for d in range(4):
+        copy(reg("LO", 0, 18, 32 * d, 32 * d + 32), reg("LA", 0, 18, 32 * rank, 32 * rank + 32))
+    pick("SND", 288, "Q0", 256, reg("LO", 0, 18))
+    ship("r_c", "SND", (lambda c: LC * sources.index(c), lambda c: 3 * LC if c is None else LC * sources.index(c) + LC), lambda c: FAR + LC * slot(c))
+    arrive("r_c", 2 * incoming, *both("W", FAR, FAR + 3 * LC))
+    for t in range(4):
+        copy(reg("bbT", 256 * t, 256 * t + 256), reg("bt", t, 1024, st=4), "S")
+
+    for t in range(R):
+        Rf, PO, PK = "Rf%d" % t, "PO%d" % t, "PK%d" % t
+        wend = [ARR[0], ARR[1], OWN[2]][t]
+        if t > 0:
+            gather(reg("PD", 0, 384), reg("M", 0, 1024), reg("nbo2", 0, 24), "S")
+        gather(reg("PC", 0, 192), reg("M", 0, 1024), reg("nbo", 0, 12), "S")
+        if t > 0:
+            turn(reg("PT", 0, 384), reg("PD", 0, 384))
+            copy(reg("EO", 0, 12), reg("PT", 0, 384, st=32))
+        for k in range(3):
+            tt(reg("PJ", 64 * k, 64 * k + 64), reg("PC", k, 192, st=3), reg("JROW", 0, 64), OP.subtract)
+        if t > 0:
+            a0 = ARR[t - 1]
+            mm(6, "UV2", 0, "W", a0, 3 * K)
+            copy(reg("E1", a0, a0 + 3 * K), ps(6, 0, 3 * K))
+            gather(reg("EG", 0, 192), reg("E1", 0, wend), reg("EO", 0, 12))
+        else:
+            gather(reg("EG", 0, 192), reg("E0", 0, 1024), reg("nbo", 0, 12))
+        z = [reg(n, 0, 64) for n in ("z1", "z2", "z3", "z4", "zr")]
+        tt(z[0], reg("EG", 0, 192, st=3), reg("EG", 1, 192, st=3), OP.add)
+        tt(z[1], z[0], reg("EG", 2, 192, st=3), OP.add)
+        tt(z[2], z[1], reg("fb", 0, 64), OP.subtract)
+        ts(z[3], z[2], -1.0, OP.mult, TINY, OP.max)
+        tt(z[4], z[2], z[3], OP.max)
+        zr = "zr"
+        turn(reg("ZT", 0, 64), z[4])
+        if t == 0:
+            for b in range(2):
+                ts(reg("zB", 32 * b, 32 * b + 32), reg("C1", 0, 32), reg("ZT", 32 * b, 32 * b + 1), OP.mult)
+            turn(reg("zr0", 0, 64), reg("zB", 0, 64))
+            zr = "zr0"
+        for q, d, s, w, x in (("V", 0, 2, 2, 2), ("S", 2, 0, 2, 2), ("S", 0, 1, 1, 1), ("S", 1, 0, 1, 1), ("S", 2, 3, 1, 1), ("S", 3, 2, 1, 1), ("S", 0, 3, 1, 3), ("V", 3, 0, 1, 3), ("V", 1, 2, 1, 3), ("V", 2, 1, 1, 3)):
+            o = reg("Zc", 64 * x, 64 * x + 64, 32 * d, 32 * d + 32 * w)
+            i = reg(zr, 0, 64, 32 * s, 32 * s + 32 * w)
+            if q == "S":
+                act(o, i, AF.Copy, scale=PRED if s > d else 1.0)
+            elif s > d:
+                ts(o, i, PRED, OP.mult)
+            else:
+                copy(o, i)
+        for b in range(2):
+            tt(reg("Zc", 256 * b, 256 * b + 64), reg(zr, 0, 64), reg("Fm", 64 * b, 64 * b + 64), OP.mult)
+        for b in range(2):
+            ts(reg("MK", 256 * b, 256 * b + 256), reg("Zc", 64 * b, 64 * b + 256), reg("ZT", 32 * b, 32 * b + 1), OP.is_ge)
+        for b in range(2):
+            scan(reg("RS", 128 * b, 128 * b + 128), reg("MK", 256 * b, 256 * b + 128), reg("MK", 256 * b + 128, 256 * b + 256))
+        for b in range(2):
+            ts(reg("KB", 32 * b, 32 * b + 32), reg("CK", 0, 32), reg("RS", 128 * b + 127, 128 * b + 128), OP.mult, reg("JCOL", b, b + 1), OP.add)
+        turn(reg("KEY", 0, 64), reg("KB", 0, 64))
+        for k in range(3):
+            tt(reg("KEY", 64 + 64 * k, 128 + 64 * k), reg("KEY", 0, 64), reg("PJ", 64 * k, 64 * k + 64), OP.add)
+        for c in range(3):
+            act(reg("DK", 256 * c, 256 * c + 256), reg("KEY", 0, 256), AF.Identity, bias=reg("TB", c, c + 1))
+        for c in range(3):
+            for k in range(4):
+                x = 10 + c if k == 0 else 3 * (k - 1) + c
+                o, i = reg("R0", x, x + 1), reg("DK", 256 * c + 64 * k, 256 * c + 64 * k + 64)
+                op("V", lambda: V.tensor_reduce(ap(o), ap(i), AxisListType.X, OP.min, apply_absolute_value=True), [i], [o])
+        for d in range(4):
+            s = d ^ 1
+            copy(reg("RX", 0, 14, 32 * d, 32 * d + 32), reg("R0", 0, 14, 32 * s, 32 * s + 32))
+        tt(reg("R1", 0, 14), reg("R0", 0, 14), reg("RX", 0, 14), OP.min)
+        for d in range(2):
+            copy(reg("RY", 0, 14, 64 * d, 64 * d + 64), reg("R1", 0, 14, 64 - 64 * d, 128 - 64 * d))
+        tt(reg(Rf, 0, 14), reg("R1", 0, 14), reg("RY", 0, 14), OP.min)
+        copy(reg(PO, 0, 14), reg(Rf, 0, 14))
+        J = reg(PO, 10, 13)
+        pick(PK, 144, "W", wend, reg(PO, 0, 9))
+        if t < 2:
+            SL, SR = "SL%d" % t, "SR%d" % t
+            ts(reg(SL, 0, 3), reg(Rf, 10, 13), float(256 * rank), OP.add)
+            send("r_s%d" % t, lambda c: [(T[SL][:, 0:3], T[SR][:, 3 * slot(c):3 * slot(c) + 3])], [reg(SL, 0, 3)])
+            arrive("r_s%d" % t, incoming, reg(SR, 0, 9))
+        for c in range(3):
+            dma("Y", "d_nd", T.nd[t:t + 1, 16 * c:16 * c + 16], T[Rf][0:16, 10 + c:11 + c], [reg(Rf, 10 + c, 11 + c, 0, 16)], [])
+        for b in range(4):
+            mm(b, "Qa", 128 * b, PK, 0, 144)
+        if t == 0:
+            mm(7, "UV2", 0, "W", FAR, 3 * LC)
+        for b in range(4):
+            gather(reg("BS", K * b, K * b + K), reg("bbT", 256 * b, 256 * b + 256), J, "S")
+            copy(reg("S0", K * b, K * b + K), ps(b, 0, K), "S")
+        if t == 0:
+            copy(reg("E1", FAR, FAR + 3 * LC), ps(7, 0, 3 * LC), "S")
+
+        def step(b, i):
+            r = [reg(n, K * b, K * b + K) for n in ("S0", "S1", "S2", "S3", "BS")]
+            if i < 2:
+                tt(r[i + 1], ps(b, K * i + K, K * i + 2 * K), r[i], OP.add)
+            elif i == 2:
+                ts(r[3], r[2], 13421773.0 * 2.0 ** -28, OP.mult)
+            else:
+                tt(reg("H", b, 4 * K, st=4), r[3], r[4], OP.add)
+
+        for w in range(7):
+            for b in range(4):
+                if 0 <= w - b < 4:
+                    step(b, w - b)
+        w0 = OWN[t]
+        quant("W", w0, w0 + 128, "H")
+        if t < 2:
+            ship("r_n%d" % t, "W", (lambda c: w0, lambda c: w0 + K), lambda c: ARR[t] + K * slot(c))
+            arrive("r_n%d" % t, 2 * incoming, *both("W", ARR[t], ARR[t] + 3 * K))
+            mm(7, "UV2", 0, "W", w0, 128)
+            copy(reg("E1", w0, w0 + 128), ps(7, 0, 128), "S")
+        scatter(reg("M", 256 * rank, 256 * rank + 256), J, reg("ID", w0, w0 + K))
+        if t < 2:
+            scatter(reg("M", 0, 1024), reg(SR, 0, 9), reg("ID", ARR[t], ARR[t] + 3 * K))
+        if t == 0:
+            quant("Qw", 0, 128, "wt")
+
+    gather(reg("FD", 0, 512), reg("M", 256 * rank, 256 * rank + 256), reg("DL", 0, 32), "S")
+    turn(reg("FT", 0, 512), reg("FD", 0, 512))
+    copy(reg("FO", 0, 16), reg("FT", 0, 512, st=32))
+    pick("FIN", 256, "W", WC, reg("FO", 0, 16))
+    dma("Y", "d_out", T.oc[:, 0:1024], cb("FIN", 0, 256), [reg("FIN", 0, 256)], [])
+    for k in range(4):
+        dma("Y", "d_out", T.osc[4 * k:4 * k + 4, 0:256], T.FINs[32 * k:32 * k + 4, 0:256], [reg("FINs", 0, 256)], [])
+    for h in range(2):
+        mm(4 + h, "Qw", 0, "FIN", 128 * h, 128)
+    for h in range(2):
+        copy(reg("ys", 128 * h, 128 * h + 128), ps(4 + h, 0, 128), "VS"[h])
+        dma("YS"[h], "d_out", T.y[:, 128 * h:128 * h + 128], T.ys[:, 128 * h:128 * h + 128], [reg("ys", 128 * h, 128 * h + 128)], [])
+    for s in ("v", "s", "p", "gq", "d_q", "d_nd", "d_out", "loc"):
+        if know["G"].get(s, 0) < count[s]:
+            g.wait_ge(T.sem[s], count[s])

@@ -11,13 +11,13 @@ PRED = 1.0 - 2.0 ** -24
 STEP = 4096.0
 
 BUF = {
-    "float32": "ID:%d C32:8 C16:16 tf:8 GCOL:8 JROW:64 IC:16 ICS:8 TB:4 Fm:128 Ft:128 CK:32 C1:32 PADD:1 SLf:256 LJ:512 LS:2 M:1024 ec:2 E0:1024 E1:%d fb:64 PC:192 PJ:192 PD:384 PT:384 EG:192 z1:64 z2:64 z3:64 z4:64 zr:64 ZT:64 zB:64 zr0:64 Zc:320 KB:64 KEY:256 DK:768 R0:14 RX:14 R1:14 RY:14 Rf0:14 Rf1:14 Rf2:14 S0:192 S1:192 S2:192 S3:192 FD:512 FT:512 ys:256" % (WC, OWN[2]),
+    "float32": "ID:%d C32:8 C16:16 tf:8 GCOL:8 JROW:64 IC:16 ICS:8 TB:4 Fm:128 Ft:128 CK:32 C1:32 PADD:1 SLf:256 LJ:512 LS:2 M:1024 ec:2 E0:1024 E1:%d fb:64 na:12 nc:12 nd1:12 nd2:12 PC:192 PJ:192 PD:384 PT:384 EG:192 z1:64 z2:64 z3:64 z4:64 zr:64 ZT:64 zB:64 zr0:64 Zc:320 KB:64 KEY:256 DK:768 R0:14 RX:14 R1:14 RY:14 Rf0:14 Rf1:14 Rf2:14 S0:192 S1:192 S2:192 S3:192 FD:512 FT:512 ys:256" % (WC, OWN[2]),
     "bfloat16": "JCOL:2 ZB:256 xt:1024 bt:1024 at:2048 wt:512 uvt:512 bbT:1024 EQ:2048 SC:1024 PB:256 PR:256 SCN:256 LE:1024 LC2:512 MK:512 RS:256 BS:192 H:512",
-    "int32": "pI:2 ti:8 nbt:12",
-    "uint16": "UL:16 DL:32 nbo:12 nbo2:24 FR:192 FA:256 LST:6 LA:18 LO:18 EO:12 PO0:14 PO1:14 PO2:14 SL0:4 SL1:4 SR0:9 SR1:9 FO:16",
+    "int32": "pI:2 ti:8 nbt:12 n1:12 n2:12 n3:12",
+    "uint16": "UL:16 DL:32 nbo:12 nbe:12 nbo2:24 FR:192 FA:256 LST:6 LA:18 LO:18 EO:12 PO0:14 PO1:14 PO2:14 SL0:4 SL1:4 SR0:9 SR1:9 FO:16",
 }
 QBUF = "Q0:256 Qb:256 Qa:512 Qw:128 UVq:128 UV2:256 SND:288 W:%d PK0:144 PK1:144 PK2:144 FIN:256" % WC
-SCRATCH = {"eld": ("dram", [6, 128, 1], "float32"), "ps": ("psum", [128, 4096], "float32")}
+SCRATCH = {"eld": ("dram", [3, 128, 2], "float32"), "ps": ("psum", [128, 4096], "float32")}
 for _d, _s in BUF.items():
     for _b in _s.split():
         SCRATCH[_b.split(":")[0]] = ("sbuf", [128, int(_b.split(":")[1])], _d)
@@ -172,17 +172,14 @@ def rank_program(g, core, T, topo):
     def slot(dst):
         return (rank - T.rank_of(dst) - 1) % 4
 
-    def send(sem, pairs, reads):
+    def send(sem, pair, reads):
         order("G", reads, [])
         tr = []
         for c in mine:
             rid, pid, _ = topo.addr(c)
-            pr = pairs(c)
-            w = len(mine[c]) // len(pr)
-            for i, (s, d) in enumerate(pr):
-                es = mine[c][i * w:(i + 1) * w]
-                tr.append(RemoteDMATransfer(dst_ids=[DstId(rid=rid, pnc=pid)], dma_engine_mask=sum(1 << e for e in es), remote_sem=T.sem[sem], src=s, dst=d))
-                count["loc"] += len(es)
+            s, d = pair(c)
+            tr.append(RemoteDMATransfer(dst_ids=[DstId(rid=rid, pnc=pid)], dma_engine_mask=sum(1 << e for e in mine[c]), remote_sem=T.sem[sem], src=s, dst=d))
+            count["loc"] += len(mine[c])
         g.remote_dma_fused(tr, local_sem=T.sem.loc)
 
     incoming = sum(len(lanes(c)[core]) for c in sources)
@@ -190,22 +187,22 @@ def rank_program(g, core, T, topo):
     def cb(name, c0, c1):
         return T[name][:, c0:c1].bitcast(dt.uint8)
 
-    def ship(sem, q, src, dst):
-        s0, s1 = src
-        send(sem, lambda c: [(cb(q, s0(c), s1(c)), cb("W", dst(c), dst(c) + s1(c) - s0(c)))], [reg(q, 0, s1(None))] if q == "SND" else [reg(q, s0(None), s1(None))])
-        send(sem, lambda c: [(T[q + "s"][:, s0(c):s1(c)], T.Ws[:, dst(c):dst(c) + s1(c) - s0(c)])], [reg(q + "s", 0, s1(None))] if q == "SND" else [reg(q + "s", s0(None), s1(None))])
+    def ship(sem, q, s0, n, dst, c0, c1):
+        send(sem, lambda c: (cb(q, s0(c), s0(c) + n), cb("W", dst(c), dst(c) + n)), [reg(q, c0, c1)])
+        send(sem, lambda c: (T[q + "s"][:, s0(c):s0(c) + n], T.Ws[:, dst(c):dst(c) + n]), [reg(q + "s", c0, c1)])
 
     flag = dict(allow_small_or_imprecise_dtypes=True)
     op("G", lambda: g.iota(T.pI[:, 0:1], [[0, 1]], 0, 1), [], [reg("pI", 0, 1)])
+    op("G", lambda: g.iota(T.ID[:, 0:1024], [[1, 1024]], 0, 0, **flag), [], [reg("ID", 0, 1024)])
     op("G", lambda: g.iota(T.C32[:], [[32, 8]], 0, 0, **flag), [], [reg("C32", 0, 8)])
-    op("G", lambda: g.iota(T.ID[:], [[1, WC]], 0, 0, **flag), [], [reg("ID", 0, WC)])
     op("G", lambda: g.iota(T.C16[:], [[16, 16]], 0, 0, **flag), [], [reg("C16", 0, 16)])
+    op("G", lambda: g.iota(T.ID[:, 1024:WC], [[1, WC - 1024]], 1024, 0, **flag), [], [reg("ID", 1024, WC)])
     fill(reg("uvt", 0, 512), 0.0)
+    dma("Y", "d_x", T.xt[:], T.x[:], [], [reg("xt", 0, 1024)])
     for h in range(2):
         for a in range(4):
             p0 = 32 * a + 16 * h
             dma("YS"[h], "d_nb", T.nbt[p0:p0 + 16, :], T.nb[:, 12 * a:12 * a + 12], [], [reg("nbt", 0, 12, p0, p0 + 16)])
-    dma("Y", "d_x", T.xt[:], T.x[:], [], [reg("xt", 0, 1024)])
     dma("Y", "d_uv", T.uvt[:, 0:4], T.u[:, 0:4], [], [reg("uvt", 0, 4)])
     dma("Y", "d_uv", T.uvt[:, 8:12], T.v[:, 0:4], [], [reg("uvt", 8, 12)])
     dma("S", "d_bb", T.bt[:], T.bb[:], [], [reg("bt", 0, 1024)])
@@ -224,14 +221,12 @@ def rank_program(g, core, T, topo):
     ts(ti(1), pI, 31, OP.bitwise_and)
     ts(ti(2), pI, 15, OP.bitwise_and)
     ts(tf(4), ti(0), 7.0, OP.mult)
-    tt(tf(0), tf(4), pI, OP.add)
     tt(tf(1), ti(0), pI, OP.add)
     ts(tf(2), ti(0), 2.0, OP.mult)
+    tt(tf(0), tf(4), pI, OP.add)
     copy(tf(3), ti(2))
     copy(tf(5), ti(1))
     ts(tf(6), ti(1), 32.0, OP.add)
-    ts(reg("GCOL", 0, 8), reg("C32", 0, 8), tf(0), OP.add)
-    ts(reg("JCOL", 0, 2), reg("C32", 0, 2), tf(1), OP.add)
     fill(reg("CK", 0, 32), STEP)
     fill(reg("C1", 0, 32), 1.0)
     fill(reg("UL", 0, 8), 0)
@@ -240,9 +235,6 @@ def rank_program(g, core, T, topo):
         fill(reg("PADD", 0, 1, 32 * a, 32 * a + 32), float(FAR + LC * ((a - rank - 1) % 4 % 3) - 1))
     fill(reg("R0", 0, 14), 0.0)
     fill(reg("H", 0, 512), 0.0)
-    ts(reg("IC", 0, 16), reg("C16", 0, 16), tf(3), OP.add)
-    ts(reg("ICS", 0, 8), reg("IC", 0, 8), -1.0, OP.mult, -0.5, OP.add)
-    ts(reg("TB", 0, 4), reg("IC", 0, 4), -STEP, OP.mult)
     copy(reg("nbo", 0, 12), reg("nbt", 0, 12))
     gather(reg("FR", 0, 192), reg("ID", 0, 1024), reg("nbo", 0, 12))
     copy(reg("FA", 0, 64), reg("FR", 2, 192, st=3))
@@ -253,12 +245,15 @@ def rank_program(g, core, T, topo):
     copy(reg("FA", 128, 256, 64, 128), reg("FA", 0, 128, 0, 64))
     quant("Q0", 0, 256, "xt")
     quant("UVq", 0, 128, "uvt")
+    ts(reg("GCOL", 0, 8), reg("C32", 0, 8), tf(0), OP.add)
+    ts(reg("IC", 0, 16), reg("C16", 0, 16), tf(3), OP.add)
+    ts(reg("ICS", 0, 8), reg("IC", 0, 8), -1.0, OP.mult, -0.5, OP.add)
     for c in range(2):
         mm(c, "Q0", 128 * c, "UVq", 0, 128)
     for c in range(2):
         copy(reg("ec", c, c + 1), ps(c, 0, 1), "S")
-    send("r_e", lambda c: [(T.ec[:, i:i + 1], T.eld[2 * slot(c) + i]) for i in range(2)], [reg("ec", 0, 2)])
-    arrive("r_e", incoming, reg("eld", 0, 6))
+    send("r_e", lambda c: (T.ec[:, 0:2], T.eld[slot(c)]), [reg("ec", 0, 2)])
+    arrive("r_e", incoming, reg("eld", 0, 3))
     dma("Y", "d_q", cb("W", 0, 256), cb("Q0", 0, 256), [reg("Q0", 0, 256)], [reg("W", 0, 256)])
     dma("Y", "d_q", T.Ws[:, 0:256], T.Q0s[:, 0:256], [reg("Q0s", 0, 256)], [reg("Ws", 0, 256)])
     copy(reg("E0", 0, 1024), reg("ID", 0, 1024), "S")
@@ -275,33 +270,45 @@ def rank_program(g, core, T, topo):
         act(reg("LJ", 256 * c, 256 * c + 255), reg("SCN", 0, 255), AF.Sign, bias=reg("ICS", 4 + c, 5 + c), accum=reg("LS", c, c + 1))
     ts(reg("LST", 0, 4), reg("LC2", 127, 512, st=128), 255.0, OP.min)
     ts(reg("LST", 4, 6), reg("LS", 0, 2), -0.5, OP.mult, 127.5, OP.add)
-    send("r_l", lambda c: [(T.LST[:, 0:6], T.LA[:, 6 * slot(c):6 * slot(c) + 6])], [reg("LST", 0, 6)])
+    send("r_l", lambda c: (T.LST[:, 0:6], T.LA[:, 6 * slot(c):6 * slot(c) + 6]), [reg("LST", 0, 6)])
     arrive("r_l", incoming, reg("LA", 0, 18))
+    for d in range(4):
+        i = 0
+        while i < 3:
+            q = (rank + 1 + i) % 4
+            n = min(3 - i, 4 - q)
+            dma("Y", "d_e", T.E0[32 * d:32 * d + 1, 256 * q:256 * (q + n)], T.eld[i:i + n], [reg("eld", i, i + n)], [reg("E0", 256 * q, 256 * (q + n), 32 * d, 32 * d + 1)])
+            i += n
     act(reg("SLf", 0, 256), reg("SCN", 0, 256), AF.Identity, bias=reg("PADD", 0, 1))
     for q in range(4):
         if q != rank:
             for d in range(4):
                 dma("Y", "d_m", T.M[32 * d:32 * d + 32, 256 * q:256 * q + 256], T.SLf[32 * q:32 * q + 32, :], [reg("SLf", 0, 256, 32 * q, 32 * q + 32)], [reg("M", 256 * q, 256 * q + 256, 32 * d, 32 * d + 32)])
     copy(reg("M", 256 * rank, 256 * rank + 256), reg("ID", 0, 256), "S")
-    for d in range(4):
-        i = 0
-        while i < 3:
-            q = (rank + 1 + i) % 4
-            n = min(3 - i, 4 - q)
-            dma("Y", "d_e", T.E0[32 * d:32 * d + 1, 256 * q:256 * (q + n)], T.eld[2 * i:2 * (i + n)], [reg("eld", 2 * i, 2 * (i + n))], [reg("E0", 256 * q, 256 * (q + n), 32 * d, 32 * d + 1)])
-            i += n
     pick("UV2", 256, "UVq", 128, reg("UL", 0, 16))
     quant("Qb", 0, 256, "bt")
     mm(5, "UV2", 0, "Q0", 0, 256)
     mm(4, "UV2", 128, "Qb", 0, 256)
-    copy(reg("E0", 256 * rank, 256 * rank + 256), ps(5, 0, 256), "S")
     copy(reg("E1", 0, 256), ps(5, 0, 256), "S")
+    for c in range(2):
+        copy(reg("E0", 256 * rank + c, 256 * rank + 256, st=2), ps(5, 128 * c, 128 * c + 128), "S")
     for a in range(4):
         copy(reg("fb", 0, 64, 32 * a, 32 * a + 32), ps(4, 64 * a, 64 * a + 64, 32 * a, 32 * a + 32), "S")
+    nbt, n1, n2, n3 = [reg(n, 0, 12) for n in ("nbt", "n1", "n2", "n3")]
+    ts(n1, nbt, 127, OP.bitwise_and)
+    ts(n2, nbt, 7, OP.arith_shift_right)
+    ts(n3, nbt, 8, OP.arith_shift_right)
+    ts(reg("na", 0, 12), n1, 2.0, OP.mult)
+    ts(reg("nc", 0, 12), n3, 254.0, OP.mult)
+    tt(reg("nd1", 0, 12), reg("na", 0, 12), n2, OP.add)
+    tt(reg("nd2", 0, 12), reg("nd1", 0, 12), reg("nc", 0, 12), OP.add)
+    copy(reg("nbe", 0, 12), reg("nd2", 0, 12))
     quant("Qa", 0, 512, "at")
     for h in range(2):
-        copy(reg("nbo2", h, 24, st=2), reg("nbt", 0, 12))
+        copy(reg("nbo2", h, 24, st=2), nbt)
         copy(reg("DL", h, 32, st=2), reg("IC", 0, 16))
+    ts(reg("TB", 0, 4), reg("IC", 0, 4), -STEP, OP.mult)
+    ts(reg("JCOL", 0, 2), reg("C32", 0, 2), tf(1), OP.add)
     ts(reg("JROW", 0, 64), reg("ID", 0, 64), tf(2), OP.add)
     for b in range(2):
         ts(reg("Ft", 64 * b, 64 * b + 64), reg("ID", 0, 64), tf(5 + b), OP.is_lt, 2.0 ** -24, OP.mult)
@@ -309,7 +316,7 @@ def rank_program(g, core, T, topo):
     for d in range(4):
         copy(reg("LO", 0, 18, 32 * d, 32 * d + 32), reg("LA", 0, 18, 32 * rank, 32 * rank + 32))
     pick("SND", 288, "Q0", 256, reg("LO", 0, 18))
-    ship("r_c", "SND", (lambda c: LC * sources.index(c), lambda c: 3 * LC if c is None else LC * sources.index(c) + LC), lambda c: FAR + LC * slot(c))
+    ship("r_c", "SND", lambda c: LC * sources.index(c), LC, lambda c: FAR + LC * slot(c), 0, 3 * LC)
     arrive("r_c", 2 * incoming, *both("W", FAR, FAR + 3 * LC))
     for t in range(4):
         copy(reg("bbT", 256 * t, 256 * t + 256), reg("bt", t, 1024, st=4), "S")
@@ -323,6 +330,8 @@ def rank_program(g, core, T, topo):
         if t > 0:
             turn(reg("PT", 0, 384), reg("PD", 0, 384))
             copy(reg("EO", 0, 12), reg("PT", 0, 384, st=32))
+        else:
+            gather(reg("EG", 0, 192), reg("E0", 0, 1024), reg("nbe", 0, 12))
         for k in range(3):
             tt(reg("PJ", 64 * k, 64 * k + 64), reg("PC", k, 192, st=3), reg("JROW", 0, 64), OP.subtract)
         if t > 0:
@@ -330,8 +339,6 @@ def rank_program(g, core, T, topo):
             mm(6, "UV2", 0, "W", a0, 3 * K)
             copy(reg("E1", a0, a0 + 3 * K), ps(6, 0, 3 * K))
             gather(reg("EG", 0, 192), reg("E1", 0, wend), reg("EO", 0, 12))
-        else:
-            gather(reg("EG", 0, 192), reg("E0", 0, 1024), reg("nbo", 0, 12))
         z = [reg(n, 0, 64) for n in ("z1", "z2", "z3", "z4", "zr")]
         tt(z[0], reg("EG", 0, 192, st=3), reg("EG", 1, 192, st=3), OP.add)
         tt(z[1], z[0], reg("EG", 2, 192, st=3), OP.add)
@@ -365,13 +372,13 @@ def rank_program(g, core, T, topo):
         turn(reg("KEY", 0, 64), reg("KB", 0, 64))
         for k in range(3):
             tt(reg("KEY", 64 + 64 * k, 128 + 64 * k), reg("KEY", 0, 64), reg("PJ", 64 * k, 64 * k + 64), OP.add)
-        for c in range(3):
-            act(reg("DK", 256 * c, 256 * c + 256), reg("KEY", 0, 256), AF.Identity, bias=reg("TB", c, c + 1))
-        for c in range(3):
-            for k in range(4):
-                x = 10 + c if k == 0 else 3 * (k - 1) + c
-                o, i = reg("R0", x, x + 1), reg("DK", 256 * c + 64 * k, 256 * c + 64 * k + 64)
-                op("V", lambda: V.tensor_reduce(ap(o), ap(i), AxisListType.X, OP.min, apply_absolute_value=True), [i], [o])
+        for c0, c1 in ((0, 64), (64, 256)):
+            for c in range(3):
+                act(reg("DK", 256 * c + c0, 256 * c + c1), reg("KEY", c0, c1), AF.Identity, bias=reg("TB", c, c + 1))
+        for c, k in [(c, 0) for c in range(3)] + [(c, k) for c in range(3) for k in (1, 2, 3)]:
+            x = 10 + c if k == 0 else 3 * (k - 1) + c
+            o, i = reg("R0", x, x + 1), reg("DK", 256 * c + 64 * k, 256 * c + 64 * k + 64)
+            op("V", lambda: V.tensor_reduce(ap(o), ap(i), AxisListType.X, OP.min, apply_absolute_value=True), [i], [o])
         for d in range(4):
             s = d ^ 1
             copy(reg("RX", 0, 14, 32 * d, 32 * d + 32), reg("R0", 0, 14, 32 * s, 32 * s + 32))
@@ -381,12 +388,15 @@ def rank_program(g, core, T, topo):
         tt(reg(Rf, 0, 14), reg("R1", 0, 14), reg("RY", 0, 14), OP.min)
         copy(reg(PO, 0, 14), reg(Rf, 0, 14))
         J = reg(PO, 10, 13)
+        w0 = OWN[t]
         pick(PK, 144, "W", wend, reg(PO, 0, 9))
         if t < 2:
             SL, SR = "SL%d" % t, "SR%d" % t
             ts(reg(SL, 0, 3), reg(Rf, 10, 13), float(256 * rank), OP.add)
-            send("r_s%d" % t, lambda c: [(T[SL][:, 0:3], T[SR][:, 3 * slot(c):3 * slot(c) + 3])], [reg(SL, 0, 3)])
+            send("r_s%d" % t, lambda c: (T[SL][:, 0:3], T[SR][:, 3 * slot(c):3 * slot(c) + 3]), [reg(SL, 0, 3)])
             arrive("r_s%d" % t, incoming, reg(SR, 0, 9))
+        else:
+            scatter(reg("M", 256 * rank, 256 * rank + 256), J, reg("ID", w0, w0 + K))
         for c in range(3):
             dma("Y", "d_nd", T.nd[t:t + 1, 16 * c:16 * c + 16], T[Rf][0:16, 10 + c:11 + c], [reg(Rf, 10 + c, 11 + c, 0, 16)], [])
         for b in range(4):
@@ -394,38 +404,29 @@ def rank_program(g, core, T, topo):
         if t == 0:
             mm(7, "UV2", 0, "W", FAR, 3 * LC)
         for b in range(4):
-            gather(reg("BS", K * b, K * b + K), reg("bbT", 256 * b, 256 * b + 256), J, "S")
             copy(reg("S0", K * b, K * b + K), ps(b, 0, K), "S")
+            gather(reg("BS", b, 4 * K, st=4), reg("bbT", 256 * b, 256 * b + 256), J, "S")
         if t == 0:
             copy(reg("E1", FAR, FAR + 3 * LC), ps(7, 0, 3 * LC), "S")
-
-        def step(b, i):
-            r = [reg(n, K * b, K * b + K) for n in ("S0", "S1", "S2", "S3", "BS")]
-            if i < 2:
-                tt(r[i + 1], ps(b, K * i + K, K * i + 2 * K), r[i], OP.add)
-            elif i == 2:
-                ts(r[3], r[2], 13421773.0 * 2.0 ** -28, OP.mult)
-            else:
-                tt(reg("H", b, 4 * K, st=4), r[3], r[4], OP.add)
-
-        for w in range(7):
-            for b in range(4):
-                if 0 <= w - b < 4:
-                    step(b, w - b)
-        w0 = OWN[t]
+        if t == 2:
+            gather(reg("FD", 0, 512), reg("M", 256 * rank, 256 * rank + 256), reg("DL", 0, 32), "S")
+        for w in range(5):
+            for b, i in ((w, 0), (w - 1, 1)):
+                if 0 <= b < 4:
+                    tt(reg("S2", b, 4 * K, st=4) if i else reg("S1", K * b, K * b + K), ps(b, K * i + K, K * i + 2 * K), reg("S1" if i else "S0", K * b, K * b + K), OP.add)
+        ts(reg("S3", 0, 4 * K), reg("S2", 0, 4 * K), 13421773.0 * 2.0 ** -28, OP.mult)
+        tt(reg("H", 0, 4 * K), reg("S3", 0, 4 * K), reg("BS", 0, 4 * K), OP.add)
         quant("W", w0, w0 + 128, "H")
         if t < 2:
-            ship("r_n%d" % t, "W", (lambda c: w0, lambda c: w0 + K), lambda c: ARR[t] + K * slot(c))
+            ship("r_n%d" % t, "W", lambda c: w0, K, lambda c: ARR[t] + K * slot(c), w0, w0 + K)
             arrive("r_n%d" % t, 2 * incoming, *both("W", ARR[t], ARR[t] + 3 * K))
             mm(7, "UV2", 0, "W", w0, 128)
             copy(reg("E1", w0, w0 + 128), ps(7, 0, 128), "S")
-        scatter(reg("M", 256 * rank, 256 * rank + 256), J, reg("ID", w0, w0 + K))
-        if t < 2:
+            scatter(reg("M", 256 * rank, 256 * rank + 256), J, reg("ID", w0, w0 + K))
             scatter(reg("M", 0, 1024), reg(SR, 0, 9), reg("ID", ARR[t], ARR[t] + 3 * K))
         if t == 0:
             quant("Qw", 0, 128, "wt")
 
-    gather(reg("FD", 0, 512), reg("M", 256 * rank, 256 * rank + 256), reg("DL", 0, 32), "S")
     turn(reg("FT", 0, 512), reg("FD", 0, 512))
     copy(reg("FO", 0, 16), reg("FT", 0, 512, st=32))
     pick("FIN", 256, "W", WC, reg("FO", 0, 16))

@@ -2,19 +2,21 @@ from concourse.bass import DstId, RemoteDMATransfer
 from concourse.mybir import AluOpType as OP, AxisListType, ActivationFunctionType as AF, dt
 
 P, K, R, LC = 256, 48, 3, 96
-FAR = P
-ARR = [FAR + 3 * LC, FAR + 3 * LC + 3 * K + 128]
-OWN = [ARR[0] + 3 * K, ARR[1] + 3 * K, ARR[1] + 3 * K + 128]
+OWN = [P, P + K]
+FAR = P + K + 128
+ARR = [FAR + 3 * LC, FAR + 3 * LC + 3 * K]
+OWN.append(ARR[1] + 3 * K)
+WEND = [ARR[0], ARR[1], OWN[2]]
 WC = OWN[2] + 128
 TINY = 2.0 ** -120
 PRED = 1.0 - 2.0 ** -24
-STEP = 4096.0
+STEP, MID = 2.0 ** 19, 2.0 ** 24
 
 BUF = {
-    "float32": "ID:%d C32:8 C16:16 tf:8 GCOL:8 JROW:64 IC:16 ICS:8 TB:4 Fm:128 Ft:128 CK:32 C1:32 PADD:1 SLf:256 LJ:512 LS:2 M:1024 ec:2 E0:1024 E1:%d fb:64 na:12 nc:12 nd1:12 nd2:12 PC:192 PJ:192 PD:384 PT:384 EG:192 z1:64 z2:64 z3:64 z4:64 zr:64 ZT:64 zB:64 zr0:64 Zc:320 KB:64 KEY:256 DK:768 R0:14 RX:14 R1:14 RY:14 Rf0:14 Rf1:14 Rf2:14 S0:192 S1:192 S2:192 S3:192 FD:512 FT:512 ys:256" % (WC, OWN[2]),
-    "bfloat16": "JCOL:2 ZB:256 xt:1024 bt:1024 at:2048 wt:512 uvt:512 bbT:1024 EQ:2048 SC:1024 PB:256 PR:256 SCN:256 LE:1024 LC2:512 MK:512 RS:256 BS:192 H:512",
-    "int32": "pI:2 ti:8 nbt:12 n1:12 n2:12 n3:12",
-    "uint16": "UL:16 DL:32 nbo:12 nbe:12 nbo2:24 FR:192 FA:256 LST:6 LA:18 LO:18 EO:12 PO0:14 PO1:14 PO2:14 SL0:4 SL1:4 SR0:9 SR1:9 FO:16",
+    "float32": "ID:%d C32:8 C16:16 C12:12 tf:8 GCOL:8 JB:64 IC:16 ICS:8 TB:4 Fm:128 Ft:128 CK:32 C1:32 PADD:1 FR:192 SLf:256 LJ:768 LS:3 M:1024 ec:2 EM:1024 FE:192 E1:%d fb:64 PC:192 PC2:192 PAB:128 PD:384 PT:384 EG:192 z1:64 z2:64 z3:64 z4:64 zr:64 ZT:64 zB:64 zr0:64 Zc:320 KB:64 KR:64 KEY:128 DK:384 R0:6 R1:6 nf0:3 nf1:3 nf2:3 S0:192 S1:192 S2:192 S3:192 FD:512 FT:512 ys:256" % (WC, OWN[2]),
+    "bfloat16": "ZB:256 xt:1024 bt:1024 at:2048 wt:512 uvt:512 bbT:1024 EQ:2048 SC:1024 PB:256 PR:256 SCN:256 LE:768 LC2:384 MK:512 RS:256 BS:192 H:512",
+    "int32": "pI:2 ti:8 nbt:12 Ri:6 Di:9 Ji:3",
+    "uint16": "UL:16 DL:32 KDL:24 nbo:12 nbe:12 FA:256 LST:6 LA:18 LO:18 EO:12 PO0:10 PO1:10 PO2:10 J0:4 J1:4 J2:4 SL0:4 SL1:4 SR0:9 SR1:9 FO:16",
 }
 QBUF = "Q0:256 Qb:256 Qa:512 Qw:128 UVq:128 UV2:256 SND:288 W:%d PK0:144 PK1:144 PK2:144 FIN:256" % WC
 SCRATCH = {"eld": ("dram", [3, 128, 2], "float32"), "ps": ("psum", [128, 4096], "float32")}
@@ -95,11 +97,18 @@ def rank_program(g, core, T, topo):
     def sc(x):
         return ap(x) if isinstance(x, tuple) else x
 
+    def act(out, in_, f, bias=None, scale=None, accum=None):
+        kw = {}
+        if bias is not None: kw["bias"] = sc(bias)
+        if scale is not None: kw["scale"] = sc(scale)
+        if accum is not None: kw["accum_out"] = ap(accum)
+        op("S", lambda: S.activation(ap(out), ap(in_), f, **kw), [in_] + [x for x in (bias, scale) if isinstance(x, tuple)], [out] + ([accum] if accum else []))
+
     def copy(out, in_, q="V"):
         if q == "V":
             op("V", lambda: V.tensor_copy(ap(out), ap(in_)), [in_], [out])
         else:
-            op("S", lambda: S.activation(ap(out), ap(in_), AF.Copy), [in_], [out])
+            act(out, in_, AF.Copy)
 
     def ts(out, in_, s1, op0, s2=None, op1=None):
         rd = [in_] + [x for x in (s1, s2) if isinstance(x, tuple)]
@@ -120,12 +129,14 @@ def rank_program(g, core, T, topo):
     def fill(out, x):
         op("V", lambda: V.memset(ap(out), x), [], [out])
 
-    def act(out, in_, f, bias=None, scale=None, accum=None):
-        kw = {}
-        if bias is not None: kw["bias"] = sc(bias)
-        if scale is not None: kw["scale"] = sc(scale)
-        if accum is not None: kw["accum_out"] = ap(accum)
-        op("S", lambda: S.activation(ap(out), ap(in_), f, **kw), [in_] + [x for x in (bias, scale) if isinstance(x, tuple)], [out] + ([accum] if accum else []))
+    def iota(out, pattern, base, alone=False):
+        if alone and count["gq"] > know["G"].get("gq", 0):
+            g.wait_ge(T.sem.gq, count["gq"])
+            know["G"]["gq"] = count["gq"]
+        if out[0] == "pI":
+            op("G", lambda: g.iota(ap(out), pattern, base, 1), [], [out])
+        else:
+            op("G", lambda: g.iota(ap(out), pattern, base, 0, allow_small_or_imprecise_dtypes=True), [], [out])
 
     def gather(out, win, off, q="V"):
         if q == "V":
@@ -144,9 +155,9 @@ def rank_program(g, core, T, topo):
     def both(q, c0, c1):
         return [reg(q, c0, c1), reg(q + "s", c0, c1)]
 
-    def quant(q, c0, c1, t):
-        n = 4 * (c1 - c0)
-        op("V", lambda: V.quantize_mx(T[q][:, c0:c1], T[q + "s"][:, c0:c1], T[t][:, 0:n]), [reg(t, 0, n)], both(q, c0, c1))
+    def quant(q, c0, c1, t, e0=0):
+        e1 = e0 + 4 * (c1 - c0)
+        op("V", lambda: V.quantize_mx(T[q][:, c0:c1], T[q + "s"][:, c0:c1], T[t][:, e0:e1]), [reg(t, e0, e1)], both(q, c0, c1))
 
     def mm(bank, a, a0, b, b0, n):
         o = reg("ps", 512 * bank, 512 * bank + n)
@@ -191,12 +202,24 @@ def rank_program(g, core, T, topo):
         send(sem, lambda c: (cb(q, s0(c), s0(c) + n), cb("W", dst(c), dst(c) + n)), [reg(q, c0, c1)])
         send(sem, lambda c: (T[q + "s"][:, s0(c):s0(c) + n], T.Ws[:, dst(c):dst(c) + n]), [reg(q + "s", c0, c1)])
 
-    flag = dict(allow_small_or_imprecise_dtypes=True)
-    op("G", lambda: g.iota(T.pI[:, 0:1], [[0, 1]], 0, 1), [], [reg("pI", 0, 1)])
-    op("G", lambda: g.iota(T.ID[:, 0:1024], [[1, 1024]], 0, 0, **flag), [], [reg("ID", 0, 1024)])
-    op("G", lambda: g.iota(T.C32[:], [[32, 8]], 0, 0, **flag), [], [reg("C32", 0, 8)])
-    op("G", lambda: g.iota(T.C16[:], [[16, 16]], 0, 0, **flag), [], [reg("C16", 0, 16)])
-    op("G", lambda: g.iota(T.ID[:, 1024:WC], [[1, WC - 1024]], 1024, 0, **flag), [], [reg("ID", 1024, WC)])
+    def ti(i):
+        return reg("ti", i, i + 1)
+
+    def tf(i):
+        return reg("tf", i, i + 1)
+
+    pI = reg("pI", 0, 1)
+    iota(pI, [[0, 1]], 0)
+    iota(reg("ID", 0, 1024), [[1, 1024]], 0)
+    iota(reg("C32", 0, 8), [[32, 8]], 0)
+    iota(reg("C16", 0, 16), [[16, 16]], 0)
+    iota(reg("ZB", 0, 256), [[0, 256]], 0)
+    iota(reg("C12", 0, 12), [[1, 3], [48, 4]], 0)
+    iota(reg("CK", 0, 32), [[0, 32]], int(STEP))
+    iota(reg("C1", 0, 32), [[0, 32]], 1)
+    iota(reg("ID", 1024, WC), [[1, WC - 1024]], 1024)
+    for a in range(4):
+        iota(reg("PADD", 0, 1, 32 * a, 32 * a + 32), [[0, 1]], FAR + LC * ((a - rank - 1) % 4 % 3) - 1, True)
     fill(reg("uvt", 0, 512), 0.0)
     dma("Y", "d_x", T.xt[:], T.x[:], [], [reg("xt", 0, 1024)])
     for h in range(2):
@@ -208,35 +231,28 @@ def rank_program(g, core, T, topo):
     dma("S", "d_bb", T.bt[:], T.bb[:], [], [reg("bt", 0, 1024)])
     dma("Y", "d_a", T.at[:], T.a[:], [], [reg("at", 0, 2048)])
     dma("Y", "d_w", T.wt[:], T.w[:], [], [reg("wt", 0, 512)])
-    fill(reg("ZB", 0, 256), 0.0)
-    pI = reg("pI", 0, 1)
-
-    def ti(i):
-        return reg("ti", i, i + 1)
-
-    def tf(i):
-        return reg("tf", i, i + 1)
-
     ts(ti(0), pI, 96, OP.bitwise_and)
     ts(ti(1), pI, 31, OP.bitwise_and)
     ts(ti(2), pI, 15, OP.bitwise_and)
     ts(tf(4), ti(0), 7.0, OP.mult)
-    tt(tf(1), ti(0), pI, OP.add)
-    ts(tf(2), ti(0), 2.0, OP.mult)
-    tt(tf(0), tf(4), pI, OP.add)
     copy(tf(3), ti(2))
+    ts(tf(2), ti(0), 2048.0, OP.mult)
+    tt(tf(0), tf(4), pI, OP.add)
     copy(tf(5), ti(1))
     ts(tf(6), ti(1), 32.0, OP.add)
-    fill(reg("CK", 0, 32), STEP)
-    fill(reg("C1", 0, 32), 1.0)
+    ts(tf(7), ti(2), 3.0, OP.mult)
     fill(reg("UL", 0, 8), 0)
     fill(reg("UL", 8, 16), 2)
-    for a in range(4):
-        fill(reg("PADD", 0, 1, 32 * a, 32 * a + 32), float(FAR + LC * ((a - rank - 1) % 4 % 3) - 1))
-    fill(reg("R0", 0, 14), 0.0)
     fill(reg("H", 0, 512), 0.0)
+    fill(reg("E1", OWN[0] + 128, FAR), 0.0)
+    act(reg("GCOL", 0, 8), reg("C32", 0, 8), AF.Identity, bias=tf(0))
+    act(reg("IC", 0, 16), reg("C16", 0, 16), AF.Identity, bias=tf(3))
+    act(reg("ICS", 0, 8), reg("IC", 0, 8), AF.Identity, scale=-1.0, bias=-0.5)
+    for q in range(8):
+        act(reg("EM", 128 * q, 128 * q + 128), reg("ID", 0, 128), AF.Identity, scale=2.0, bias=float(256 * (q // 2) + q % 2))
     copy(reg("nbo", 0, 12), reg("nbt", 0, 12))
     gather(reg("FR", 0, 192), reg("ID", 0, 1024), reg("nbo", 0, 12))
+    gather(reg("FE", 0, 192), reg("EM", 0, 1024), reg("nbo", 0, 12), "S")
     copy(reg("FA", 0, 64), reg("FR", 2, 192, st=3))
     for d in range(4):
         s = d ^ 1
@@ -245,9 +261,6 @@ def rank_program(g, core, T, topo):
     copy(reg("FA", 128, 256, 64, 128), reg("FA", 0, 128, 0, 64))
     quant("Q0", 0, 256, "xt")
     quant("UVq", 0, 128, "uvt")
-    ts(reg("GCOL", 0, 8), reg("C32", 0, 8), tf(0), OP.add)
-    ts(reg("IC", 0, 16), reg("C16", 0, 16), tf(3), OP.add)
-    ts(reg("ICS", 0, 8), reg("IC", 0, 8), -1.0, OP.mult, -0.5, OP.add)
     for c in range(2):
         mm(c, "Q0", 128 * c, "UVq", 0, 128)
     for c in range(2):
@@ -256,20 +269,18 @@ def rank_program(g, core, T, topo):
     arrive("r_e", incoming, reg("eld", 0, 3))
     dma("Y", "d_q", cb("W", 0, 256), cb("Q0", 0, 256), [reg("Q0", 0, 256)], [reg("W", 0, 256)])
     dma("Y", "d_q", T.Ws[:, 0:256], T.Q0s[:, 0:256], [reg("Q0s", 0, 256)], [reg("Ws", 0, 256)])
-    copy(reg("E0", 0, 1024), reg("ID", 0, 1024), "S")
     for c in range(8):
         ts(reg("EQ", 256 * c, 256 * c + 256), reg("FA", 0, 256), reg("GCOL", c, c + 1), OP.is_equal)
         scan(reg("SC", 128 * c, 128 * c + 128), reg("EQ", 256 * c, 256 * c + 128), reg("EQ", 256 * c + 128, 256 * c + 256))
         act(reg("PB", 32 * c, 32 * c + 32), reg("ZB", 0, 32), AF.Sign, bias=reg("SC", 128 * c + 127, 128 * c + 128))
     turn(reg("PR", 0, 256), reg("PB", 0, 256))
     scan(reg("SCN", 0, 256), reg("PR", 0, 256), reg("ZB", 0, 256))
-    for c in range(4):
+    for c in range(3):
         ts(reg("LE", 256 * c, 256 * c + 256), reg("SCN", 0, 256), reg("IC", c, c + 1), OP.is_le)
         scan(reg("LC2", 128 * c, 128 * c + 128), reg("LE", 256 * c, 256 * c + 128), reg("LE", 256 * c + 128, 256 * c + 256))
-    for c in range(2):
-        act(reg("LJ", 256 * c, 256 * c + 255), reg("SCN", 0, 255), AF.Sign, bias=reg("ICS", 4 + c, 5 + c), accum=reg("LS", c, c + 1))
-    ts(reg("LST", 0, 4), reg("LC2", 127, 512, st=128), 255.0, OP.min)
-    ts(reg("LST", 4, 6), reg("LS", 0, 2), -0.5, OP.mult, 127.5, OP.add)
+        act(reg("LJ", 256 * c, 256 * c + 255), reg("SCN", 0, 255), AF.Sign, bias=reg("ICS", 3 + c, 4 + c), accum=reg("LS", c, c + 1))
+    ts(reg("LST", 0, 3), reg("LC2", 127, 384, st=128), 255.0, OP.min)
+    ts(reg("LST", 3, 6), reg("LS", 0, 3), -0.5, OP.mult, 127.5, OP.add)
     send("r_l", lambda c: (T.LST[:, 0:6], T.LA[:, 6 * slot(c):6 * slot(c) + 6]), [reg("LST", 0, 6)])
     arrive("r_l", incoming, reg("LA", 0, 18))
     for d in range(4):
@@ -277,71 +288,62 @@ def rank_program(g, core, T, topo):
         while i < 3:
             q = (rank + 1 + i) % 4
             n = min(3 - i, 4 - q)
-            dma("Y", "d_e", T.E0[32 * d:32 * d + 1, 256 * q:256 * (q + n)], T.eld[i:i + n], [reg("eld", i, i + n)], [reg("E0", 256 * q, 256 * (q + n), 32 * d, 32 * d + 1)])
+            dma("Y", "d_e", T.EM[32 * d:32 * d + 1, 256 * q:256 * (q + n)], T.eld[i:i + n], [reg("eld", i, i + n)], [reg("EM", 256 * q, 256 * (q + n), 32 * d, 32 * d + 1)])
             i += n
     act(reg("SLf", 0, 256), reg("SCN", 0, 256), AF.Identity, bias=reg("PADD", 0, 1))
     for q in range(4):
         if q != rank:
             for d in range(4):
                 dma("Y", "d_m", T.M[32 * d:32 * d + 32, 256 * q:256 * q + 256], T.SLf[32 * q:32 * q + 32, :], [reg("SLf", 0, 256, 32 * q, 32 * q + 32)], [reg("M", 256 * q, 256 * q + 256, 32 * d, 32 * d + 32)])
-    copy(reg("M", 256 * rank, 256 * rank + 256), reg("ID", 0, 256), "S")
+    for h in range(2):
+        ts(reg("KDL", h, 24, st=2), reg("C12", 0, 12), tf(7), OP.add)
+    gather(reg("PD", 0, 384), reg("FE", 0, 192), reg("KDL", 0, 24), "S")
     pick("UV2", 256, "UVq", 128, reg("UL", 0, 16))
     quant("Qb", 0, 256, "bt")
     mm(5, "UV2", 0, "Q0", 0, 256)
     mm(4, "UV2", 128, "Qb", 0, 256)
-    copy(reg("E1", 0, 256), ps(5, 0, 256), "S")
-    for c in range(2):
-        copy(reg("E0", 256 * rank + c, 256 * rank + 256, st=2), ps(5, 128 * c, 128 * c + 128), "S")
-    for a in range(4):
-        copy(reg("fb", 0, 64, 32 * a, 32 * a + 32), ps(4, 64 * a, 64 * a + 64, 32 * a, 32 * a + 32), "S")
-    nbt, n1, n2, n3 = [reg(n, 0, 12) for n in ("nbt", "n1", "n2", "n3")]
-    ts(n1, nbt, 127, OP.bitwise_and)
-    ts(n2, nbt, 7, OP.arith_shift_right)
-    ts(n3, nbt, 8, OP.arith_shift_right)
-    ts(reg("na", 0, 12), n1, 2.0, OP.mult)
-    ts(reg("nc", 0, 12), n3, 254.0, OP.mult)
-    tt(reg("nd1", 0, 12), reg("na", 0, 12), n2, OP.add)
-    tt(reg("nd2", 0, 12), reg("nd1", 0, 12), reg("nc", 0, 12), OP.add)
-    copy(reg("nbe", 0, 12), reg("nd2", 0, 12))
-    quant("Qa", 0, 512, "at")
-    for h in range(2):
-        copy(reg("nbo2", h, 24, st=2), nbt)
-        copy(reg("DL", h, 32, st=2), reg("IC", 0, 16))
-    ts(reg("TB", 0, 4), reg("IC", 0, 4), -STEP, OP.mult)
-    ts(reg("JCOL", 0, 2), reg("C32", 0, 2), tf(1), OP.add)
-    ts(reg("JROW", 0, 64), reg("ID", 0, 64), tf(2), OP.add)
+    turn(reg("PT", 0, 384), reg("PD", 0, 384))
+    copy(reg("nbe", 0, 12), reg("PT", 0, 384, st=32))
     for b in range(2):
         ts(reg("Ft", 64 * b, 64 * b + 64), reg("ID", 0, 64), tf(5 + b), OP.is_lt, 2.0 ** -24, OP.mult)
-        ts(reg("Fm", 64 * b, 64 * b + 64), reg("Ft", 64 * b, 64 * b + 64), PRED, OP.add)
+    for c in range(2):
+        copy(reg("EM", 256 * rank + c, 256 * rank + 256, st=2), ps(5, 128 * c, 128 * c + 128), "S")
+    for a in range(4):
+        copy(reg("fb", 0, 64, 32 * a, 32 * a + 32), ps(4, 64 * a, 64 * a + 64, 32 * a, 32 * a + 32), "S")
+    act(reg("Fm", 0, 128), reg("Ft", 0, 128), AF.Identity, bias=PRED)
+    copy(reg("M", 256 * rank, 256 * rank + 256), reg("ID", 0, 256), "S")
+    act(reg("JB", 0, 64), reg("ID", 0, 64), AF.Identity, scale=1024.0, bias=tf(2))
+    act(reg("TB", 0, 4), reg("IC", 0, 4), AF.Identity, scale=-STEP, bias=MID)
+    for t in range(4):
+        copy(reg("bbT", 256 * t, 256 * t + 256), reg("bt", t, 1024, st=4), "S")
     for d in range(4):
         copy(reg("LO", 0, 18, 32 * d, 32 * d + 32), reg("LA", 0, 18, 32 * rank, 32 * rank + 32))
     pick("SND", 288, "Q0", 256, reg("LO", 0, 18))
     ship("r_c", "SND", lambda c: LC * sources.index(c), LC, lambda c: FAR + LC * slot(c), 0, 3 * LC)
     arrive("r_c", 2 * incoming, *both("W", FAR, FAR + 3 * LC))
-    for t in range(4):
-        copy(reg("bbT", 256 * t, 256 * t + 256), reg("bt", t, 1024, st=4), "S")
+
+    EG = [reg("EG", 64 * k, 64 * k + 64) for k in range(3)]
+    z = [reg(n, 0, 64) for n in ("z1", "z2", "z3", "z4", "zr")]
+
+    def payload01(pc):
+        ts(reg("zB", 0, 64), reg(pc, 1, 192, st=3), 512.0, OP.mult)
+        tt(reg("PAB", 0, 64), reg("zB", 0, 64), reg(pc, 0, 192, st=3), OP.add)
+
+    def payload2(pc):
+        tt(reg("PAB", 64, 128), reg(pc, 2, 192, st=3), reg("JB", 0, 64), OP.add)
 
     for t in range(R):
-        Rf, PO, PK = "Rf%d" % t, "PO%d" % t, "PK%d" % t
-        wend = [ARR[0], ARR[1], OWN[2]][t]
-        if t > 0:
-            gather(reg("PD", 0, 384), reg("M", 0, 1024), reg("nbo2", 0, 24), "S")
-        gather(reg("PC", 0, 192), reg("M", 0, 1024), reg("nbo", 0, 12), "S")
-        if t > 0:
-            turn(reg("PT", 0, 384), reg("PD", 0, 384))
-            copy(reg("EO", 0, 12), reg("PT", 0, 384, st=32))
+        PO, PK, Ju, SL, SR = "PO%d" % t, "PK%d" % t, "J%d" % t, "SL%d" % t, "SR%d" % t
+        wend = WEND[t]
+        if t == 0:
+            gather(reg("EG", 0, 192), reg("EM", 0, 1024), reg("nbe", 0, 12))
+            tt(z[0], EG[0], EG[1], OP.add)
         else:
-            gather(reg("EG", 0, 192), reg("E0", 0, 1024), reg("nbe", 0, 12))
-        for k in range(3):
-            tt(reg("PJ", 64 * k, 64 * k + 64), reg("PC", k, 192, st=3), reg("JROW", 0, 64), OP.subtract)
-        if t > 0:
             a0 = ARR[t - 1]
             mm(6, "UV2", 0, "W", a0, 3 * K)
             copy(reg("E1", a0, a0 + 3 * K), ps(6, 0, 3 * K))
-            gather(reg("EG", 0, 192), reg("E1", 0, wend), reg("EO", 0, 12))
-        z = [reg(n, 0, 64) for n in ("z1", "z2", "z3", "z4", "zr")]
-        tt(z[0], reg("EG", 0, 192, st=3), reg("EG", 1, 192, st=3), OP.add)
-        tt(z[1], z[0], reg("EG", 2, 192, st=3), OP.add)
+            gather(EG[2], reg("E1", 0, wend), reg("EO", 8, 12))
+        tt(z[1], z[0], EG[2], OP.add)
         tt(z[2], z[1], reg("fb", 0, 64), OP.subtract)
         ts(z[3], z[2], -1.0, OP.mult, TINY, OP.max)
         tt(z[4], z[2], z[3], OP.max)
@@ -368,48 +370,58 @@ def rank_program(g, core, T, topo):
         for b in range(2):
             scan(reg("RS", 128 * b, 128 * b + 128), reg("MK", 256 * b, 256 * b + 128), reg("MK", 256 * b + 128, 256 * b + 256))
         for b in range(2):
-            ts(reg("KB", 32 * b, 32 * b + 32), reg("CK", 0, 32), reg("RS", 128 * b + 127, 128 * b + 128), OP.mult, reg("JCOL", b, b + 1), OP.add)
-        turn(reg("KEY", 0, 64), reg("KB", 0, 64))
-        for k in range(3):
-            tt(reg("KEY", 64 + 64 * k, 128 + 64 * k), reg("KEY", 0, 64), reg("PJ", 64 * k, 64 * k + 64), OP.add)
-        for c0, c1 in ((0, 64), (64, 256)):
-            for c in range(3):
-                act(reg("DK", 256 * c + c0, 256 * c + c1), reg("KEY", c0, c1), AF.Identity, bias=reg("TB", c, c + 1))
-        for c, k in [(c, 0) for c in range(3)] + [(c, k) for c in range(3) for k in (1, 2, 3)]:
-            x = 10 + c if k == 0 else 3 * (k - 1) + c
-            o, i = reg("R0", x, x + 1), reg("DK", 256 * c + 64 * k, 256 * c + 64 * k + 64)
-            op("V", lambda: V.tensor_reduce(ap(o), ap(i), AxisListType.X, OP.min, apply_absolute_value=True), [i], [o])
+            ts(reg("KB", 32 * b, 32 * b + 32), reg("CK", 0, 32), reg("RS", 128 * b + 127, 128 * b + 128), OP.mult, -MID, OP.add)
+        turn(reg("KR", 0, 64), reg("KB", 0, 64))
+        if t == 0:
+            gather(reg("PC", 0, 192), reg("M", 0, 1024), reg("nbo", 0, 12), "S")
+            payload01("PC")
+            payload2("PC")
+        for k in range(2):
+            tt(reg("KEY", 64 * k, 64 * k + 64), reg("KR", 0, 64), reg("PAB", 64 * k, 64 * k + 64), OP.add)
+        for c in range(3):
+            act(reg("DK", 128 * c, 128 * c + 128), reg("KEY", 0, 128), AF.Identity, bias=reg("TB", c, c + 1))
+        if t == 0:
+            quant("Qa", 0, 256, "at")
+        for c in range(3):
+            for k in range(2):
+                o, i = reg("R0", 3 * k + c, 3 * k + c + 1), reg("DK", 128 * c + 64 * k, 128 * c + 64 * k + 64)
+                op("V", lambda: V.tensor_reduce(ap(o), ap(i), AxisListType.X, OP.min, apply_absolute_value=True), [i], [o])
         for d in range(4):
             s = d ^ 1
-            copy(reg("RX", 0, 14, 32 * d, 32 * d + 32), reg("R0", 0, 14, 32 * s, 32 * s + 32))
-        tt(reg("R1", 0, 14), reg("R0", 0, 14), reg("RX", 0, 14), OP.min)
+            tt(reg("R1", 0, 6, 32 * d, 32 * d + 32), reg("R0", 0, 6, 32 * d, 32 * d + 32), reg("R0", 0, 6, 32 * s, 32 * s + 32), OP.min)
         for d in range(2):
-            copy(reg("RY", 0, 14, 64 * d, 64 * d + 64), reg("R1", 0, 14, 64 - 64 * d, 128 - 64 * d))
-        tt(reg(Rf, 0, 14), reg("R1", 0, 14), reg("RY", 0, 14), OP.min)
-        copy(reg(PO, 0, 14), reg(Rf, 0, 14))
-        J = reg(PO, 10, 13)
-        w0 = OWN[t]
+            tt(reg("Ri", 0, 6, 64 * d, 64 * d + 64), reg("R1", 0, 6, 64 * d, 64 * d + 64), reg("R1", 0, 6, 64 - 64 * d, 128 - 64 * d), OP.min)
+        ts(reg("Di", 0, 3), reg("Ri", 0, 3), 511, OP.bitwise_and)
+        ts(reg("Di", 3, 6), reg("Ri", 0, 3), 9, OP.logical_shift_right)
+        ts(reg("Di", 6, 9), reg("Ri", 3, 6), 1023, OP.bitwise_and)
+        copy(reg(PO, 0, 9), reg("Di", 0, 9))
+        J, w0 = reg(Ju, 0, 3), OWN[t]
         pick(PK, 144, "W", wend, reg(PO, 0, 9))
+        ts(reg("Ji", 0, 3), reg("Ri", 3, 6), 10, OP.logical_shift_right)
+        copy(J, reg("Ji", 0, 3))
         if t < 2:
-            SL, SR = "SL%d" % t, "SR%d" % t
-            ts(reg(SL, 0, 3), reg(Rf, 10, 13), float(256 * rank), OP.add)
+            ts(reg(SL, 0, 3), reg("Ji", 0, 3), float(256 * rank), OP.add)
             send("r_s%d" % t, lambda c: (T[SL][:, 0:3], T[SR][:, 3 * slot(c):3 * slot(c) + 3]), [reg(SL, 0, 3)])
             arrive("r_s%d" % t, incoming, reg(SR, 0, 9))
-        else:
-            scatter(reg("M", 256 * rank, 256 * rank + 256), J, reg("ID", w0, w0 + K))
-        for c in range(3):
-            dma("Y", "d_nd", T.nd[t:t + 1, 16 * c:16 * c + 16], T[Rf][0:16, 10 + c:11 + c], [reg(Rf, 10 + c, 11 + c, 0, 16)], [])
+        if t == 0:
+            quant("Qa", 256, 512, "at", 1024)
+        scatter(reg("M", 256 * rank, 256 * rank + 256), J, reg("ID", w0, w0 + K))
         for b in range(4):
             mm(b, "Qa", 128 * b, PK, 0, 144)
         if t == 0:
             mm(7, "UV2", 0, "W", FAR, 3 * LC)
         for b in range(4):
             copy(reg("S0", K * b, K * b + K), ps(b, 0, K), "S")
+        for b in range(4):
             gather(reg("BS", b, 4 * K, st=4), reg("bbT", 256 * b, 256 * b + 256), J, "S")
-        if t == 0:
-            copy(reg("E1", FAR, FAR + 3 * LC), ps(7, 0, 3 * LC), "S")
         if t == 2:
             gather(reg("FD", 0, 512), reg("M", 256 * rank, 256 * rank + 256), reg("DL", 0, 32), "S")
+        else:
+            gather(reg("PC", 0, 192), reg("M", 0, 1024), reg("nbo", 0, 12), "S")
+            gather(reg("PD", 0, 256), reg("PC", 0, 192), reg("KDL", 0, 16), "S")
+        if t == 0:
+            copy(reg("E1", 0, 256), ps(5, 0, 256), "S")
+            copy(reg("E1", FAR, FAR + 3 * LC), ps(7, 0, 3 * LC), "S")
         for w in range(5):
             for b, i in ((w, 0), (w - 1, 1)):
                 if 0 <= b < 4:
@@ -417,19 +429,36 @@ def rank_program(g, core, T, topo):
         ts(reg("S3", 0, 4 * K), reg("S2", 0, 4 * K), 13421773.0 * 2.0 ** -28, OP.mult)
         tt(reg("H", 0, 4 * K), reg("S3", 0, 4 * K), reg("BS", 0, 4 * K), OP.add)
         quant("W", w0, w0 + 128, "H")
+        nf = reg("nf%d" % t, 0, 3)
         if t < 2:
             ship("r_n%d" % t, "W", lambda c: w0, K, lambda c: ARR[t] + K * slot(c), w0, w0 + K)
             arrive("r_n%d" % t, 2 * incoming, *both("W", ARR[t], ARR[t] + 3 * K))
             mm(7, "UV2", 0, "W", w0, 128)
             copy(reg("E1", w0, w0 + 128), ps(7, 0, 128), "S")
-            scatter(reg("M", 256 * rank, 256 * rank + 256), J, reg("ID", w0, w0 + K))
+            turn(reg("PT", 0, 256), reg("PD", 0, 256))
+            copy(reg("EO", 0, 8), reg("PT", 0, 256, st=32))
+            copy(nf, reg("Ji", 0, 3))
             scatter(reg("M", 0, 1024), reg(SR, 0, 9), reg("ID", ARR[t], ARR[t] + 3 * K))
+            gather(reg("PC2", 0, 192), reg("M", 0, 1024), reg("nbo", 0, 12), "S")
+            gather(reg("PD", 256, 384), reg("PC2", 0, 192), reg("KDL", 16, 24), "S")
+            gather(reg("EG", 0, 128), reg("E1", 0, FAR), reg("EO", 0, 8))
+            tt(z[0], EG[0], EG[1], OP.add)
+            payload01("PC")
+            turn(reg("PT", 256, 384), reg("PD", 256, 384))
+            copy(reg("EO", 8, 12), reg("PT", 256, 384, st=32))
+            payload2("PC2")
+        else:
+            turn(reg("FT", 0, 512), reg("FD", 0, 512))
+            copy(reg("FO", 0, 16), reg("FT", 0, 512, st=32))
+            pick("FIN", 256, "W", WC, reg("FO", 0, 16))
+            copy(nf, reg("Ji", 0, 3))
+        for c in range(3):
+            dma("Y", "d_nd", T.nd[t:t + 1, 16 * c:16 * c + 16], T[nf[0]][0:16, c:c + 1], [nf], [])
         if t == 0:
             quant("Qw", 0, 128, "wt")
+            for h in range(2):
+                copy(reg("DL", h, 32, st=2), reg("IC", 0, 16))
 
-    turn(reg("FT", 0, 512), reg("FD", 0, 512))
-    copy(reg("FO", 0, 16), reg("FT", 0, 512, st=32))
-    pick("FIN", 256, "W", WC, reg("FO", 0, 16))
     dma("Y", "d_out", T.oc[:, 0:1024], cb("FIN", 0, 256), [reg("FIN", 0, 256)], [])
     for k in range(4):
         dma("Y", "d_out", T.osc[4 * k:4 * k + 4, 0:256], T.FINs[32 * k:32 * k + 4, 0:256], [reg("FINs", 0, 256)], [])

@@ -8,17 +8,20 @@ ARR = [FAR + 3 * LC, FAR + 3 * LC + 3 * K]
 OWN.append(ARR[1] + 3 * K)
 WEND = [ARR[0], ARR[1], OWN[2]]
 WC = OWN[2] + 128
-TINY = 2.0 ** -120
+TINY = 2.0 ** -122
 PRED = 1.0 - 2.0 ** -24
 STEP, MID = 2.0 ** 19, 2.0 ** 24
+SCN_S = 3
+LEN_S = 2
+CY, LAT, LOAD, HOP = 1.05e-3, 0.15, 2.0, 2.5
 
 BUF = {
-    "float32": "ID:%d C32:8 C16:16 C12:12 tf:8 GCOL:8 JB:64 IC:16 ICS:8 TB:4 Fm:128 Ft:128 CK:32 C1:32 PADD:1 FR:192 SLf:256 LJ:768 LS:3 M:1024 ec:2 EM:1024 FE:192 E1:%d fb:64 PC:192 PC2:192 PAB:128 PD:384 PT:384 EG:192 z1:64 z2:64 z3:64 z4:64 zr:64 ZT:64 zB:64 zr0:64 Zc:320 KB:64 KR:64 KEY:128 DK:384 R0:6 R1:6 nf0:3 nf1:3 nf2:3 S0:192 S1:192 S2:192 S3:192 FD:512 FT:512 ys:256" % (WC, OWN[2]),
-    "bfloat16": "ZB:256 xt:1024 bt:1024 at:2048 wt:512 uvt:512 bbT:1024 EQ:2048 SC:1024 PB:256 PR:256 SCN:256 LE:768 LC2:384 MK:512 RS:256 BS:192 H:512",
-    "int32": "pI:2 ti:8 nbt:12 Ri:6 Di:9 Ji:3",
-    "uint16": "UL:16 DL:32 KDL:24 nbo:12 nbe:12 FA:256 LST:6 LA:18 LO:18 EO:12 PO0:10 PO1:10 PO2:10 J0:4 J1:4 J2:4 SL0:4 SL1:4 SR0:9 SR1:9 FO:16",
+    "float32": "ID:%d C12:12 tf:8 GCOL:8 JB:64 IC:16 ICS:8 TB:4 Fm:128 Ft:128 CK:32 C1:32 PADD:1 FRA:192 FRB:192 FR:192 SLf:256 LJ:768 LS:6 SS:8 SJ:256 Mo:256 M:1024 ec:2 EM:1024 E1:%d fb:64 PC:192 PAB:128 PAYT:128 PDn:384 PTn:384 PD:384 PT:384 EG:192 z0:64 z1:64 z2:64 zr:64 ZT:64 zB:64 zK:64 zr0:64 Zc:320 RS:256 KB:128 KEY:128 DK:384 R0:6 R1:6 nf:9 SU:768 FD:512 FT:512 ys:256" % (WC, OWN[2]),
+    "bfloat16": "ZB:256 xt:1024 bt:1024 at:2048 wt:512 uvs:32 uvt:1024 bbT:1024 EQ:2048 SC:1024 PB:256 PR:256 SCN:256 LE:1536 LC2:768 MK:512 H:512",
+    "int32": "pI:8 ti:24 nbI:12 nbP:24 Ne:60 Ri:6 Di:9 Ji:3",
+    "uint16": "UL:8 DL:32 KDL:24 nbp:24 nbo:12 nbe:12 nbD:24 nbK:12 FA:256 LST:6 LA:18 LO:18 EO:12 PO:30 J:12 SL0:4 SL1:4 SR0:9 SR1:9 FO:16",
 }
-QBUF = "Q0:256 Qb:256 Qa:512 Qw:128 UVq:128 UV2:256 SND:288 W:%d PK0:144 PK1:144 PK2:144 FIN:256" % WC
+QBUF = "Q0:256 Qb:256 Qa:512 Qw:128 UV2:256 SND:288 W:%d PK0:144 PK1:144 PK2:144 FIN:256" % WC
 SCRATCH = {"eld": ("dram", [3, 128, 2], "float32"), "ps": ("psum", [128, 4096], "float32")}
 for _d, _s in BUF.items():
     for _b in _s.split():
@@ -26,7 +29,7 @@ for _d, _s in BUF.items():
 for _b in QBUF.split():
     SCRATCH[_b.split(":")[0]] = ("sbuf", [128, int(_b.split(":")[1])], "float8_e4m3fn_x4")
     SCRATCH[_b.split(":")[0] + "s"] = ("sbuf", [128, int(_b.split(":")[1])], "uint8")
-SEMAPHORES = "v s p gq d_nb d_x d_uv d_bb d_a d_w d_q d_m d_e d_nd d_out r_e r_l r_c r_s0 r_s1 r_n0 r_n1 loc".split()
+SEMAPHORES = "v s p gq d_nb d_nc d_x d_uv d_bb d_a d_w d_q d_m d_e d_nd d_out r_e r_l r_c r_s0 r_s1 r_n0 r_n1 loc".split()
 
 
 def rank_program(g, core, T, topo):
@@ -37,8 +40,9 @@ def rank_program(g, core, T, topo):
     queue = {"V": V, "S": S, "P": PE, "G": g, "Y": Y}
     sem_of = {"V": "v", "S": "s", "P": "p", "G": "gq"}
     count = {s: 0 for s in SEMAPHORES}
+    total = {s: 0 for s in SEMAPHORES}
     know = {q: {} for q in queue}
-    snaps, touched = {}, {}
+    snaps, touched, nodes, boost = {}, {}, [], {"b": 0.0}
 
     def reg(name, c0, c1, p0=0, p1=128, st=1):
         return (name, p0, p1, c0, c1, st)
@@ -54,12 +58,18 @@ def rank_program(g, core, T, topo):
             return False
         return not (a[5] == b[5] > 1 and a[3] % a[5] != b[3] % b[5])
 
+    def width(r):
+        return -(-(r[4] - r[3]) // r[5])
+
+    def node(q, reads, writes, emit, dur, lat, sem=None, after=()):
+        nodes.append({"q": q, "r": reads, "w": writes, "emit": emit, "dur": dur, "lat": lat, "sem": sem, "after": list(after), "bonus": boost["b"]})
+        return len(nodes) - 1
+
     def order(q, reads, writes):
         want = {}
         for r, w in [(r, False) for r in reads] + [(r, True) for r in writes]:
             for (o, ow, oq, sem, val) in touched.get(r[0], []):
                 if meet(r, o) and (ow or ((w or r[0] == "ps") and oq != q)):
-                    val = count[sem] if val is None else val
                     if know[q].get(sem, 0) < val:
                         want[sem] = max(want.get(sem, 0), val)
         for s in sorted(want):
@@ -77,91 +87,159 @@ def rank_program(g, core, T, topo):
         for r in writes:
             touched.setdefault(r[0], []).append((r, True, q, sem, val))
 
-    def op(q, fn, reads, writes):
-        order(q, reads, writes)
+    def op(q, fn, reads, writes, dur):
         s = sem_of[q]
-        count[s] += 1
-        fn().then_inc(T.sem[s], 1)
-        snaps[(s, count[s])] = dict(know[q])
-        note(reads, writes, q, s, count[s])
+
+        def emit():
+            order(q, reads, writes)
+            count[s] += 1
+            fn().then_inc(T.sem[s], 1)
+            snaps[(s, count[s])] = dict(know[q])
+            note(reads, writes, q, s, count[s])
+        node(q, reads, writes, emit, max(dur, 64 * CY), LAT)
 
     def dma(q, sem, out, in_, reads, writes):
-        order(q, reads, writes)
-        count[sem] += 16
-        queue[q].dma_start(out, in_).then_inc(T.sem[sem], 16)
-        note(reads, writes, "dma", sem, None)
+        total[sem] += 16
 
-    def arrive(sem, total, *writes):
-        note([], writes, "far", sem, total)
+        def emit():
+            order(q, reads, writes)
+            count[sem] += 16
+            queue[q].dma_start(out, in_).then_inc(T.sem[sem], 16)
+            note(reads, writes, "dma", sem, total[sem])
+        node(q, reads, writes, emit, 0.07, LOAD, sem)
+
+    def arrive(sem, n, after, *writes):
+        node("far", [], list(writes), lambda: note([], writes, "far", sem, n), 0.0, LAT, None, after)
+
+    def plan():
+        n = len(nodes)
+        hist, deps, group = {}, [], {}
+        for i, x in enumerate(nodes):
+            if x["sem"] is not None:
+                group.setdefault(x["sem"], []).append(i)
+        for i, x in enumerate(nodes):
+            d = set(x["after"])
+            for r, w in [(r, False) for r in x["r"]] + [(r, True) for r in x["w"]]:
+                for (o, ow, j) in hist.get(r[0], []):
+                    if j != i and meet(r, o) and (ow or w or (r[0] == "ps" and nodes[j]["q"] != x["q"])):
+                        d.add(j)
+            for j in list(d):
+                if nodes[j]["sem"] is not None and nodes[j]["sem"] != x["sem"]:
+                    d.update(group[nodes[j]["sem"]])
+            d.discard(i)
+            deps.append(d)
+            for r in x["r"]:
+                hist.setdefault(r[0], []).append((r, False, i))
+            for r in x["w"]:
+                hist.setdefault(r[0], []).append((r, True, i))
+        succ = [[] for _ in range(n)]
+        for i in range(n):
+            for j in deps[i]:
+                succ[j].append(i)
+        prio, left = [0.0] * n, [len(s) for s in succ]
+        stack = [i for i in range(n) if not left[i]]
+        while stack:
+            i = stack.pop()
+            x = nodes[i]
+            prio[i] = x["dur"] + x["bonus"] + max([x["lat"] + prio[k] for k in succ[i]] + [0.0])
+            for j in deps[i]:
+                left[j] -= 1
+                if not left[j]:
+                    stack.append(j)
+        busy = {q: [] for q in queue}
+        start, over = [0.0] * n, [0.0] * n
+        for i in sorted(range(n), key=lambda i: (-prio[i], i)):
+            x = nodes[i]
+            t = max([over[j] for j in deps[i]] + [0.0])
+            if x["q"] in busy:
+                b, at = busy[x["q"]], 0
+                for at in range(len(b) + 1):
+                    if at == len(b) or t + x["dur"] <= b[at][0] + 1e-9:
+                        break
+                    t = max(t, b[at][1])
+                b.insert(at, (t, t + x["dur"]))
+            start[i], over[i] = t, t + x["dur"] + x["lat"]
+        for i in sorted(range(n), key=lambda i: (start[i], -prio[i], i)):
+            nodes[i]["emit"]()
 
     def sc(x):
         return ap(x) if isinstance(x, tuple) else x
+
+    def short(r):
+        return SCRATCH[r[0]][2] in ("bfloat16", "uint16")
 
     def act(out, in_, f, bias=None, scale=None, accum=None):
         kw = {}
         if bias is not None: kw["bias"] = sc(bias)
         if scale is not None: kw["scale"] = sc(scale)
         if accum is not None: kw["accum_out"] = ap(accum)
-        op("S", lambda: S.activation(ap(out), ap(in_), f, **kw), [in_] + [x for x in (bias, scale) if isinstance(x, tuple)], [out] + ([accum] if accum else []))
+        op("S", lambda: S.activation(ap(out), ap(in_), f, **kw), [in_] + [x for x in (bias, scale) if isinstance(x, tuple)], [out] + ([accum] if accum else []), width(in_) * CY)
 
     def copy(out, in_, q="V"):
         if q == "V":
-            op("V", lambda: V.tensor_copy(ap(out), ap(in_)), [in_], [out])
+            op("V", lambda: V.tensor_copy(ap(out), ap(in_)), [in_], [out], width(in_) * CY)
         else:
             act(out, in_, AF.Copy)
 
     def ts(out, in_, s1, op0, s2=None, op1=None):
         rd = [in_] + [x for x in (s1, s2) if isinstance(x, tuple)]
+        d = width(in_) * CY * (0.5 if short(out) and short(in_) else 1.0)
         if op1 is None:
-            op("V", lambda: V.tensor_scalar(ap(out), ap(in_), sc(s1), None, op0), rd, [out])
+            op("V", lambda: V.tensor_scalar(ap(out), ap(in_), sc(s1), None, op0), rd, [out], d)
         else:
-            op("V", lambda: V.tensor_scalar(ap(out), ap(in_), sc(s1), sc(s2), op0, op1), rd, [out])
+            op("V", lambda: V.tensor_scalar(ap(out), ap(in_), sc(s1), sc(s2), op0, op1), rd, [out], d)
 
     def tt(out, a, b, o):
-        op("V", lambda: V.tensor_tensor(ap(out), ap(a), ap(b), o), [a, b], [out])
+        op("V", lambda: V.tensor_tensor(ap(out), ap(a), ap(b), o), [a, b], [out], width(out) * CY * 2)
+
+    def tt_by(out, win, off, b, o):
+        op("V", lambda: V.tensor_tensor(ap(out), ap(win).indirect(ap(off)), ap(b), o), [win, off, b], [out], 0.05 + width(out) * CY * 1.6)
 
     def scan(out, a, b):
-        op("V", lambda: V.tensor_tensor_scan(ap(out), ap(a), ap(b), 0.0, OP.add, OP.add), [a, b], [out])
+        op("V", lambda: V.tensor_tensor_scan(ap(out), ap(a), ap(b), 0.0, OP.add, OP.add), [a, b], [out], width(out) * CY * (0.5 if short(out) else 1.0))
 
     def turn(out, in_):
-        op("V", lambda: V.transpose(ap(out), ap(in_)), [in_], [out])
+        op("V", lambda: V.transpose(ap(out), ap(in_)), [in_], [out], width(out) * CY)
 
     def fill(out, x):
-        op("V", lambda: V.memset(ap(out), x), [], [out])
+        op("V", lambda: V.memset(ap(out), x), [], [out], width(out) * CY)
 
-    def iota(out, pattern, base, alone=False):
-        if alone and count["gq"] > know["G"].get("gq", 0):
-            g.wait_ge(T.sem.gq, count["gq"])
-            know["G"]["gq"] = count["gq"]
-        if out[0] == "pI":
-            op("G", lambda: g.iota(ap(out), pattern, base, 1), [], [out])
+    def least(o, i):
+        op("V", lambda: V.tensor_reduce(ap(o), ap(i), AxisListType.X, OP.min, apply_absolute_value=True), [i], [o], width(i) * CY)
+
+    def iota(out, pattern, base, mult=0):
+        n = 1
+        for s, c in pattern:
+            n *= c
+        if SCRATCH[out[0]][2] == "int32":
+            op("G", lambda: g.iota(ap(out), pattern, base, mult), [], [out], 0.13 + 2 * n * CY)
         else:
-            op("G", lambda: g.iota(ap(out), pattern, base, 0, allow_small_or_imprecise_dtypes=True), [], [out])
+            op("G", lambda: g.iota(ap(out), pattern, base, mult, allow_small_or_imprecise_dtypes=True), [], [out], 0.13 + 2 * n * CY)
 
     def gather(out, win, off, q="V"):
         if q == "V":
-            op("V", lambda: V.tensor_copy(ap(out), ap(win).indirect(ap(off))), [win, off], [out])
+            op("V", lambda: V.tensor_copy(ap(out), ap(win).indirect(ap(off))), [win, off], [out], 0.05 + 1.6 * width(out) * CY)
         else:
-            op("S", lambda: S.activation(ap(out), ap(win).indirect(ap(off)), AF.Copy), [win, off], [out])
+            op("S", lambda: S.activation(ap(out), ap(win).indirect(ap(off)), AF.Copy), [win, off], [out], 0.065 + 1.6 * width(out) * CY)
 
     def scatter(win, off, in_):
-        op("V", lambda: V.tensor_copy(ap(win).indirect(ap(off)), ap(in_)), [in_, off], [win])
+        op("V", lambda: V.tensor_copy(ap(win).indirect(ap(off)), ap(in_)), [in_, off], [win], 0.05 + 3 * width(in_) * CY)
 
-    def pick(dst, c1, src, w1, off):
-        a, b = reg(dst, 0, c1), reg(src, 0, w1)
-        op("V", lambda: V.tensor_copy(ap(a).bitcast(dt.uint32), ap(b).bitcast(dt.uint32).indirect(ap(off))), [b, off], [a])
-        gather(reg(dst + "s", 0, c1), reg(src + "s", 0, w1), off, "S")
+    def pick(dst, c0, c1, src, w1, off):
+        a, b = reg(dst, c0, c1), reg(src, 0, w1)
+        op("V", lambda: V.tensor_copy(ap(a).bitcast(dt.uint32), ap(b).bitcast(dt.uint32).indirect(ap(off))), [b, off], [a], 0.05 + 1.6 * (c1 - c0) * CY)
+        gather(reg(dst + "s", c0, c1), reg(src + "s", 0, w1), off, "S")
 
     def both(q, c0, c1):
         return [reg(q, c0, c1), reg(q + "s", c0, c1)]
 
     def quant(q, c0, c1, t, e0=0):
         e1 = e0 + 4 * (c1 - c0)
-        op("V", lambda: V.quantize_mx(T[q][:, c0:c1], T[q + "s"][:, c0:c1], T[t][:, e0:e1]), [reg(t, e0, e1)], both(q, c0, c1))
+        op("V", lambda: V.quantize_mx(T[q][:, c0:c1], T[q + "s"][:, c0:c1], T[t][:, e0:e1]), [reg(t, e0, e1)], both(q, c0, c1), 0.012 + 1.06 * (c1 - c0) * CY)
 
     def mm(bank, a, a0, b, b0, n):
         o = reg("ps", 512 * bank, 512 * bank + n)
-        op("P", lambda: PE.matmul_mx(ap(o), T[a][:, a0:a0 + 128], T[a + "s"][:, a0:a0 + 128], T[b][:, b0:b0 + n], T[b + "s"][:, b0:b0 + n], True, True), both(a, a0, a0 + 128) + both(b, b0, b0 + n), [o])
+        op("P", lambda: PE.matmul_mx(ap(o), T[a][:, a0:a0 + 128], T[a + "s"][:, a0:a0 + 128], T[b][:, b0:b0 + n], T[b + "s"][:, b0:b0 + n], True, True), both(a, a0, a0 + 128) + both(b, b0, b0 + n), [o], (n + 16) * CY)
 
     def ps(bank, c0, c1, p0=0, p1=128):
         return reg("ps", 512 * bank + c0, 512 * bank + c1, p0, p1)
@@ -184,14 +262,16 @@ def rank_program(g, core, T, topo):
         return (rank - T.rank_of(dst) - 1) % 4
 
     def send(sem, pair, reads):
-        order("G", reads, [])
-        tr = []
-        for c in mine:
-            rid, pid, _ = topo.addr(c)
-            s, d = pair(c)
-            tr.append(RemoteDMATransfer(dst_ids=[DstId(rid=rid, pnc=pid)], dma_engine_mask=sum(1 << e for e in mine[c]), remote_sem=T.sem[sem], src=s, dst=d))
-            count["loc"] += len(mine[c])
-        g.remote_dma_fused(tr, local_sem=T.sem.loc)
+        def emit():
+            order("G", reads, [])
+            tr = []
+            for c in mine:
+                rid, pid, _ = topo.addr(c)
+                s, d = pair(c)
+                tr.append(RemoteDMATransfer(dst_ids=[DstId(rid=rid, pnc=pid)], dma_engine_mask=sum(1 << e for e in mine[c]), remote_sem=T.sem[sem], src=s, dst=d))
+                count["loc"] += len(mine[c])
+            g.remote_dma_fused(tr, local_sem=T.sem.loc)
+        return [node("G", reads, [], emit, 0.3, HOP)]
 
     incoming = sum(len(lanes(c)[core]) for c in sources)
 
@@ -199,8 +279,8 @@ def rank_program(g, core, T, topo):
         return T[name][:, c0:c1].bitcast(dt.uint8)
 
     def ship(sem, q, s0, n, dst, c0, c1):
-        send(sem, lambda c: (cb(q, s0(c), s0(c) + n), cb("W", dst(c), dst(c) + n)), [reg(q, c0, c1)])
-        send(sem, lambda c: (T[q + "s"][:, s0(c):s0(c) + n], T.Ws[:, dst(c):dst(c) + n]), [reg(q + "s", c0, c1)])
+        a = send(sem, lambda c: (cb(q, s0(c), s0(c) + n), cb("W", dst(c), dst(c) + n)), [reg(q, c0, c1)])
+        return a + send(sem, lambda c: (T[q + "s"][:, s0(c):s0(c) + n], T.Ws[:, dst(c):dst(c) + n]), [reg(q + "s", c0, c1)])
 
     def ti(i):
         return reg("ti", i, i + 1)
@@ -208,81 +288,101 @@ def rank_program(g, core, T, topo):
     def tf(i):
         return reg("tf", i, i + 1)
 
-    pI = reg("pI", 0, 1)
-    iota(pI, [[0, 1]], 0)
-    iota(reg("ID", 0, 1024), [[1, 1024]], 0)
-    iota(reg("C32", 0, 8), [[32, 8]], 0)
-    iota(reg("C16", 0, 16), [[16, 16]], 0)
-    iota(reg("ZB", 0, 256), [[0, 256]], 0)
-    iota(reg("C12", 0, 12), [[1, 3], [48, 4]], 0)
-    iota(reg("CK", 0, 32), [[0, 32]], int(STEP))
-    iota(reg("C1", 0, 32), [[0, 32]], 1)
-    iota(reg("ID", 1024, WC), [[1, WC - 1024]], 1024)
-    for a in range(4):
-        iota(reg("PADD", 0, 1, 32 * a, 32 * a + 32), [[0, 1]], FAR + LC * ((a - rank - 1) % 4 % 3) - 1, True)
-    fill(reg("uvt", 0, 512), 0.0)
+    for h in range(2):
+        for a in range(4):
+            p0, b0 = 32 * a + 16 * h, 24 * (a // 2)
+            dma("YS"[h], "d_nb", T.nbP[p0:p0 + 16, :], T.nb[:, b0:b0 + 24], [], [reg("nbP", 0, 24, p0, p0 + 16)])
     dma("Y", "d_x", T.xt[:], T.x[:], [], [reg("xt", 0, 1024)])
+    dma("S", "d_uv", T.uvs[:, 0:4], T.u[:, 0:4], [], [reg("uvs", 0, 4)])
+    dma("S", "d_uv", T.uvs[:, 16:20], T.v[:, 0:4], [], [reg("uvs", 16, 20)])
     for h in range(2):
         for a in range(4):
             p0 = 32 * a + 16 * h
-            dma("YS"[h], "d_nb", T.nbt[p0:p0 + 16, :], T.nb[:, 12 * a:12 * a + 12], [], [reg("nbt", 0, 12, p0, p0 + 16)])
-    dma("Y", "d_uv", T.uvt[:, 0:4], T.u[:, 0:4], [], [reg("uvt", 0, 4)])
-    dma("Y", "d_uv", T.uvt[:, 8:12], T.v[:, 0:4], [], [reg("uvt", 8, 12)])
-    dma("S", "d_bb", T.bt[:], T.bb[:], [], [reg("bt", 0, 1024)])
+            dma("Y", "d_nc", T.nbI[p0:p0 + 16, :], T.nb[:, 12 * a:12 * a + 12], [], [reg("nbI", 0, 12, p0, p0 + 16)])
+    dma("Y", "d_bb", T.bt[:], T.bb[:], [], [reg("bt", 0, 1024)])
     dma("Y", "d_a", T.at[:], T.a[:], [], [reg("at", 0, 2048)])
     dma("Y", "d_w", T.wt[:], T.w[:], [], [reg("wt", 0, 512)])
+    pI = reg("pI", 0, 1)
+    iota(reg("pI", 0, 8), [[0, 8]], 0, 1)
+    iota(reg("ID", 0, 256), [[1, 256]], 0)
+    iota(reg("C12", 0, 12), [[1, 3], [48, 4]], 0)
+    for q in range(4):
+        if q != rank:
+            iota(reg("EM", 256 * q, 256 * q + 256), [[0, 256]], 0)
+    iota(reg("M", 256 * rank, 256 * rank + 256), [[0, 256]], 0)
+    for k, q in ((1, "V"), (2, "S"), (3, "V"), (4, "S")):
+        n = min(256, WC - 256 * k)
+        if q == "V":
+            ts(reg("ID", 256 * k, 256 * k + n), reg("ID", 0, n), 256.0 * k, OP.add)
+        else:
+            act(reg("ID", 256 * k, 256 * k + n), reg("ID", 0, n), AF.Identity, bias=256.0 * k)
     ts(ti(0), pI, 96, OP.bitwise_and)
     ts(ti(1), pI, 31, OP.bitwise_and)
     ts(ti(2), pI, 15, OP.bitwise_and)
+    ts(reg("ti", 8, 16), reg("pI", 0, 8), 3, OP.bitwise_and)
     ts(tf(4), ti(0), 7.0, OP.mult)
     copy(tf(3), ti(2))
-    ts(tf(2), ti(0), 2048.0, OP.mult)
+    ts(tf(2), ti(0), 2048.0, OP.mult, -MID, OP.add)
     tt(tf(0), tf(4), pI, OP.add)
     copy(tf(5), ti(1))
     ts(tf(6), ti(1), 32.0, OP.add)
     ts(tf(7), ti(2), 3.0, OP.mult)
-    fill(reg("UL", 0, 8), 0)
-    fill(reg("UL", 8, 16), 2)
+    copy(reg("UL", 0, 8), reg("ti", 8, 16))
+    fill(reg("ZB", 0, 256), 0.0)
+    fill(reg("CK", 0, 32), STEP)
+    fill(reg("C1", 0, 32), 1.0)
     fill(reg("H", 0, 512), 0.0)
     fill(reg("E1", OWN[0] + 128, FAR), 0.0)
-    act(reg("GCOL", 0, 8), reg("C32", 0, 8), AF.Identity, bias=tf(0))
-    act(reg("IC", 0, 16), reg("C16", 0, 16), AF.Identity, bias=tf(3))
+    for a in range(4):
+        fill(reg("PADD", 0, 1, 32 * a, 32 * a + 32), float(FAR + LC * ((a - rank - 1) % 4 % 3) - 1))
+    act(reg("GCOL", 0, 8), reg("ID", 0, 8), AF.Identity, scale=32.0, bias=tf(0))
+    act(reg("IC", 0, 16), reg("ID", 0, 16), AF.Identity, scale=16.0, bias=tf(3))
     act(reg("ICS", 0, 8), reg("IC", 0, 8), AF.Identity, scale=-1.0, bias=-0.5)
-    for q in range(8):
-        act(reg("EM", 128 * q, 128 * q + 128), reg("ID", 0, 128), AF.Identity, scale=2.0, bias=float(256 * (q // 2) + q % 2))
-    copy(reg("nbo", 0, 12), reg("nbt", 0, 12))
-    gather(reg("FR", 0, 192), reg("ID", 0, 1024), reg("nbo", 0, 12))
-    gather(reg("FE", 0, 192), reg("EM", 0, 1024), reg("nbo", 0, 12), "S")
-    copy(reg("FA", 0, 64), reg("FR", 2, 192, st=3))
-    for d in range(4):
-        s = d ^ 1
-        copy(reg("FA", 64, 128, 32 * d, 32 * d + 32), reg("FA", 0, 64, 32 * s, 32 * s + 32))
+    copy(reg("nbp", 0, 24), reg("nbP", 0, 24))
+    gather(reg("FRA", 0, 192), reg("ID", 0, 1024), reg("nbp", 0, 12))
+    gather(reg("FRB", 0, 192), reg("ID", 0, 1024), reg("nbp", 12, 24), "S")
+    copy(reg("FA", 0, 64), reg("FRA", 2, 192, st=3))
+    copy(reg("FA", 64, 128), reg("FRB", 2, 192, st=3))
     copy(reg("FA", 128, 256, 0, 64), reg("FA", 0, 128, 64, 128))
     copy(reg("FA", 128, 256, 64, 128), reg("FA", 0, 128, 0, 64))
+    for k in range(2):
+        o = 512 * k
+        gather(reg("uvt", o, o + 128), reg("uvs", 16 * k, 16 * k + 4), reg("UL", 0, 8), "S")
+        copy(reg("uvt", o + 128, o + 256), reg("uvt", o, o + 128), "S")
+        copy(reg("uvt", o + 256, o + 512), reg("uvt", o, o + 256), "S")
     quant("Q0", 0, 256, "xt")
-    quant("UVq", 0, 128, "uvt")
+    quant("UV2", 0, 128, "uvt")
+    quant("UV2", 128, 256, "uvt", 512)
     for c in range(2):
-        mm(c, "Q0", 128 * c, "UVq", 0, 128)
+        mm(c, "Q0", 128 * c, "UV2", 0, 128)
     for c in range(2):
         copy(reg("ec", c, c + 1), ps(c, 0, 1), "S")
-    send("r_e", lambda c: (T.ec[:, 0:2], T.eld[slot(c)]), [reg("ec", 0, 2)])
-    arrive("r_e", incoming, reg("eld", 0, 3))
+    i = send("r_e", lambda c: (T.ec[:, 0:2], T.eld[slot(c)]), [reg("ec", 0, 2)])
+    arrive("r_e", incoming, i, reg("eld", 0, 3))
     dma("Y", "d_q", cb("W", 0, 256), cb("Q0", 0, 256), [reg("Q0", 0, 256)], [reg("W", 0, 256)])
     dma("Y", "d_q", T.Ws[:, 0:256], T.Q0s[:, 0:256], [reg("Q0s", 0, 256)], [reg("Ws", 0, 256)])
     for c in range(8):
-        ts(reg("EQ", 256 * c, 256 * c + 256), reg("FA", 0, 256), reg("GCOL", c, c + 1), OP.is_equal)
-        scan(reg("SC", 128 * c, 128 * c + 128), reg("EQ", 256 * c, 256 * c + 128), reg("EQ", 256 * c + 128, 256 * c + 256))
-        act(reg("PB", 32 * c, 32 * c + 32), reg("ZB", 0, 32), AF.Sign, bias=reg("SC", 128 * c + 127, 128 * c + 128))
+        eq = reg("EQ", 256 * c, 256 * c + 256)
+        ts(eq, reg("FA", 0, 256), reg("GCOL", c, c + 1), OP.is_equal)
+        if c < 8 - SCN_S:
+            scan(reg("SC", 128 * c, 128 * c + 128), reg("EQ", 256 * c, 256 * c + 128), reg("EQ", 256 * c + 128, 256 * c + 256))
+            n = reg("SC", 128 * c + 127, 128 * c + 128)
+        else:
+            n = reg("SS", c, c + 1)
+            act(reg("SJ", 0, 256), eq, AF.Copy, accum=n)
+        act(reg("PB", 32 * c, 32 * c + 32), reg("ZB", 0, 32), AF.Sign, bias=n)
     turn(reg("PR", 0, 256), reg("PB", 0, 256))
     scan(reg("SCN", 0, 256), reg("PR", 0, 256), reg("ZB", 0, 256))
-    for c in range(3):
+    nv = 6 - LEN_S
+    for c in range(nv):
         ts(reg("LE", 256 * c, 256 * c + 256), reg("SCN", 0, 256), reg("IC", c, c + 1), OP.is_le)
         scan(reg("LC2", 128 * c, 128 * c + 128), reg("LE", 256 * c, 256 * c + 128), reg("LE", 256 * c + 128, 256 * c + 256))
-        act(reg("LJ", 256 * c, 256 * c + 255), reg("SCN", 0, 255), AF.Sign, bias=reg("ICS", 3 + c, 4 + c), accum=reg("LS", c, c + 1))
-    ts(reg("LST", 0, 3), reg("LC2", 127, 384, st=128), 255.0, OP.min)
-    ts(reg("LST", 3, 6), reg("LS", 0, 3), -0.5, OP.mult, 127.5, OP.add)
-    send("r_l", lambda c: (T.LST[:, 0:6], T.LA[:, 6 * slot(c):6 * slot(c) + 6]), [reg("LST", 0, 6)])
-    arrive("r_l", incoming, reg("LA", 0, 18))
+    for c in range(nv, 6):
+        act(reg("LJ", 256 * (c % 3), 256 * (c % 3) + 255), reg("SCN", 0, 255), AF.Sign, bias=reg("ICS", c, c + 1), accum=reg("LS", c, c + 1))
+    ts(reg("LST", 0, nv), reg("LC2", 127, 128 * nv, st=128), 255.0, OP.min)
+    ts(reg("LST", nv, 6), reg("LS", nv, 6), -0.5, OP.mult, 127.5, OP.add)
+    i = send("r_l", lambda c: (T.LST[:, 0:6], T.LA[:, 6 * slot(c):6 * slot(c) + 6]), [reg("LST", 0, 6)])
+    arrive("r_l", incoming, i, reg("LA", 0, 18))
     for d in range(4):
         i = 0
         while i < 3:
@@ -295,15 +395,27 @@ def rank_program(g, core, T, topo):
         if q != rank:
             for d in range(4):
                 dma("Y", "d_m", T.M[32 * d:32 * d + 32, 256 * q:256 * q + 256], T.SLf[32 * q:32 * q + 32, :], [reg("SLf", 0, 256, 32 * q, 32 * q + 32)], [reg("M", 256 * q, 256 * q + 256, 32 * d, 32 * d + 32)])
+    n0, n1, n2, n3, n4 = [reg("Ne", 12 * i, 12 * i + 12) for i in range(5)]
+    nbI = reg("nbI", 0, 12)
+    ts(n0, nbI, 127, OP.bitwise_and)
+    ts(n1, nbI, 7, OP.logical_shift_right, 1, OP.bitwise_and)
+    tt(n2, n0, nbI, OP.add)
+    ts(n3, n1, -127.0, OP.mult)
+    tt(n4, n2, n3, OP.add)
+    copy(reg("nbe", 0, 12), n4)
+    copy(reg("nbo", 0, 12), nbI)
     for h in range(2):
         ts(reg("KDL", h, 24, st=2), reg("C12", 0, 12), tf(7), OP.add)
-    gather(reg("PD", 0, 384), reg("FE", 0, 192), reg("KDL", 0, 24), "S")
-    pick("UV2", 256, "UVq", 128, reg("UL", 0, 16))
+    gather(reg("FR", 0, 192), reg("ID", 0, 1024), reg("nbo", 0, 12), "S")
+    gather(reg("PDn", 0, 384), reg("FR", 0, 192), reg("KDL", 0, 24), "S")
+    turn(reg("PTn", 0, 384), reg("PDn", 0, 384))
+    ts(reg("nbD", 0, 16), reg("PTn", 0, 256, st=16), float(-256 * rank), OP.add)
+    ts(reg("nbK", 0, 8), reg("PTn", 0, 256, st=32), float(-256 * rank), OP.add)
+    copy(reg("nbD", 16, 24), reg("PTn", 256, 384, st=16))
+    copy(reg("nbK", 8, 12), reg("PTn", 256, 384, st=32))
     quant("Qb", 0, 256, "bt")
     mm(5, "UV2", 0, "Q0", 0, 256)
     mm(4, "UV2", 128, "Qb", 0, 256)
-    turn(reg("PT", 0, 384), reg("PD", 0, 384))
-    copy(reg("nbe", 0, 12), reg("PT", 0, 384, st=32))
     for b in range(2):
         ts(reg("Ft", 64 * b, 64 * b + 64), reg("ID", 0, 64), tf(5 + b), OP.is_lt, 2.0 ** -24, OP.mult)
     for c in range(2):
@@ -311,162 +423,169 @@ def rank_program(g, core, T, topo):
     for a in range(4):
         copy(reg("fb", 0, 64, 32 * a, 32 * a + 32), ps(4, 64 * a, 64 * a + 64, 32 * a, 32 * a + 32), "S")
     act(reg("Fm", 0, 128), reg("Ft", 0, 128), AF.Identity, bias=PRED)
-    copy(reg("M", 256 * rank, 256 * rank + 256), reg("ID", 0, 256), "S")
+    copy(reg("Mo", 0, 256), reg("ID", 0, 256), "S")
     act(reg("JB", 0, 64), reg("ID", 0, 64), AF.Identity, scale=1024.0, bias=tf(2))
     act(reg("TB", 0, 4), reg("IC", 0, 4), AF.Identity, scale=-STEP, bias=MID)
     for t in range(4):
         copy(reg("bbT", 256 * t, 256 * t + 256), reg("bt", t, 1024, st=4), "S")
     for d in range(4):
         copy(reg("LO", 0, 18, 32 * d, 32 * d + 32), reg("LA", 0, 18, 32 * rank, 32 * rank + 32))
-    pick("SND", 288, "Q0", 256, reg("LO", 0, 18))
-    ship("r_c", "SND", lambda c: LC * sources.index(c), LC, lambda c: FAR + LC * slot(c), 0, 3 * LC)
-    arrive("r_c", 2 * incoming, *both("W", FAR, FAR + 3 * LC))
+    pick("SND", 0, 288, "Q0", 256, reg("LO", 0, 18))
+    i = ship("r_c", "SND", lambda c: LC * sources.index(c), LC, lambda c: FAR + LC * slot(c), 0, 3 * LC)
+    arrive("r_c", 2 * incoming, i, *both("W", FAR, FAR + 3 * LC))
 
-    EG = [reg("EG", 64 * k, 64 * k + 64) for k in range(3)]
-    z = [reg(n, 0, 64) for n in ("z1", "z2", "z3", "z4", "zr")]
+    z0, z1, z2, EG = reg("z0", 0, 64), reg("z1", 0, 64), reg("z2", 0, 64), reg("EG", 0, 64)
+    M = reg("M", 0, 1024)
+    Mo = reg("Mo", 0, 256)
 
-    def payload01(pc):
-        ts(reg("zB", 0, 64), reg(pc, 1, 192, st=3), 512.0, OP.mult)
-        tt(reg("PAB", 0, 64), reg("zB", 0, 64), reg(pc, 0, 192, st=3), OP.add)
+    def payload01():
+        gather(reg("PC", 0, 128), Mo, reg("nbK", 0, 8), "S")
+        act(reg("zK", 0, 64), reg("PC", 64, 128), AF.Identity, scale=512.0, bias=-MID)
+        tt(reg("PAB", 0, 64), reg("zK", 0, 64), reg("PC", 0, 64), OP.add)
+        turn(reg("PAYT", 0, 64), reg("PAB", 0, 64))
 
-    def payload2(pc):
-        tt(reg("PAB", 64, 128), reg(pc, 2, 192, st=3), reg("JB", 0, 64), OP.add)
+    def payload2():
+        gather(reg("PC", 128, 192), M, reg("nbK", 8, 12), "S")
+        tt(reg("PAB", 64, 128), reg("PC", 128, 192), reg("JB", 0, 64), OP.add)
+        turn(reg("PAYT", 64, 128), reg("PAB", 64, 128))
 
     for t in range(R):
-        PO, PK, Ju, SL, SR = "PO%d" % t, "PK%d" % t, "J%d" % t, "SL%d" % t, "SR%d" % t
-        wend = WEND[t]
+        PK, SL, SR = "PK%d" % t, "SL%d" % t, "SR%d" % t
+        PO, J, nf = reg("PO", 10 * t, 10 * t + 9), reg("J", 4 * t, 4 * t + 3), reg("nf", 3 * t, 3 * t + 3)
+        wend, w0 = WEND[t], OWN[t]
         if t == 0:
             gather(reg("EG", 0, 192), reg("EM", 0, 1024), reg("nbe", 0, 12))
-            tt(z[0], EG[0], EG[1], OP.add)
+            tt(z0, reg("EG", 0, 192, st=3), reg("EG", 1, 192, st=3), OP.add)
+            tt(z1, z0, reg("EG", 2, 192, st=3), OP.add)
+            payload01()
+            payload2()
         else:
             a0 = ARR[t - 1]
             mm(6, "UV2", 0, "W", a0, 3 * K)
             copy(reg("E1", a0, a0 + 3 * K), ps(6, 0, 3 * K))
-            gather(EG[2], reg("E1", 0, wend), reg("EO", 8, 12))
-        tt(z[1], z[0], EG[2], OP.add)
-        tt(z[2], z[1], reg("fb", 0, 64), OP.subtract)
-        ts(z[3], z[2], -1.0, OP.mult, TINY, OP.max)
-        tt(z[4], z[2], z[3], OP.max)
-        zr = "zr"
-        turn(reg("ZT", 0, 64), z[4])
+            tt_by(z1, reg("E1", FAR, wend), reg("EO", 8, 12), z0, OP.add)
+        tt(z2, z1, reg("fb", 0, 64), OP.subtract)
+        act(reg("zr", 0, 64), z2, AF.Abs, bias=TINY)
+        turn(reg("ZT", 0, 64), reg("zr", 0, 64))
+        zr, zs = "zr", "z2"
         if t == 0:
             for b in range(2):
                 ts(reg("zB", 32 * b, 32 * b + 32), reg("C1", 0, 32), reg("ZT", 32 * b, 32 * b + 1), OP.mult)
             turn(reg("zr0", 0, 64), reg("zB", 0, 64))
-            zr = "zr0"
-        for q, d, s, w, x in (("V", 0, 2, 2, 2), ("S", 2, 0, 2, 2), ("S", 0, 1, 1, 1), ("S", 1, 0, 1, 1), ("S", 2, 3, 1, 1), ("S", 3, 2, 1, 1), ("S", 0, 3, 1, 3), ("V", 3, 0, 1, 3), ("V", 1, 2, 1, 3), ("V", 2, 1, 1, 3)):
+            zr = zs = "zr0"
+        for b in range(2):
+            tt(reg("Zc", 256 * b, 256 * b + 64), reg(zr, 0, 64), reg("Fm", 64 * b, 64 * b + 64), OP.mult)
+        for q, d, s, w, x in (("S", 0, 2, 2, 2), ("S", 2, 0, 2, 2), ("S", 0, 1, 1, 1), ("S", 1, 0, 1, 1), ("S", 2, 3, 1, 1), ("S", 3, 2, 1, 1), ("S", 0, 3, 1, 3), ("V", 3, 0, 1, 3), ("V", 1, 2, 1, 3), ("S", 2, 1, 1, 3)):
             o = reg("Zc", 64 * x, 64 * x + 64, 32 * d, 32 * d + 32 * w)
-            i = reg(zr, 0, 64, 32 * s, 32 * s + 32 * w)
+            i = reg(zs if q == "S" else zr, 0, 64, 32 * s, 32 * s + 32 * w)
+            f = PRED if s > d else 1.0
             if q == "S":
-                act(o, i, AF.Copy, scale=PRED if s > d else 1.0)
+                if t == 0:
+                    act(o, i, AF.Copy, scale=f)
+                else:
+                    act(o, i, AF.Abs, scale=f, bias=TINY * f)
             elif s > d:
-                ts(o, i, PRED, OP.mult)
+                ts(o, i, f, OP.mult)
             else:
                 copy(o, i)
         for b in range(2):
-            tt(reg("Zc", 256 * b, 256 * b + 64), reg(zr, 0, 64), reg("Fm", 64 * b, 64 * b + 64), OP.mult)
-        for b in range(2):
-            ts(reg("MK", 256 * b, 256 * b + 256), reg("Zc", 64 * b, 64 * b + 256), reg("ZT", 32 * b, 32 * b + 1), OP.is_ge)
-        for b in range(2):
+            for h in range(2):
+                o = 256 * b + 128 * h
+                ts(reg("MK", o, o + 128), reg("Zc", 64 * b + 128 * h, 64 * b + 128 * h + 128), reg("ZT", 32 * b, 32 * b + 1), OP.is_ge)
             scan(reg("RS", 128 * b, 128 * b + 128), reg("MK", 256 * b, 256 * b + 128), reg("MK", 256 * b + 128, 256 * b + 256))
-        for b in range(2):
-            ts(reg("KB", 32 * b, 32 * b + 32), reg("CK", 0, 32), reg("RS", 128 * b + 127, 128 * b + 128), OP.mult, -MID, OP.add)
-        turn(reg("KR", 0, 64), reg("KB", 0, 64))
-        if t == 0:
-            gather(reg("PC", 0, 192), reg("M", 0, 1024), reg("nbo", 0, 12), "S")
-            payload01("PC")
-            payload2("PC")
         for k in range(2):
-            tt(reg("KEY", 64 * k, 64 * k + 64), reg("KR", 0, 64), reg("PAB", 64 * k, 64 * k + 64), OP.add)
+            for b in range(2):
+                o = 64 * k + 32 * b
+                ts(reg("KB", o, o + 32), reg("CK", 0, 32), reg("RS", 128 * b + 127, 128 * b + 128), OP.mult, reg("PAYT", o, o + 1), OP.add)
+        turn(reg("KEY", 0, 128), reg("KB", 0, 128))
         for c in range(3):
-            act(reg("DK", 128 * c, 128 * c + 128), reg("KEY", 0, 128), AF.Identity, bias=reg("TB", c, c + 1))
-        if t == 0:
-            quant("Qa", 0, 256, "at")
+            o = reg("DK", 128 * c, 128 * c + 128)
+            if c == 2:
+                ts(o, reg("KEY", 0, 128), reg("TB", c, c + 1), OP.add)
+            else:
+                act(o, reg("KEY", 0, 128), AF.Identity, bias=reg("TB", c, c + 1))
         for c in range(3):
             for k in range(2):
-                o, i = reg("R0", 3 * k + c, 3 * k + c + 1), reg("DK", 128 * c + 64 * k, 128 * c + 64 * k + 64)
-                op("V", lambda: V.tensor_reduce(ap(o), ap(i), AxisListType.X, OP.min, apply_absolute_value=True), [i], [o])
+                least(reg("R0", 3 * k + c, 3 * k + c + 1), reg("DK", 128 * c + 64 * k, 128 * c + 64 * k + 64))
+        for d in range(2):
+            tt(reg("R1", 0, 6, 64 * d, 64 * d + 64), reg("R0", 0, 6, 64 * d, 64 * d + 64), reg("R0", 0, 6, 64 - 64 * d, 128 - 64 * d), OP.min)
         for d in range(4):
             s = d ^ 1
-            tt(reg("R1", 0, 6, 32 * d, 32 * d + 32), reg("R0", 0, 6, 32 * d, 32 * d + 32), reg("R0", 0, 6, 32 * s, 32 * s + 32), OP.min)
-        for d in range(2):
-            tt(reg("Ri", 0, 6, 64 * d, 64 * d + 64), reg("R1", 0, 6, 64 * d, 64 * d + 64), reg("R1", 0, 6, 64 - 64 * d, 128 - 64 * d), OP.min)
+            tt(reg("Ri", 0, 6, 32 * d, 32 * d + 32), reg("R1", 0, 6, 32 * d, 32 * d + 32), reg("R1", 0, 6, 32 * s, 32 * s + 32), OP.min)
         ts(reg("Di", 0, 3), reg("Ri", 0, 3), 511, OP.bitwise_and)
         ts(reg("Di", 3, 6), reg("Ri", 0, 3), 9, OP.logical_shift_right)
         ts(reg("Di", 6, 9), reg("Ri", 3, 6), 1023, OP.bitwise_and)
-        copy(reg(PO, 0, 9), reg("Di", 0, 9))
-        J, w0 = reg(Ju, 0, 3), OWN[t]
-        pick(PK, 144, "W", wend, reg(PO, 0, 9))
+        copy(PO, reg("Di", 0, 9))
+        pick(PK, 0, 144, "W", wend, PO)
         ts(reg("Ji", 0, 3), reg("Ri", 3, 6), 10, OP.logical_shift_right)
         copy(J, reg("Ji", 0, 3))
         if t < 2:
             ts(reg(SL, 0, 3), reg("Ji", 0, 3), float(256 * rank), OP.add)
-            send("r_s%d" % t, lambda c: (T[SL][:, 0:3], T[SR][:, 3 * slot(c):3 * slot(c) + 3]), [reg(SL, 0, 3)])
-            arrive("r_s%d" % t, incoming, reg(SR, 0, 9))
+            i = send("r_s%d" % t, lambda c, SL=SL, SR=SR: (T[SL][:, 0:3], T[SR][:, 3 * slot(c):3 * slot(c) + 3]), [reg(SL, 0, 3)])
+            arrive("r_s%d" % t, incoming, i, reg(SR, 0, 9))
+        scatter(Mo, J, reg("ID", w0, w0 + K))
         if t == 0:
+            quant("Qa", 0, 256, "at")
             quant("Qa", 256, 512, "at", 1024)
-        scatter(reg("M", 256 * rank, 256 * rank + 256), J, reg("ID", w0, w0 + K))
         for b in range(4):
             mm(b, "Qa", 128 * b, PK, 0, 144)
+        for b in range(4):
+            s0, s1, s2, s3 = [reg("SU", 192 * k + K * b, 192 * k + K * b + K) for k in range(4)]
+            copy(s0, ps(b, 0, K), "S")
+            tt(s1, ps(b, K, 2 * K), s0, OP.add)
+            tt(s2, ps(b, 2 * K, 3 * K), s1, OP.add)
+            act(s3, s2, AF.Copy, scale=13421773.0 * 2.0 ** -28)
+            boost["b"] = 0.2 * (3 - b)
+            tt_by(reg("H", b, 4 * K, st=4), reg("bbT", 256 * b, 256 * b + 256), J, s3, OP.add)
+            boost["b"] = 0.0
         if t == 0:
             mm(7, "UV2", 0, "W", FAR, 3 * LC)
-        for b in range(4):
-            copy(reg("S0", K * b, K * b + K), ps(b, 0, K), "S")
-        for b in range(4):
-            gather(reg("BS", b, 4 * K, st=4), reg("bbT", 256 * b, 256 * b + 256), J, "S")
-        if t == 2:
-            gather(reg("FD", 0, 512), reg("M", 256 * rank, 256 * rank + 256), reg("DL", 0, 32), "S")
-        else:
-            gather(reg("PC", 0, 192), reg("M", 0, 1024), reg("nbo", 0, 12), "S")
-            gather(reg("PD", 0, 256), reg("PC", 0, 192), reg("KDL", 0, 16), "S")
-        if t == 0:
             copy(reg("E1", 0, 256), ps(5, 0, 256), "S")
             copy(reg("E1", FAR, FAR + 3 * LC), ps(7, 0, 3 * LC), "S")
-        for w in range(5):
-            for b, i in ((w, 0), (w - 1, 1)):
-                if 0 <= b < 4:
-                    tt(reg("S2", b, 4 * K, st=4) if i else reg("S1", K * b, K * b + K), ps(b, K * i + K, K * i + 2 * K), reg("S1" if i else "S0", K * b, K * b + K), OP.add)
-        ts(reg("S3", 0, 4 * K), reg("S2", 0, 4 * K), 13421773.0 * 2.0 ** -28, OP.mult)
-        tt(reg("H", 0, 4 * K), reg("S3", 0, 4 * K), reg("BS", 0, 4 * K), OP.add)
         quant("W", w0, w0 + 128, "H")
-        nf = reg("nf%d" % t, 0, 3)
         if t < 2:
-            ship("r_n%d" % t, "W", lambda c: w0, K, lambda c: ARR[t] + K * slot(c), w0, w0 + K)
-            arrive("r_n%d" % t, 2 * incoming, *both("W", ARR[t], ARR[t] + 3 * K))
+            i = ship("r_n%d" % t, "W", lambda c, w0=w0: w0, K, lambda c, t=t: ARR[t] + K * slot(c), w0, w0 + K)
+            arrive("r_n%d" % t, 2 * incoming, i, *both("W", ARR[t], ARR[t] + 3 * K))
             mm(7, "UV2", 0, "W", w0, 128)
             copy(reg("E1", w0, w0 + 128), ps(7, 0, 128), "S")
-            turn(reg("PT", 0, 256), reg("PD", 0, 256))
-            copy(reg("EO", 0, 8), reg("PT", 0, 256, st=32))
-            copy(nf, reg("Ji", 0, 3))
-            scatter(reg("M", 0, 1024), reg(SR, 0, 9), reg("ID", ARR[t], ARR[t] + 3 * K))
-            gather(reg("PC2", 0, 192), reg("M", 0, 1024), reg("nbo", 0, 12), "S")
-            gather(reg("PD", 256, 384), reg("PC2", 0, 192), reg("KDL", 16, 24), "S")
-            gather(reg("EG", 0, 128), reg("E1", 0, FAR), reg("EO", 0, 8))
-            tt(z[0], EG[0], EG[1], OP.add)
-            payload01("PC")
+            for h in range(2):
+                o = 128 * h
+                gather(reg("PD", o, o + 128), Mo, reg("nbD", 8 * h, 8 * h + 8), "S")
+                turn(reg("PT", o, o + 128), reg("PD", o, o + 128))
+                copy(reg("EO", 4 * h, 4 * h + 4), reg("PT", o, o + 128, st=32))
+            payload01()
+            scatter(M, reg(SR, 0, 9), reg("ID", ARR[t], ARR[t] + 3 * K))
+            gather(reg("PD", 256, 384), M, reg("nbD", 16, 24), "S")
             turn(reg("PT", 256, 384), reg("PD", 256, 384))
-            copy(reg("EO", 8, 12), reg("PT", 256, 384, st=32))
-            payload2("PC2")
+            ts(reg("EO", 8, 12), reg("PT", 256, 384, st=32), float(-FAR), OP.add)
+            payload2()
+            gather(EG, reg("E1", 0, FAR), reg("EO", 0, 4))
+            tt_by(z0, reg("E1", 0, FAR), reg("EO", 4, 8), EG, OP.add)
         else:
-            turn(reg("FT", 0, 512), reg("FD", 0, 512))
-            copy(reg("FO", 0, 16), reg("FT", 0, 512, st=32))
-            pick("FIN", 256, "W", WC, reg("FO", 0, 16))
-            copy(nf, reg("Ji", 0, 3))
+            for h in range(4):
+                o = 128 * h
+                gather(reg("FD", o, o + 128), Mo, reg("DL", 8 * h, 8 * h + 8), "S")
+                turn(reg("FT", o, o + 128), reg("FD", o, o + 128))
+                copy(reg("FO", 4 * h, 4 * h + 4), reg("FT", o, o + 128, st=32))
+            for h in range(2):
+                pick("FIN", 128 * h, 128 * h + 128, "W", WC, reg("FO", 8 * h, 8 * h + 8))
+        copy(nf, reg("Ji", 0, 3))
         for c in range(3):
-            dma("Y", "d_nd", T.nd[t:t + 1, 16 * c:16 * c + 16], T[nf[0]][0:16, c:c + 1], [nf], [])
+            dma("Y", "d_nd", T.nd[t:t + 1, 16 * c:16 * c + 16], T.nf[0:16, 3 * t + c:3 * t + c + 1], [nf], [])
         if t == 0:
             quant("Qw", 0, 128, "wt")
             for h in range(2):
                 copy(reg("DL", h, 32, st=2), reg("IC", 0, 16))
 
-    dma("Y", "d_out", T.oc[:, 0:1024], cb("FIN", 0, 256), [reg("FIN", 0, 256)], [])
-    for k in range(4):
-        dma("Y", "d_out", T.osc[4 * k:4 * k + 4, 0:256], T.FINs[32 * k:32 * k + 4, 0:256], [reg("FINs", 0, 256)], [])
     for h in range(2):
         mm(4 + h, "Qw", 0, "FIN", 128 * h, 128)
-    for h in range(2):
         copy(reg("ys", 128 * h, 128 * h + 128), ps(4 + h, 0, 128), "VS"[h])
+    dma("Y", "d_out", T.oc[:, 0:1024], cb("FIN", 0, 256), [reg("FIN", 0, 256)], [])
+    for k in range(4):
+        dma("YYSS"[k], "d_out", T.osc[4 * k:4 * k + 4, 0:256], T.FINs[32 * k:32 * k + 4, 0:256], [reg("FINs", 0, 256)], [])
+    for h in range(2):
         dma("YS"[h], "d_out", T.y[:, 128 * h:128 * h + 128], T.ys[:, 128 * h:128 * h + 128], [reg("ys", 128 * h, 128 * h + 128)], [])
+    plan()
     for s in ("v", "s", "p", "gq", "d_q", "d_nd", "d_out", "loc"):
         if know["G"].get(s, 0) < count[s]:
             g.wait_ge(T.sem[s], count[s])

@@ -8,20 +8,22 @@ ARR = [FAR + 3 * LC, FAR + 3 * LC + 3 * K]
 OWN.append(ARR[1] + 3 * K)
 WEND = [ARR[0], ARR[1], OWN[2]]
 WC = OWN[2] + 128
+PW = 2 * K + 128
 TINY = 2.0 ** -122
 PRED = 1.0 - 2.0 ** -24
 STEP, MID = 2.0 ** 19, 2.0 ** 24
-SCN_S = 3
-LEN_S = 2
-CY, LAT, LOAD, HOP = 1.05e-3, 0.15, 2.0, 2.5
+SCN_S = 2
+LEN_S = 3
+INP = 2
+CY, LAT, LOAD, HOP, BYTE = 1.3e-3, 0.16, 1.4, 2.0, 2.0e-6
 
 BUF = {
-    "float32": "ID:%d C12:12 tf:8 GCOL:8 JB:64 IC:16 ICS:8 TB:4 Fm:128 Ft:128 CK:32 C1:32 PADD:1 FRA:192 FRB:192 FR:192 SLf:256 LJ:768 LS:6 SS:8 SJ:256 Mo:256 M:1024 ec:2 EM:1024 E1:%d fb:64 PC:192 PAB:128 PAYT:128 PDn:384 PTn:384 PD:384 PT:384 EG:192 z0:64 z1:64 z2:64 zr:64 ZT:64 zB:64 zK:64 zr0:64 Zc:320 RS:256 KB:128 KEY:128 DK:384 R0:6 R1:6 nf:9 SU:768 FD:512 FT:512 ys:256" % (WC, OWN[2]),
+    "float32": "ID:%d C12:12 tf:8 GCOL:8 JB:64 IC:16 ICS:8 TB:4 Fm:128 Ft:128 CK:32 C1:32 PADD:1 FRA:192 FRB:192 FR:192 SLf:256 LJ:768 LS:6 SS:8 SJ:256 Mo:256 M:1024 ec:2 EM:768 E1:%d fb:64 PC:192 PAB:128 PAYT:128 PDn:384 PTn:384 PD:384 PT:384 EG:64 zK:64 z0:64 z1:64 z2:64 zr:64 ZT:64 zB:64 zr0:64 Zc:320 RS:128 KB:128 KEY:128 DK:384 R0:6 R1:6 nf:9 SU:768 FD:512 FT:512 ys:256 yn:144" % (WC, OWN[2]),
     "bfloat16": "ZB:256 xt:1024 bt:1024 at:2048 wt:512 uvs:32 uvt:1024 bbT:1024 EQ:2048 SC:1024 PB:256 PR:256 SCN:256 LE:1536 LC2:768 MK:512 H:512",
-    "int32": "pI:8 ti:24 nbI:12 nbP:24 Ne:60 Ri:6 Di:9 Ji:3",
-    "uint16": "UL:8 DL:32 KDL:24 nbp:24 nbo:12 nbe:12 nbD:24 nbK:12 FA:256 LST:6 LA:18 LO:18 EO:12 PO:30 J:12 SL0:4 SL1:4 SR0:9 SR1:9 FO:16",
+    "int32": "pI:8 ti:24 nbI:12 nbP:24 Ne:28 Ri:6 Di:9 Ji:3",
+    "uint16": "UL:8 DL:32 KDL:24 nbp:24 nbo:12 nbe:4 nbD:24 nbK:12 FA:256 LST:6 LA:18 LO:18 EO:12 PO:30 J:12 SL0:4 SL1:4 SR0:9 SR1:9 FO:16",
 }
-QBUF = "Q0:256 Qb:256 Qa:512 Qw:128 UV2:256 SND:288 W:%d PK0:144 PK1:144 PK2:144 FIN:256" % WC
+QBUF = "Q0:256 Qb:256 Qa:512 Qw:128 UV2:256 SND:288 W:%d PK0:%d PK1:%d PK2:%d FIN:256" % (WC, PW, PW, PW)
 SCRATCH = {"eld": ("dram", [3, 128, 2], "float32"), "ps": ("psum", [128, 4096], "float32")}
 for _d, _s in BUF.items():
     for _b in _s.split():
@@ -29,7 +31,7 @@ for _d, _s in BUF.items():
 for _b in QBUF.split():
     SCRATCH[_b.split(":")[0]] = ("sbuf", [128, int(_b.split(":")[1])], "float8_e4m3fn_x4")
     SCRATCH[_b.split(":")[0] + "s"] = ("sbuf", [128, int(_b.split(":")[1])], "uint8")
-SEMAPHORES = "v s p gq d_nb d_nc d_x d_uv d_bb d_a d_w d_q d_m d_e d_nd d_out r_e r_l r_c r_s0 r_s1 r_n0 r_n1 loc".split()
+SEMAPHORES = "v s p gq d_nb d_nc d_x d_y d_p d_uv d_bb d_a d_w d_q d_m d_e d_nd d_out r_e r_l r_c r_s0 r_s1 r_n0 r_n1 loc".split()
 
 
 def rank_program(g, core, T, topo):
@@ -106,7 +108,7 @@ def rank_program(g, core, T, topo):
             count[sem] += 16
             queue[q].dma_start(out, in_).then_inc(T.sem[sem], 16)
             note(reads, writes, "dma", sem, total[sem])
-        node(q, reads, writes, emit, 0.07, LOAD, sem)
+        node(q, reads, writes, emit, 0.07, LOAD + BYTE * sum(width(r) * (r[2] - r[1]) for r in writes), sem)
 
     def arrive(sem, n, after, *writes):
         node("far", [], list(writes), lambda: note([], writes, "far", sem, n), 0.0, LAT, None, after)
@@ -202,7 +204,7 @@ def rank_program(g, core, T, topo):
         op("V", lambda: V.transpose(ap(out), ap(in_)), [in_], [out], width(out) * CY)
 
     def fill(out, x):
-        op("V", lambda: V.memset(ap(out), x), [], [out], width(out) * CY)
+        op("V", lambda: V.memset(ap(out), x), [], [out], width(out) * CY * (0.5 if short(out) else 1.0))
 
     def least(o, i):
         op("V", lambda: V.tensor_reduce(ap(o), ap(i), AxisListType.X, OP.min, apply_absolute_value=True), [i], [o], width(i) * CY)
@@ -237,9 +239,9 @@ def rank_program(g, core, T, topo):
         e1 = e0 + 4 * (c1 - c0)
         op("V", lambda: V.quantize_mx(T[q][:, c0:c1], T[q + "s"][:, c0:c1], T[t][:, e0:e1]), [reg(t, e0, e1)], both(q, c0, c1), 0.012 + 1.06 * (c1 - c0) * CY)
 
-    def mm(bank, a, a0, b, b0, n):
+    def mm(bank, a, a0, b, b0, n, start=True, stop=True):
         o = reg("ps", 512 * bank, 512 * bank + n)
-        op("P", lambda: PE.matmul_mx(ap(o), T[a][:, a0:a0 + 128], T[a + "s"][:, a0:a0 + 128], T[b][:, b0:b0 + n], T[b + "s"][:, b0:b0 + n], True, True), both(a, a0, a0 + 128) + both(b, b0, b0 + n), [o], (n + 16) * CY)
+        op("P", lambda: PE.matmul_mx(ap(o), T[a][:, a0:a0 + 128], T[a + "s"][:, a0:a0 + 128], T[b][:, b0:b0 + n], T[b + "s"][:, b0:b0 + n], start, stop), both(a, a0, a0 + 128) + both(b, b0, b0 + n), [o], (n + 16) * CY)
 
     def ps(bank, c0, c1, p0=0, p1=128):
         return reg("ps", 512 * bank + c0, 512 * bank + c1, p0, p1)
@@ -292,7 +294,10 @@ def rank_program(g, core, T, topo):
         for a in range(4):
             p0, b0 = 32 * a + 16 * h, 24 * (a // 2)
             dma("YS"[h], "d_nb", T.nbP[p0:p0 + 16, :], T.nb[:, b0:b0 + 24], [], [reg("nbP", 0, 24, p0, p0 + 16)])
-    dma("Y", "d_x", T.xt[:], T.x[:], [], [reg("xt", 0, 1024)])
+    boost["b"] = 1.0
+    for h in range(2):
+        dma("Y", ("d_x", "d_y")[h], T.xt[:, 512 * h:512 * h + 512], T.x[:, 512 * h:512 * h + 512], [], [reg("xt", 512 * h, 512 * h + 512)])
+    boost["b"] = 0.0
     dma("S", "d_uv", T.uvs[:, 0:4], T.u[:, 0:4], [], [reg("uvs", 0, 4)])
     dma("S", "d_uv", T.uvs[:, 16:20], T.v[:, 0:4], [], [reg("uvs", 16, 20)])
     for h in range(2):
@@ -306,10 +311,9 @@ def rank_program(g, core, T, topo):
     iota(reg("pI", 0, 8), [[0, 8]], 0, 1)
     iota(reg("ID", 0, 256), [[1, 256]], 0)
     iota(reg("C12", 0, 12), [[1, 3], [48, 4]], 0)
-    for q in range(4):
-        if q != rank:
-            iota(reg("EM", 256 * q, 256 * q + 256), [[0, 256]], 0)
-    iota(reg("M", 256 * rank, 256 * rank + 256), [[0, 256]], 0)
+    for q in range(3):
+        iota(reg("EM", 256 * q, 256 * q + 256), [[0, 256]], 0)
+    act(reg("M", 256 * rank, 256 * rank + 256), reg("ID", 0, 256), AF.Copy)
     for k, q in ((1, "V"), (2, "S"), (3, "V"), (4, "S")):
         n = min(256, WC - 256 * k)
         if q == "V":
@@ -331,7 +335,7 @@ def rank_program(g, core, T, topo):
     fill(reg("ZB", 0, 256), 0.0)
     fill(reg("CK", 0, 32), STEP)
     fill(reg("C1", 0, 32), 1.0)
-    fill(reg("H", 0, 512), 0.0)
+    fill(reg("H", 4 * K, 512), 0.0)
     fill(reg("E1", OWN[0] + 128, FAR), 0.0)
     for a in range(4):
         fill(reg("PADD", 0, 1, 32 * a, 32 * a + 32), float(FAR + LC * ((a - rank - 1) % 4 % 3) - 1))
@@ -350,7 +354,8 @@ def rank_program(g, core, T, topo):
         gather(reg("uvt", o, o + 128), reg("uvs", 16 * k, 16 * k + 4), reg("UL", 0, 8), "S")
         copy(reg("uvt", o + 128, o + 256), reg("uvt", o, o + 128), "S")
         copy(reg("uvt", o + 256, o + 512), reg("uvt", o, o + 256), "S")
-    quant("Q0", 0, 256, "xt")
+    for h in range(2):
+        quant("Q0", 128 * h, 128 * h + 128, "xt", 512 * h)
     quant("UV2", 0, 128, "uvt")
     quant("UV2", 128, 256, "uvt", 512)
     for c in range(2):
@@ -361,6 +366,9 @@ def rank_program(g, core, T, topo):
     arrive("r_e", incoming, i, reg("eld", 0, 3))
     dma("Y", "d_q", cb("W", 0, 256), cb("Q0", 0, 256), [reg("Q0", 0, 256)], [reg("W", 0, 256)])
     dma("Y", "d_q", T.Ws[:, 0:256], T.Q0s[:, 0:256], [reg("Q0s", 0, 256)], [reg("Ws", 0, 256)])
+    for t in range(R):
+        dma("Y", "d_p", cb("PK%d" % t, 3 * K, PW), cb("Q0", 0, PW - 3 * K), [reg("Q0", 0, PW - 3 * K)], [reg("PK%d" % t, 3 * K, PW)])
+        dma("Y", "d_p", T["PK%ds" % t][:, 3 * K:PW], T.Q0s[:, 0:PW - 3 * K], [reg("Q0s", 0, PW - 3 * K)], [reg("PK%ds" % t, 3 * K, PW)])
     for c in range(8):
         eq = reg("EQ", 256 * c, 256 * c + 256)
         ts(eq, reg("FA", 0, 256), reg("GCOL", c, c + 1), OP.is_equal)
@@ -384,42 +392,39 @@ def rank_program(g, core, T, topo):
     i = send("r_l", lambda c: (T.LST[:, 0:6], T.LA[:, 6 * slot(c):6 * slot(c) + 6]), [reg("LST", 0, 6)])
     arrive("r_l", incoming, i, reg("LA", 0, 18))
     for d in range(4):
-        i = 0
-        while i < 3:
-            q = (rank + 1 + i) % 4
-            n = min(3 - i, 4 - q)
-            dma("Y", "d_e", T.EM[32 * d:32 * d + 1, 256 * q:256 * (q + n)], T.eld[i:i + n], [reg("eld", i, i + n)], [reg("EM", 256 * q, 256 * (q + n), 32 * d, 32 * d + 1)])
-            i += n
+        dma("Y", "d_e", T.EM[32 * d:32 * d + 1, 0:768], T.eld[0:3], [reg("eld", 0, 3)], [reg("EM", 0, 768, 32 * d, 32 * d + 1)])
     act(reg("SLf", 0, 256), reg("SCN", 0, 256), AF.Identity, bias=reg("PADD", 0, 1))
     for q in range(4):
         if q != rank:
             for d in range(4):
                 dma("Y", "d_m", T.M[32 * d:32 * d + 32, 256 * q:256 * q + 256], T.SLf[32 * q:32 * q + 32, :], [reg("SLf", 0, 256, 32 * q, 32 * q + 32)], [reg("M", 256 * q, 256 * q + 256, 32 * d, 32 * d + 32)])
-    n0, n1, n2, n3, n4 = [reg("Ne", 12 * i, 12 * i + 12) for i in range(5)]
-    nbI = reg("nbI", 0, 12)
-    ts(n0, nbI, 127, OP.bitwise_and)
-    ts(n1, nbI, 7, OP.logical_shift_right, 1, OP.bitwise_and)
-    tt(n2, n0, nbI, OP.add)
-    ts(n3, n1, -127.0, OP.mult)
-    tt(n4, n2, n3, OP.add)
-    copy(reg("nbe", 0, 12), n4)
-    copy(reg("nbo", 0, 12), nbI)
+    copy(reg("nbo", 0, 12), reg("nbI", 0, 12))
     for h in range(2):
         ts(reg("KDL", h, 24, st=2), reg("C12", 0, 12), tf(7), OP.add)
     gather(reg("FR", 0, 192), reg("ID", 0, 1024), reg("nbo", 0, 12), "S")
-    gather(reg("PDn", 0, 384), reg("FR", 0, 192), reg("KDL", 0, 24), "S")
-    turn(reg("PTn", 0, 384), reg("PDn", 0, 384))
+    gather(reg("PDn", 0, 256), reg("FR", 0, 192), reg("KDL", 0, 16), "S")
+    gather(reg("PDn", 256, 384), reg("FR", 0, 192), reg("KDL", 16, 24), "S")
+    turn(reg("PTn", 0, 256), reg("PDn", 0, 256))
+    turn(reg("PTn", 256, 384), reg("PDn", 256, 384))
     ts(reg("nbD", 0, 16), reg("PTn", 0, 256, st=16), float(-256 * rank), OP.add)
     ts(reg("nbK", 0, 8), reg("PTn", 0, 256, st=32), float(-256 * rank), OP.add)
     copy(reg("nbD", 16, 24), reg("PTn", 256, 384, st=16))
     copy(reg("nbK", 8, 12), reg("PTn", 256, 384, st=32))
+    m0, m1, n0, n1, n2, n3, n4 = [reg("Ne", 4 * i, 4 * i + 4) for i in range(7)]
+    ts(m0, reg("PTn", 256, 384, st=32), float(1024 - 256 * (rank + 1)), OP.add)
+    ts(m1, m0, 1023, OP.bitwise_and)
+    ts(n0, m0, 127, OP.bitwise_and)
+    ts(n1, m0, 7, OP.logical_shift_right, 1, OP.bitwise_and)
+    tt(n2, n0, m1, OP.add)
+    ts(n3, n1, -127.0, OP.mult)
+    tt(n4, n2, n3, OP.add)
+    copy(reg("nbe", 0, 4), n4)
     quant("Qb", 0, 256, "bt")
     mm(5, "UV2", 0, "Q0", 0, 256)
     mm(4, "UV2", 128, "Qb", 0, 256)
     for b in range(2):
         ts(reg("Ft", 64 * b, 64 * b + 64), reg("ID", 0, 64), tf(5 + b), OP.is_lt, 2.0 ** -24, OP.mult)
-    for c in range(2):
-        copy(reg("EM", 256 * rank + c, 256 * rank + 256, st=2), ps(5, 128 * c, 128 * c + 128), "S")
+    copy(reg("E1", 0, 256), ps(5, 0, 256), "S")
     for a in range(4):
         copy(reg("fb", 0, 64, 32 * a, 32 * a + 32), ps(4, 64 * a, 64 * a + 64, 32 * a, 32 * a + 32), "S")
     act(reg("Fm", 0, 128), reg("Ft", 0, 128), AF.Identity, bias=PRED)
@@ -449,14 +454,17 @@ def rank_program(g, core, T, topo):
         tt(reg("PAB", 64, 128), reg("PC", 128, 192), reg("JB", 0, 64), OP.add)
         turn(reg("PAYT", 64, 128), reg("PAB", 64, 128))
 
+    quant("Qw", 0, 128, "wt")
+    mm(5, "Qw", 0, "Q0", 0, 256)
+    copy(reg("ys", 0, 256), ps(5, 0, 256), "S")
     for t in range(R):
         PK, SL, SR = "PK%d" % t, "SL%d" % t, "SR%d" % t
         PO, J, nf = reg("PO", 10 * t, 10 * t + 9), reg("J", 4 * t, 4 * t + 3), reg("nf", 3 * t, 3 * t + 3)
         wend, w0 = WEND[t], OWN[t]
         if t == 0:
-            gather(reg("EG", 0, 192), reg("EM", 0, 1024), reg("nbe", 0, 12))
-            tt(z0, reg("EG", 0, 192, st=3), reg("EG", 1, 192, st=3), OP.add)
-            tt(z1, z0, reg("EG", 2, 192, st=3), OP.add)
+            gather(EG, reg("E1", 0, 256), reg("nbK", 0, 4))
+            tt_by(z0, reg("E1", 0, 256), reg("nbK", 4, 8), EG, OP.add)
+            tt_by(z1, reg("EM", 0, 768), reg("nbe", 0, 4), z0, OP.add)
             payload01()
             payload2()
         else:
@@ -488,15 +496,16 @@ def rank_program(g, core, T, topo):
                 ts(o, i, f, OP.mult)
             else:
                 copy(o, i)
-        for b in range(2):
-            for h in range(2):
+        for h in range(2):
+            for b in (1, 0):
                 o = 256 * b + 128 * h
                 ts(reg("MK", o, o + 128), reg("Zc", 64 * b + 128 * h, 64 * b + 128 * h + 128), reg("ZT", 32 * b, 32 * b + 1), OP.is_ge)
-            scan(reg("RS", 128 * b, 128 * b + 128), reg("MK", 256 * b, 256 * b + 128), reg("MK", 256 * b + 128, 256 * b + 256))
+        act(reg("SJ", 0, 256), reg("MK", 256, 512), AF.Copy, accum=reg("SS", 0, 1))
+        scan(reg("RS", 0, 128), reg("MK", 0, 128), reg("MK", 128, 256))
         for k in range(2):
-            for b in range(2):
-                o = 64 * k + 32 * b
-                ts(reg("KB", o, o + 32), reg("CK", 0, 32), reg("RS", 128 * b + 127, 128 * b + 128), OP.mult, reg("PAYT", o, o + 1), OP.add)
+            o = 64 * k
+            ts(reg("KB", o, o + 32), reg("CK", 0, 32), reg("RS", 127, 128), OP.mult, reg("PAYT", o, o + 1), OP.add)
+            act(reg("KB", o + 32, o + 64), reg("CK", 0, 32), AF.Identity, scale=reg("SS", 0, 1), bias=reg("PAYT", o + 32, o + 33))
         turn(reg("KEY", 0, 128), reg("KB", 0, 128))
         for c in range(3):
             o = reg("DK", 128 * c, 128 * c + 128)
@@ -527,20 +536,25 @@ def rank_program(g, core, T, topo):
         if t == 0:
             quant("Qa", 0, 256, "at")
             quant("Qa", 256, 512, "at", 1024)
-        for b in range(4):
-            mm(b, "Qa", 128 * b, PK, 0, 144)
+        for b in range(4 - INP):
+            mm(b, "Qa", 128 * b, PK, 0, 3 * K)
+        for b in range(4 - INP, 4):
+            for k in range(3):
+                mm(b, "Qa", 128 * b, PK, K * k, 128, k == 0, k == 2)
         for b in range(4):
             s0, s1, s2, s3 = [reg("SU", 192 * k + K * b, 192 * k + K * b + K) for k in range(4)]
-            copy(s0, ps(b, 0, K), "S")
-            tt(s1, ps(b, K, 2 * K), s0, OP.add)
-            tt(s2, ps(b, 2 * K, 3 * K), s1, OP.add)
+            if b < 4 - INP:
+                copy(s0, ps(b, 0, K), "S")
+                tt(s1, ps(b, K, 2 * K), s0, OP.add)
+                tt(s2, ps(b, 2 * K, 3 * K), s1, OP.add)
+            else:
+                s2 = ps(b, 0, K)
             act(s3, s2, AF.Copy, scale=13421773.0 * 2.0 ** -28)
             boost["b"] = 0.2 * (3 - b)
             tt_by(reg("H", b, 4 * K, st=4), reg("bbT", 256 * b, 256 * b + 256), J, s3, OP.add)
             boost["b"] = 0.0
         if t == 0:
             mm(7, "UV2", 0, "W", FAR, 3 * LC)
-            copy(reg("E1", 0, 256), ps(5, 0, 256), "S")
             copy(reg("E1", FAR, FAR + 3 * LC), ps(7, 0, 3 * LC), "S")
         quant("W", w0, w0 + 128, "H")
         if t < 2:
@@ -572,14 +586,13 @@ def rank_program(g, core, T, topo):
         copy(nf, reg("Ji", 0, 3))
         for c in range(3):
             dma("Y", "d_nd", T.nd[t:t + 1, 16 * c:16 * c + 16], T.nf[0:16, 3 * t + c:3 * t + c + 1], [nf], [])
+        mm(4, "Qw", 0, "W", w0, 128)
+        copy(reg("yn", K * t, K * t + K), ps(4, 0, K), "S")
+        scatter(reg("ys", 0, 256), J, reg("yn", K * t, K * t + K))
         if t == 0:
-            quant("Qw", 0, 128, "wt")
             for h in range(2):
                 copy(reg("DL", h, 32, st=2), reg("IC", 0, 16))
 
-    for h in range(2):
-        mm(4 + h, "Qw", 0, "FIN", 128 * h, 128)
-        copy(reg("ys", 128 * h, 128 * h + 128), ps(4 + h, 0, 128), "VS"[h])
     dma("Y", "d_out", T.oc[:, 0:1024], cb("FIN", 0, 256), [reg("FIN", 0, 256)], [])
     for k in range(4):
         dma("YYSS"[k], "d_out", T.osc[4 * k:4 * k + 4, 0:256], T.FINs[32 * k:32 * k + 4, 0:256], [reg("FINs", 0, 256)], [])

@@ -12,26 +12,38 @@ PW = 2 * K + 128
 TINY = 2.0 ** -122
 PRED = 1.0 - 2.0 ** -24
 STEP, MID = 2.0 ** 19, 2.0 ** 24
+STEP1 = 512.0
+UP = 2.0 ** 23
+VPART = 128
+NP = 2
+INP = 2
 SCN_S = 2
 LEN_S = 3
-INP = 2
-CY, LAT, LOAD, HOP, BYTE = 1.3e-3, 0.16, 1.4, 2.0, 2.0e-6
+ORDER = [int(_i) for _i in """
+53 10 8 23 48 11 9 0 6 4 24 1 5 2 37 3 7 34 12 13 47 14 15 38 16 36 17 18 41 39 19 25 189 46 20 21 30 31 26 22 32 67 57 60 27 74 61 62 73 68 188 33 85 69 63 86 64 58 143 83 84 146 65 66 182 75 77 28 78 185 144 59 105 163 195 108 70 87 106 79 90 93 80 81 88 96 91 109 99 102 107 94 89 97 92 100 110 95 103 98 145 101 54 104 55 56 35 111 148 150 112 82 42 129 126 127 113 128 147 115 119 117 114 116 120 154 118 149 121 122 71 123 72 124 157 155 167 162 156 76 151 130 159 158 164 212 173 160 131 132 133 213 134 135 161 136 168 137 45 169 138 170 139 214 171 140 141 29 50 222 165 166 125 223 153 215 216 200 224 201 172 203 202 225 226 142 240 40 227 205 207 204 238 229 230 231 206 232 234 233 235 236 217 228 237 239 241 194 219 242 218 243 198 220 244 221 49 246 174 247 245 248 250 196 249 175 251 177 252 254 208 253 178 303 255 197 256 259 257 258 260 152 261 199 262 263 264 266 304 265 43 267 268 269 176 270 279 272 271 281 179 273 282 280 289 283 284 285 286 180 275 274 183 294 181 52 184 290 44 295 291 276 296 292 278 297 287 51 293 288 298 299 301 300 302 314 355 191 305 306 309 307 209 359 277 336 187 315 210 356 357 358 325 326 310 311 192 337 186 190 312 340 338 316 339 317 341 308 318 319 320 327 193 360 313 362 329 330 331 322 363 328 321 211 323 364 324 342 344 365 343 366 370 333 371 367 372 332 377 373 374 375 334 378 376 369 380 379 368 381 382 383 385 384 345 346 386 388 387 390 389 347 392 391 393 395 397 394 348 396 351 398 349 399 400 352 401 403 404 402 353 405 406 411 412 407 410 335 350 408 469 361 470 471 415 413 414 472 354 416 417 428 418 419 439 429 420 423 477 421 473 440 409 424 450 478 474 430 451 425 431 433 432 434 426 441 422 452 454 480 427 435 443 475 453 481 442 482 479 483 455 444 437 436 445 476 438 484 488 489 446 485 490 496 495 487 491 448 447 493 494 492 498 497 486 500 499 456 501 503 502 457 458 460 504 506 459 508 505 461 510 507 509 511 513 515 462 512 514 465 516 463 449 517 518 466 519 520 464 521 522 524 523 467 525 549 526 550 551 537 536 552 541 527 528 539 538 468 540 529 542 543 530 531 544 553 533 532 534 546 554 535 545 547 548 555 556 559 557 560 558 561 562
+""".split()]
 
 BUF = {
-    "float32": "ID:%d C12:12 tf:8 GCOL:8 JB:64 IC:16 ICS:8 TB:4 Fm:128 Ft:128 CK:32 C1:32 PADD:1 FRA:192 FRB:192 FR:192 SLf:256 LJ:768 LS:6 SS:8 SJ:256 Mo:256 M:1024 ec:2 EM:768 E1:%d fb:64 PC:192 PAB:128 PAYT:128 PDn:384 PTn:384 PD:384 PT:384 EG:64 zK:64 z0:64 z1:64 z2:64 zr:64 ZT:64 zB:64 zr0:64 Zc:320 RS:128 KB:128 KEY:128 DK:384 R0:6 R1:6 nf:9 SU:768 FD:512 FT:512 ys:256 yn:144" % (WC, OWN[2]),
+    "float32": "ID:%d JB:64 Fm:128 Ft:128 FRA:192 FRB:192 FR:192 SLf:256 LJ:768 SJ:256 Mo:256 MoD:512 LRo:512 LRf:256 LIo:64 LIf:32 en:96 G4:192 ST:1024 M:1024 ec:2 EM:768 E1:%d fb:64 PC:192 PAB:128 PAYT:128 PDn:384 PTn:384 PD:384 PT:384 EG:64 zK:64 z0:64 z1:64 z2:64 zr:64 ZT:64 zB:64 zr0:64 Zc:320 KB:192 KEY:192 DK:384 RS:128 nf:9 SU:768 FT:512 ys:256 yn:144" % (WC, OWN[2]),
     "bfloat16": "ZB:256 xt:1024 bt:1024 at:2048 wt:512 uvs:32 uvt:1024 bbT:1024 EQ:2048 SC:1024 PB:256 PR:256 SCN:256 LE:1536 LC2:768 MK:512 H:512",
-    "int32": "pI:8 ti:24 nbI:12 nbP:24 Ne:28 Ri:6 Di:9 Ji:3",
-    "uint16": "UL:8 DL:32 KDL:24 nbp:24 nbo:12 nbe:4 nbD:24 nbK:12 FA:256 LST:6 LA:18 LO:18 EO:12 PO:30 J:12 SL0:4 SL1:4 SR0:9 SR1:9 FO:16",
+    "int32": "pI:8 ti:24 nbI:12 nbP:24 Ne:28 Ri:6 Di:9 Ji:3 Dj:12",
+    "uint16": "UL:8 DL:32 FN:512 nbG:48 Lu:96 JD:8 KDL:24 nbp:24 nbo:12 nbe:4 nbD:24 nbK:12 FA:256 LST:6 LA:18 LO:18 EO:12 PO:30 J:12 SL0:4 SL1:4 SR0:9 SR1:9 FO:16",
 }
-QBUF = "Q0:256 Qb:256 Qa:512 Qw:128 UV2:256 SND:288 W:%d PK0:%d PK1:%d PK2:%d FIN:256" % (WC, PW, PW, PW)
-SCRATCH = {"eld": ("dram", [3, 128, 2], "float32"), "ps": ("psum", [128, 4096], "float32")}
+SMALL = "C12:12 tf:12 GCOL:8 IC:16 ICS:8 TB:4 CK:32 C1:32 PADD:4 LS:8 SS:8 VP:96 PAYJ:4 OFF:192 ZN:4 Rf:4 R0:8 R1:8"
+PART = {}
+_n = 0
+for _b in SMALL.split():
+    PART[_b.split(":")[0]] = _n
+    _n += int(_b.split(":")[1])
+QBUF = "Q0:256 Qb:256 Qa:512 Qw:128 UV2:256 SND:288 W:%d PK0:%d PA1:768 PA2:768 FIN:256" % (WC, PW)
+SCRATCH = {"eld": ("dram", [3, 128, 2], "float32"), "ps": ("psum", [128, 4096], "float32"), "KC": ("sbuf", [128, _n], "float32")}
 for _d, _s in BUF.items():
     for _b in _s.split():
         SCRATCH[_b.split(":")[0]] = ("sbuf", [128, int(_b.split(":")[1])], _d)
 for _b in QBUF.split():
     SCRATCH[_b.split(":")[0]] = ("sbuf", [128, int(_b.split(":")[1])], "float8_e4m3fn_x4")
     SCRATCH[_b.split(":")[0] + "s"] = ("sbuf", [128, int(_b.split(":")[1])], "uint8")
-SEMAPHORES = "v s p gq d_nb d_nc d_x d_y d_p d_uv d_bb d_a d_w d_q d_m d_e d_nd d_out r_e r_l r_c r_s0 r_s1 r_n0 r_n1 loc".split()
+SEMAPHORES = "v s p gq d_nb d_nc d_x d_y d_p d_uv d_bb d_a d_w d_q d_m d_e d_nd d_out d_g d_l0 d_l1 d_l2 d_l3 d_l4 d_l5 r_e r_l r_c r_s0 r_s1 r_n0 r_n1 loc".split()
 
 
 def rank_program(g, core, T, topo):
@@ -44,9 +56,11 @@ def rank_program(g, core, T, topo):
     count = {s: 0 for s in SEMAPHORES}
     total = {s: 0 for s in SEMAPHORES}
     know = {q: {} for q in queue}
-    snaps, touched, nodes, boost = {}, {}, [], {"b": 0.0}
+    snaps, touched, calls = {}, {}, []
 
     def reg(name, c0, c1, p0=0, p1=128, st=1):
+        if name in PART:
+            return ("KC", p0, p1, c0 + PART[name], c1 + PART[name], st)
         return (name, p0, p1, c0, c1, st)
 
     def ap(r):
@@ -60,18 +74,11 @@ def rank_program(g, core, T, topo):
             return False
         return not (a[5] == b[5] > 1 and a[3] % a[5] != b[3] % b[5])
 
-    def width(r):
-        return -(-(r[4] - r[3]) // r[5])
-
-    def node(q, reads, writes, emit, dur, lat, sem=None, after=()):
-        nodes.append({"q": q, "r": reads, "w": writes, "emit": emit, "dur": dur, "lat": lat, "sem": sem, "after": list(after), "bonus": boost["b"]})
-        return len(nodes) - 1
-
-    def order(q, reads, writes):
+    def order(q, reads, writes, acc=False):
         want = {}
         for r, w in [(r, False) for r in reads] + [(r, True) for r in writes]:
             for (o, ow, oq, sem, val) in touched.get(r[0], []):
-                if meet(r, o) and (ow or ((w or r[0] == "ps") and oq != q)):
+                if meet(r, o) and not (acc and oq == q and r[0] == "ps") and (ow or ((w or r[0] == "ps") and oq != q)):
                     if know[q].get(sem, 0) < val:
                         want[sem] = max(want.get(sem, 0), val)
         for s in sorted(want):
@@ -89,16 +96,16 @@ def rank_program(g, core, T, topo):
         for r in writes:
             touched.setdefault(r[0], []).append((r, True, q, sem, val))
 
-    def op(q, fn, reads, writes, dur):
+    def op(q, fn, reads, writes, acc=False):
         s = sem_of[q]
 
         def emit():
-            order(q, reads, writes)
+            order(q, reads, writes, acc)
             count[s] += 1
             fn().then_inc(T.sem[s], 1)
             snaps[(s, count[s])] = dict(know[q])
             note(reads, writes, q, s, count[s])
-        node(q, reads, writes, emit, max(dur, 64 * CY), LAT)
+        calls.append(emit)
 
     def dma(q, sem, out, in_, reads, writes):
         total[sem] += 16
@@ -108,128 +115,70 @@ def rank_program(g, core, T, topo):
             count[sem] += 16
             queue[q].dma_start(out, in_).then_inc(T.sem[sem], 16)
             note(reads, writes, "dma", sem, total[sem])
-        node(q, reads, writes, emit, 0.07, LOAD + BYTE * sum(width(r) * (r[2] - r[1]) for r in writes), sem)
+        calls.append(emit)
 
-    def arrive(sem, n, after, *writes):
-        node("far", [], list(writes), lambda: note([], writes, "far", sem, n), 0.0, LAT, None, after)
-
-    def plan():
-        n = len(nodes)
-        hist, deps, group = {}, [], {}
-        for i, x in enumerate(nodes):
-            if x["sem"] is not None:
-                group.setdefault(x["sem"], []).append(i)
-        for i, x in enumerate(nodes):
-            d = set(x["after"])
-            for r, w in [(r, False) for r in x["r"]] + [(r, True) for r in x["w"]]:
-                for (o, ow, j) in hist.get(r[0], []):
-                    if j != i and meet(r, o) and (ow or w or (r[0] == "ps" and nodes[j]["q"] != x["q"])):
-                        d.add(j)
-            for j in list(d):
-                if nodes[j]["sem"] is not None and nodes[j]["sem"] != x["sem"]:
-                    d.update(group[nodes[j]["sem"]])
-            d.discard(i)
-            deps.append(d)
-            for r in x["r"]:
-                hist.setdefault(r[0], []).append((r, False, i))
-            for r in x["w"]:
-                hist.setdefault(r[0], []).append((r, True, i))
-        succ = [[] for _ in range(n)]
-        for i in range(n):
-            for j in deps[i]:
-                succ[j].append(i)
-        prio, left = [0.0] * n, [len(s) for s in succ]
-        stack = [i for i in range(n) if not left[i]]
-        while stack:
-            i = stack.pop()
-            x = nodes[i]
-            prio[i] = x["dur"] + x["bonus"] + max([x["lat"] + prio[k] for k in succ[i]] + [0.0])
-            for j in deps[i]:
-                left[j] -= 1
-                if not left[j]:
-                    stack.append(j)
-        busy = {q: [] for q in queue}
-        start, over = [0.0] * n, [0.0] * n
-        for i in sorted(range(n), key=lambda i: (-prio[i], i)):
-            x = nodes[i]
-            t = max([over[j] for j in deps[i]] + [0.0])
-            if x["q"] in busy:
-                b, at = busy[x["q"]], 0
-                for at in range(len(b) + 1):
-                    if at == len(b) or t + x["dur"] <= b[at][0] + 1e-9:
-                        break
-                    t = max(t, b[at][1])
-                b.insert(at, (t, t + x["dur"]))
-            start[i], over[i] = t, t + x["dur"] + x["lat"]
-        for i in sorted(range(n), key=lambda i: (start[i], -prio[i], i)):
-            nodes[i]["emit"]()
+    def arrive(sem, n, *writes):
+        calls.append(lambda: note([], writes, "far", sem, n))
 
     def sc(x):
         return ap(x) if isinstance(x, tuple) else x
-
-    def short(r):
-        return SCRATCH[r[0]][2] in ("bfloat16", "uint16")
 
     def act(out, in_, f, bias=None, scale=None, accum=None):
         kw = {}
         if bias is not None: kw["bias"] = sc(bias)
         if scale is not None: kw["scale"] = sc(scale)
         if accum is not None: kw["accum_out"] = ap(accum)
-        op("S", lambda: S.activation(ap(out), ap(in_), f, **kw), [in_] + [x for x in (bias, scale) if isinstance(x, tuple)], [out] + ([accum] if accum else []), width(in_) * CY)
+        op("S", lambda: S.activation(ap(out), ap(in_), f, **kw), [in_] + [x for x in (bias, scale) if isinstance(x, tuple)], [out] + ([accum] if accum else []))
 
     def copy(out, in_, q="V"):
         if q == "V":
-            op("V", lambda: V.tensor_copy(ap(out), ap(in_)), [in_], [out], width(in_) * CY)
+            op("V", lambda: V.tensor_copy(ap(out), ap(in_)), [in_], [out])
         else:
             act(out, in_, AF.Copy)
 
     def ts(out, in_, s1, op0, s2=None, op1=None):
         rd = [in_] + [x for x in (s1, s2) if isinstance(x, tuple)]
-        d = width(in_) * CY * (0.5 if short(out) and short(in_) else 1.0)
         if op1 is None:
-            op("V", lambda: V.tensor_scalar(ap(out), ap(in_), sc(s1), None, op0), rd, [out], d)
+            op("V", lambda: V.tensor_scalar(ap(out), ap(in_), sc(s1), None, op0), rd, [out])
         else:
-            op("V", lambda: V.tensor_scalar(ap(out), ap(in_), sc(s1), sc(s2), op0, op1), rd, [out], d)
+            op("V", lambda: V.tensor_scalar(ap(out), ap(in_), sc(s1), sc(s2), op0, op1), rd, [out])
 
     def tt(out, a, b, o):
-        op("V", lambda: V.tensor_tensor(ap(out), ap(a), ap(b), o), [a, b], [out], width(out) * CY * 2)
+        op("V", lambda: V.tensor_tensor(ap(out), ap(a), ap(b), o), [a, b], [out])
 
     def tt_by(out, win, off, b, o):
-        op("V", lambda: V.tensor_tensor(ap(out), ap(win).indirect(ap(off)), ap(b), o), [win, off, b], [out], 0.05 + width(out) * CY * 1.6)
+        op("V", lambda: V.tensor_tensor(ap(out), ap(win).indirect(ap(off)), ap(b), o), [win, off, b], [out])
 
     def scan(out, a, b):
-        op("V", lambda: V.tensor_tensor_scan(ap(out), ap(a), ap(b), 0.0, OP.add, OP.add), [a, b], [out], width(out) * CY * (0.5 if short(out) else 1.0))
+        op("V", lambda: V.tensor_tensor_scan(ap(out), ap(a), ap(b), 0.0, OP.add, OP.add), [a, b], [out])
 
     def turn(out, in_):
-        op("V", lambda: V.transpose(ap(out), ap(in_)), [in_], [out], width(out) * CY)
+        op("V", lambda: V.transpose(ap(out), ap(in_)), [in_], [out])
 
     def fill(out, x):
-        op("V", lambda: V.memset(ap(out), x), [], [out], width(out) * CY * (0.5 if short(out) else 1.0))
+        op("V", lambda: V.memset(ap(out), x), [], [out])
 
     def least(o, i):
-        op("V", lambda: V.tensor_reduce(ap(o), ap(i), AxisListType.X, OP.min, apply_absolute_value=True), [i], [o], width(i) * CY)
+        op("V", lambda: V.tensor_reduce(ap(o), ap(i), AxisListType.X, OP.min, apply_absolute_value=True), [i], [o])
 
     def iota(out, pattern, base, mult=0):
-        n = 1
-        for s, c in pattern:
-            n *= c
         if SCRATCH[out[0]][2] == "int32":
-            op("G", lambda: g.iota(ap(out), pattern, base, mult), [], [out], 0.13 + 2 * n * CY)
+            op("G", lambda: g.iota(ap(out), pattern, base, mult), [], [out])
         else:
-            op("G", lambda: g.iota(ap(out), pattern, base, mult, allow_small_or_imprecise_dtypes=True), [], [out], 0.13 + 2 * n * CY)
+            op("G", lambda: g.iota(ap(out), pattern, base, mult, allow_small_or_imprecise_dtypes=True), [], [out])
 
     def gather(out, win, off, q="V"):
         if q == "V":
-            op("V", lambda: V.tensor_copy(ap(out), ap(win).indirect(ap(off))), [win, off], [out], 0.05 + 1.6 * width(out) * CY)
+            op("V", lambda: V.tensor_copy(ap(out), ap(win).indirect(ap(off))), [win, off], [out])
         else:
-            op("S", lambda: S.activation(ap(out), ap(win).indirect(ap(off)), AF.Copy), [win, off], [out], 0.065 + 1.6 * width(out) * CY)
+            op("S", lambda: S.activation(ap(out), ap(win).indirect(ap(off)), AF.Copy), [win, off], [out])
 
     def scatter(win, off, in_):
-        op("V", lambda: V.tensor_copy(ap(win).indirect(ap(off)), ap(in_)), [in_, off], [win], 0.05 + 3 * width(in_) * CY)
+        op("V", lambda: V.tensor_copy(ap(win).indirect(ap(off)), ap(in_)), [in_, off], [win])
 
     def pick(dst, c0, c1, src, w1, off):
         a, b = reg(dst, c0, c1), reg(src, 0, w1)
-        op("V", lambda: V.tensor_copy(ap(a).bitcast(dt.uint32), ap(b).bitcast(dt.uint32).indirect(ap(off))), [b, off], [a], 0.05 + 1.6 * (c1 - c0) * CY)
+        op("V", lambda: V.tensor_copy(ap(a).bitcast(dt.uint32), ap(b).bitcast(dt.uint32).indirect(ap(off))), [b, off], [a])
         gather(reg(dst + "s", c0, c1), reg(src + "s", 0, w1), off, "S")
 
     def both(q, c0, c1):
@@ -237,11 +186,11 @@ def rank_program(g, core, T, topo):
 
     def quant(q, c0, c1, t, e0=0):
         e1 = e0 + 4 * (c1 - c0)
-        op("V", lambda: V.quantize_mx(T[q][:, c0:c1], T[q + "s"][:, c0:c1], T[t][:, e0:e1]), [reg(t, e0, e1)], both(q, c0, c1), 0.012 + 1.06 * (c1 - c0) * CY)
+        op("V", lambda: V.quantize_mx(T[q][:, c0:c1], T[q + "s"][:, c0:c1], T[t][:, e0:e1]), [reg(t, e0, e1)], both(q, c0, c1))
 
     def mm(bank, a, a0, b, b0, n, start=True, stop=True):
         o = reg("ps", 512 * bank, 512 * bank + n)
-        op("P", lambda: PE.matmul_mx(ap(o), T[a][:, a0:a0 + 128], T[a + "s"][:, a0:a0 + 128], T[b][:, b0:b0 + n], T[b + "s"][:, b0:b0 + n], start, stop), both(a, a0, a0 + 128) + both(b, b0, b0 + n), [o], (n + 16) * CY)
+        op("P", lambda: PE.matmul_mx(ap(o), T[a][:, a0:a0 + 128], T[a + "s"][:, a0:a0 + 128], T[b][:, b0:b0 + n], T[b + "s"][:, b0:b0 + n], start, stop), both(a, a0, a0 + 128) + both(b, b0, b0 + n), [o], not start)
 
     def ps(bank, c0, c1, p0=0, p1=128):
         return reg("ps", 512 * bank + c0, 512 * bank + c1, p0, p1)
@@ -273,7 +222,7 @@ def rank_program(g, core, T, topo):
                 tr.append(RemoteDMATransfer(dst_ids=[DstId(rid=rid, pnc=pid)], dma_engine_mask=sum(1 << e for e in mine[c]), remote_sem=T.sem[sem], src=s, dst=d))
                 count["loc"] += len(mine[c])
             g.remote_dma_fused(tr, local_sem=T.sem.loc)
-        return [node("G", reads, [], emit, 0.3, HOP)]
+        calls.append(emit)
 
     incoming = sum(len(lanes(c)[core]) for c in sources)
 
@@ -281,8 +230,11 @@ def rank_program(g, core, T, topo):
         return T[name][:, c0:c1].bitcast(dt.uint8)
 
     def ship(sem, q, s0, n, dst, c0, c1):
-        a = send(sem, lambda c: (cb(q, s0(c), s0(c) + n), cb("W", dst(c), dst(c) + n)), [reg(q, c0, c1)])
-        return a + send(sem, lambda c: (T[q + "s"][:, s0(c):s0(c) + n], T.Ws[:, dst(c):dst(c) + n]), [reg(q + "s", c0, c1)])
+        send(sem, lambda c: (cb(q, s0(c), s0(c) + n), cb("W", dst(c), dst(c) + n)), [reg(q, c0, c1)])
+        send(sem, lambda c: (T[q + "s"][:, s0(c):s0(c) + n], T.Ws[:, dst(c):dst(c) + n]), [reg(q + "s", c0, c1)])
+
+    def as_list(sem, l, c, row, r0):
+        dma("Y", sem, T[l][:, c:c + 16], T[row][0:128:16, r0:r0 + 256], [reg(row, r0, r0 + 256)], [reg(l, c, c + 16)])
 
     def ti(i):
         return reg("ti", i, i + 1)
@@ -294,10 +246,8 @@ def rank_program(g, core, T, topo):
         for a in range(4):
             p0, b0 = 32 * a + 16 * h, 24 * (a // 2)
             dma("YS"[h], "d_nb", T.nbP[p0:p0 + 16, :], T.nb[:, b0:b0 + 24], [], [reg("nbP", 0, 24, p0, p0 + 16)])
-    boost["b"] = 1.0
     for h in range(2):
         dma("Y", ("d_x", "d_y")[h], T.xt[:, 512 * h:512 * h + 512], T.x[:, 512 * h:512 * h + 512], [], [reg("xt", 512 * h, 512 * h + 512)])
-    boost["b"] = 0.0
     dma("S", "d_uv", T.uvs[:, 0:4], T.u[:, 0:4], [], [reg("uvs", 0, 4)])
     dma("S", "d_uv", T.uvs[:, 16:20], T.v[:, 0:4], [], [reg("uvs", 16, 20)])
     for h in range(2):
@@ -329,6 +279,8 @@ def rank_program(g, core, T, topo):
     ts(tf(2), ti(0), 2048.0, OP.mult, -MID, OP.add)
     tt(tf(0), tf(4), pI, OP.add)
     copy(tf(5), ti(1))
+    ts(tf(8), ti(0), 2.0, OP.mult)
+    tt(tf(9), tf(8), ti(1), OP.add)
     ts(tf(6), ti(1), 32.0, OP.add)
     ts(tf(7), ti(2), 3.0, OP.mult)
     copy(reg("UL", 0, 8), reg("ti", 8, 16))
@@ -362,13 +314,12 @@ def rank_program(g, core, T, topo):
         mm(c, "Q0", 128 * c, "UV2", 0, 128)
     for c in range(2):
         copy(reg("ec", c, c + 1), ps(c, 0, 1), "S")
-    i = send("r_e", lambda c: (T.ec[:, 0:2], T.eld[slot(c)]), [reg("ec", 0, 2)])
-    arrive("r_e", incoming, i, reg("eld", 0, 3))
+    send("r_e", lambda c: (T.ec[:, 0:2], T.eld[slot(c)]), [reg("ec", 0, 2)])
+    arrive("r_e", incoming, reg("eld", 0, 3))
     dma("Y", "d_q", cb("W", 0, 256), cb("Q0", 0, 256), [reg("Q0", 0, 256)], [reg("W", 0, 256)])
     dma("Y", "d_q", T.Ws[:, 0:256], T.Q0s[:, 0:256], [reg("Q0s", 0, 256)], [reg("Ws", 0, 256)])
-    for t in range(R):
-        dma("Y", "d_p", cb("PK%d" % t, 3 * K, PW), cb("Q0", 0, PW - 3 * K), [reg("Q0", 0, PW - 3 * K)], [reg("PK%d" % t, 3 * K, PW)])
-        dma("Y", "d_p", T["PK%ds" % t][:, 3 * K:PW], T.Q0s[:, 0:PW - 3 * K], [reg("Q0s", 0, PW - 3 * K)], [reg("PK%ds" % t, 3 * K, PW)])
+    dma("Y", "d_p", cb("PK0", 3 * K, PW), cb("Q0", 0, PW - 3 * K), [reg("Q0", 0, PW - 3 * K)], [reg("PK0", 3 * K, PW)])
+    dma("Y", "d_p", T["PK0s"][:, 3 * K:PW], T.Q0s[:, 0:PW - 3 * K], [reg("Q0s", 0, PW - 3 * K)], [reg("PK0s", 3 * K, PW)])
     for c in range(8):
         eq = reg("EQ", 256 * c, 256 * c + 256)
         ts(eq, reg("FA", 0, 256), reg("GCOL", c, c + 1), OP.is_equal)
@@ -389,8 +340,8 @@ def rank_program(g, core, T, topo):
         act(reg("LJ", 256 * (c % 3), 256 * (c % 3) + 255), reg("SCN", 0, 255), AF.Sign, bias=reg("ICS", c, c + 1), accum=reg("LS", c, c + 1))
     ts(reg("LST", 0, nv), reg("LC2", 127, 128 * nv, st=128), 255.0, OP.min)
     ts(reg("LST", nv, 6), reg("LS", nv, 6), -0.5, OP.mult, 127.5, OP.add)
-    i = send("r_l", lambda c: (T.LST[:, 0:6], T.LA[:, 6 * slot(c):6 * slot(c) + 6]), [reg("LST", 0, 6)])
-    arrive("r_l", incoming, i, reg("LA", 0, 18))
+    send("r_l", lambda c: (T.LST[:, 0:6], T.LA[:, 6 * slot(c):6 * slot(c) + 6]), [reg("LST", 0, 6)])
+    arrive("r_l", incoming, reg("LA", 0, 18))
     for d in range(4):
         dma("Y", "d_e", T.EM[32 * d:32 * d + 1, 0:768], T.eld[0:3], [reg("eld", 0, 3)], [reg("EM", 0, 768, 32 * d, 32 * d + 1)])
     act(reg("SLf", 0, 256), reg("SCN", 0, 256), AF.Identity, bias=reg("PADD", 0, 1))
@@ -406,7 +357,6 @@ def rank_program(g, core, T, topo):
     gather(reg("PDn", 256, 384), reg("FR", 0, 192), reg("KDL", 16, 24), "S")
     turn(reg("PTn", 0, 256), reg("PDn", 0, 256))
     turn(reg("PTn", 256, 384), reg("PDn", 256, 384))
-    ts(reg("nbD", 0, 16), reg("PTn", 0, 256, st=16), float(-256 * rank), OP.add)
     ts(reg("nbK", 0, 8), reg("PTn", 0, 256, st=32), float(-256 * rank), OP.add)
     copy(reg("nbD", 16, 24), reg("PTn", 256, 384, st=16))
     copy(reg("nbK", 8, 12), reg("PTn", 256, 384, st=32))
@@ -429,6 +379,22 @@ def rank_program(g, core, T, topo):
         copy(reg("fb", 0, 64, 32 * a, 32 * a + 32), ps(4, 64 * a, 64 * a + 64, 32 * a, 32 * a + 32), "S")
     act(reg("Fm", 0, 128), reg("Ft", 0, 128), AF.Identity, bias=PRED)
     copy(reg("Mo", 0, 256), reg("ID", 0, 256), "S")
+    for k in range(2):
+        for i in range(2):
+            ts(reg("FN", 256 * k + 64 * i, 256 * k + 64 * i + 64), reg(("FRA", "FRB")[i], k, 192, st=3), float(-256 * rank), OP.add)
+        copy(reg("FN", 256 * k + 128, 256 * k + 256, 0, 64), reg("FN", 256 * k, 256 * k + 128, 64, 128))
+    for h in range(2):
+        for k in range(3):
+            f, o = ("FN", 256 * k) if k < 2 else ("FA", 0)
+            dma("Y", "d_g", T.nbG[64 * h:64 * h + 64, 16 * k:16 * k + 16], T[f][0:64:16, o:o + 256], [reg(f, o, o + 256, 0, 64)], [reg("nbG", 16 * k, 16 * k + 16, 64 * h, 64 * h + 64)])
+    for h in range(2):
+        copy(reg("DL", h, 32, st=2), reg("IC", 0, 16))
+    iota(reg("VP", 0, 96), [[0, 2], [1, 48]], OWN[2])
+    iota(reg("OFF", 0, 96), [[-16, 3], [0, 2], [-1, 16]], 0)
+    for k in range(2):
+        ts(reg("PAYJ", k, k + 1), tf(9), 1.0 / STEP1, OP.mult, k * 32.0 / STEP1, OP.add)
+    act(reg("OFF", 96, 192), reg("OFF", 0, 96), AF.Identity, bias=reg("PAYJ", 1, 2))
+    act(reg("OFF", 0, 96), reg("OFF", 0, 96), AF.Identity, bias=reg("PAYJ", 0, 1))
     act(reg("JB", 0, 64), reg("ID", 0, 64), AF.Identity, scale=1024.0, bias=tf(2))
     act(reg("TB", 0, 4), reg("IC", 0, 4), AF.Identity, scale=-STEP, bias=MID)
     for t in range(4):
@@ -436,12 +402,13 @@ def rank_program(g, core, T, topo):
     for d in range(4):
         copy(reg("LO", 0, 18, 32 * d, 32 * d + 32), reg("LA", 0, 18, 32 * rank, 32 * rank + 32))
     pick("SND", 0, 288, "Q0", 256, reg("LO", 0, 18))
-    i = ship("r_c", "SND", lambda c: LC * sources.index(c), LC, lambda c: FAR + LC * slot(c), 0, 3 * LC)
-    arrive("r_c", 2 * incoming, i, *both("W", FAR, FAR + 3 * LC))
+    ship("r_c", "SND", lambda c: LC * sources.index(c), LC, lambda c: FAR + LC * slot(c), 0, 3 * LC)
+    arrive("r_c", 2 * incoming, *both("W", FAR, FAR + 3 * LC))
 
     z0, z1, z2, EG = reg("z0", 0, 64), reg("z1", 0, 64), reg("z2", 0, 64), reg("EG", 0, 64)
     M = reg("M", 0, 1024)
     Mo = reg("Mo", 0, 256)
+    C005 = 13421773.0 * 2.0 ** -28
 
     def payload01():
         gather(reg("PC", 0, 128), Mo, reg("nbK", 0, 8), "S")
@@ -458,8 +425,9 @@ def rank_program(g, core, T, topo):
     mm(5, "Qw", 0, "Q0", 0, 256)
     copy(reg("ys", 0, 256), ps(5, 0, 256), "S")
     for t in range(R):
-        PK, SL, SR = "PK%d" % t, "SL%d" % t, "SR%d" % t
+        SL, SR = "SL%d" % t, "SR%d" % t
         PO, J, nf = reg("PO", 10 * t, 10 * t + 9), reg("J", 4 * t, 4 * t + 3), reg("nf", 3 * t, 3 * t + 3)
+        nk, Jn = (2, reg("Ji", 0, 3)) if t == 0 else (1, reg("Dj", 0, 3))
         wend, w0 = WEND[t], OWN[t]
         if t == 0:
             gather(EG, reg("E1", 0, 256), reg("nbK", 0, 4))
@@ -496,109 +464,152 @@ def rank_program(g, core, T, topo):
                 ts(o, i, f, OP.mult)
             else:
                 copy(o, i)
+        ts(reg("ZN", 0, 1), reg("ZT", 32, 33), -UP, OP.mult)
+        ts(reg("MK", 256, 256 + VPART), reg("Zc", 64, 64 + VPART), reg("ZT", 32, 33), OP.is_ge, 1.0, OP.subtract)
+        act(reg("MK", 256 + VPART, 512), reg("Zc", 64 + VPART, 320), AF.Sign, scale=UP, bias=reg("ZN", 0, 1))
         for h in range(2):
-            for b in (1, 0):
-                o = 256 * b + 128 * h
-                ts(reg("MK", o, o + 128), reg("Zc", 64 * b + 128 * h, 64 * b + 128 * h + 128), reg("ZT", 32 * b, 32 * b + 1), OP.is_ge)
-        act(reg("SJ", 0, 256), reg("MK", 256, 512), AF.Copy, accum=reg("SS", 0, 1))
+            ts(reg("MK", 128 * h, 128 * h + 128), reg("Zc", 128 * h, 128 * h + 128), reg("ZT", 0, 1), OP.is_ge)
+        act(reg("SJ", 0, 256), reg("MK", 256, 512), AF.Sign, bias=1.0, accum=reg("SS", 0, 1))
         scan(reg("RS", 0, 128), reg("MK", 0, 128), reg("MK", 128, 256))
-        for k in range(2):
-            o = 64 * k
-            ts(reg("KB", o, o + 32), reg("CK", 0, 32), reg("RS", 127, 128), OP.mult, reg("PAYT", o, o + 1), OP.add)
-            act(reg("KB", o + 32, o + 64), reg("CK", 0, 32), AF.Identity, scale=reg("SS", 0, 1), bias=reg("PAYT", o + 32, o + 33))
-        turn(reg("KEY", 0, 128), reg("KB", 0, 128))
-        for c in range(3):
-            o = reg("DK", 128 * c, 128 * c + 128)
-            if c == 2:
-                ts(o, reg("KEY", 0, 128), reg("TB", c, c + 1), OP.add)
-            else:
-                act(o, reg("KEY", 0, 128), AF.Identity, bias=reg("TB", c, c + 1))
-        for c in range(3):
+        if t == 0:
             for k in range(2):
-                least(reg("R0", 3 * k + c, 3 * k + c + 1), reg("DK", 128 * c + 64 * k, 128 * c + 64 * k + 64))
+                o = 64 * k
+                ts(reg("KB", o, o + 32), reg("CK", 0, 32), reg("RS", 127, 128), OP.mult, reg("PAYT", o, o + 1), OP.add)
+                act(reg("KB", o + 32, o + 64), reg("CK", 0, 32), AF.Identity, scale=reg("SS", 0, 1), bias=reg("PAYT", o + 32, o + 33))
+            turn(reg("KEY", 0, 128), reg("KB", 0, 128))
+            for c in range(3):
+                o, tb = reg("DK", 128 * c, 128 * c + 128), reg("TB", c, c + 1)
+                if c == 2:
+                    ts(o, reg("KEY", 0, 128), tb, OP.add)
+                else:
+                    act(o, reg("KEY", 0, 128), AF.Identity, bias=tb)
+            for c in range(3):
+                for k in range(2):
+                    least(reg("R0", 3 * k + c, 3 * k + c + 1), reg("DK", 128 * c + 64 * k, 128 * c + 64 * k + 64))
+        else:
+            for c in range(3):
+                o = 64 * c
+                ts(reg("KB", o, o + 32), reg("OFF", 32 * c, 32 * c + 32), reg("RS", 127, 128), OP.add)
+                act(reg("KB", o + 32, o + 64), reg("OFF", 96 + 32 * c, 128 + 32 * c), AF.Identity, bias=reg("SS", 0, 1))
+            for c in range(3):
+                o = 64 * c
+                turn(reg("KEY", o, o + 64), reg("KB", o, o + 64))
+                least(reg("R0", c, c + 1), reg("KEY", o, o + 64))
+        n3 = 3 * nk
         for d in range(2):
-            tt(reg("R1", 0, 6, 64 * d, 64 * d + 64), reg("R0", 0, 6, 64 * d, 64 * d + 64), reg("R0", 0, 6, 64 - 64 * d, 128 - 64 * d), OP.min)
+            tt(reg("R1", 0, n3, 64 * d, 64 * d + 64), reg("R0", 0, n3, 64 * d, 64 * d + 64), reg("R0", 0, n3, 64 - 64 * d, 128 - 64 * d), OP.min)
+        Rd = "Ri" if t == 0 else "Rf"
         for d in range(4):
             s = d ^ 1
-            tt(reg("Ri", 0, 6, 32 * d, 32 * d + 32), reg("R1", 0, 6, 32 * d, 32 * d + 32), reg("R1", 0, 6, 32 * s, 32 * s + 32), OP.min)
-        ts(reg("Di", 0, 3), reg("Ri", 0, 3), 511, OP.bitwise_and)
-        ts(reg("Di", 3, 6), reg("Ri", 0, 3), 9, OP.logical_shift_right)
-        ts(reg("Di", 6, 9), reg("Ri", 3, 6), 1023, OP.bitwise_and)
-        copy(PO, reg("Di", 0, 9))
-        pick(PK, 0, 144, "W", wend, PO)
-        ts(reg("Ji", 0, 3), reg("Ri", 3, 6), 10, OP.logical_shift_right)
-        copy(J, reg("Ji", 0, 3))
+            tt(reg(Rd, 0, n3, 32 * d, 32 * d + 32), reg("R1", 0, n3, 32 * d, 32 * d + 32), reg("R1", 0, n3, 32 * s, 32 * s + 32), OP.min)
+        if t == 0:
+            ts(reg("Di", 0, 3), reg("Ri", 0, 3), 511, OP.bitwise_and)
+            ts(reg("Di", 3, 6), reg("Ri", 0, 3), 9, OP.logical_shift_right)
+            ts(reg("Di", 6, 9), reg("Ri", 3, 6), 1023, OP.bitwise_and)
+            copy(PO, reg("Di", 0, 9))
+            pick("PK0", 0, 144, "W", wend, PO)
+            ts(Jn, reg("Ri", 3, 6), 10, OP.logical_shift_right)
+            copy(J, Jn)
+        else:
+            ts(J, reg("Rf", 0, 3), STEP1, OP.mult)
+            ts(Jn, reg("Rf", 0, 3), STEP1, OP.mult)
         if t < 2:
-            ts(reg(SL, 0, 3), reg("Ji", 0, 3), float(256 * rank), OP.add)
-            i = send("r_s%d" % t, lambda c, SL=SL, SR=SR: (T[SL][:, 0:3], T[SR][:, 3 * slot(c):3 * slot(c) + 3]), [reg(SL, 0, 3)])
-            arrive("r_s%d" % t, incoming, i, reg(SR, 0, 9))
-        scatter(Mo, J, reg("ID", w0, w0 + K))
+            ts(reg(SL, 0, 3), Jn, float(256 * rank), OP.add)
+            send("r_s%d" % t, lambda c, SL=SL, SR=SR: (T[SL][:, 0:3], T[SR][:, 3 * slot(c):3 * slot(c) + 3]), [reg(SL, 0, 3)])
+            arrive("r_s%d" % t, incoming, reg(SR, 0, 9))
+        if t < 2:
+            scatter(Mo, J, reg("ID", w0, w0 + K))
+        else:
+            ts(reg("Dj", 8, 11), Jn, 240, OP.bitwise_and)
+            tt(reg("Dj", 4, 7), Jn, reg("Dj", 8, 11), OP.add)
+            copy(reg("JD", 0, 3), reg("Dj", 4, 7))
+            ts(reg("JD", 3, 6), reg("Dj", 4, 7), 16.0, OP.add)
+            scatter(reg("MoD", 0, 512), reg("JD", 0, 6), reg("VP", 0, 96))
+            for h in range(4):
+                turn(reg("FT", 128 * h, 128 * h + 128), reg("MoD", 128 * h, 128 * h + 128))
+            for h in range(2):
+                copy(reg("FO", 8 * h, 8 * h + 8), reg("FT", 256 * h, 256 * h + 256, st=32))
         if t == 0:
             quant("Qa", 0, 256, "at")
             quant("Qa", 256, 512, "at", 1024)
-        for b in range(4 - INP):
-            mm(b, "Qa", 128 * b, PK, 0, 3 * K)
-        for b in range(4 - INP, 4):
-            for k in range(3):
-                mm(b, "Qa", 128 * b, PK, K * k, 128, k == 0, k == 2)
-        for b in range(4):
-            s0, s1, s2, s3 = [reg("SU", 192 * k + K * b, 192 * k + K * b + K) for k in range(4)]
-            if b < 4 - INP:
-                copy(s0, ps(b, 0, K), "S")
-                tt(s1, ps(b, K, 2 * K), s0, OP.add)
-                tt(s2, ps(b, 2 * K, 3 * K), s1, OP.add)
-            else:
-                s2 = ps(b, 0, K)
-            act(s3, s2, AF.Copy, scale=13421773.0 * 2.0 ** -28)
-            boost["b"] = 0.2 * (3 - b)
-            tt_by(reg("H", b, 4 * K, st=4), reg("bbT", 256 * b, 256 * b + 256), J, s3, OP.add)
-            boost["b"] = 0.0
+            for b in range(4 - INP):
+                mm(b, "Qa", 128 * b, "PK0", 0, 3 * K)
+            for b in range(4 - INP, 4):
+                for k in range(3):
+                    mm(b, "Qa", 128 * b, "PK0", K * k, 128, k == 0, k == 2)
+            for b in range(4):
+                s0, s1, s2, s3 = [reg("SU", 192 * k + K * b, 192 * k + K * b + K) for k in range(4)]
+                if b < 4 - INP:
+                    copy(s0, ps(b, 0, K), "S")
+                    tt(s1, ps(b, K, 2 * K), s0, OP.add)
+                    tt(s2, ps(b, 2 * K, 3 * K), s1, OP.add)
+                else:
+                    s2 = ps(b, 0, K)
+                act(s3, s2, AF.Copy, scale=C005)
+                tt_by(reg("H", b, 4 * K, st=4), reg("bbT", 256 * b, 256 * b + 256), J, s3, OP.add)
+        else:
+            for b in range(4):
+                gather(reg("G4", K * b, K * b + K), reg("bbT", 256 * b, 256 * b + 256), J, "S")
+            for b in range(4):
+                tt_by(reg("H", b, 4 * K, st=4), reg("ST", 256 * b, 256 * b + 256), J, reg("G4", K * b, K * b + K), OP.add)
         if t == 0:
             mm(7, "UV2", 0, "W", FAR, 3 * LC)
             copy(reg("E1", FAR, FAR + 3 * LC), ps(7, 0, 3 * LC), "S")
         quant("W", w0, w0 + 128, "H")
         if t < 2:
-            i = ship("r_n%d" % t, "W", lambda c, w0=w0: w0, K, lambda c, t=t: ARR[t] + K * slot(c), w0, w0 + K)
-            arrive("r_n%d" % t, 2 * incoming, i, *both("W", ARR[t], ARR[t] + 3 * K))
+            ship("r_n%d" % t, "W", lambda c, w0=w0: w0, K, lambda c, t=t: ARR[t] + K * slot(c), w0, w0 + K)
+            arrive("r_n%d" % t, 2 * incoming, *both("W", ARR[t], ARR[t] + 3 * K))
+            u = t + 1
+            PA = "PA%d" % u
             mm(7, "UV2", 0, "W", w0, 128)
-            copy(reg("E1", w0, w0 + 128), ps(7, 0, 128), "S")
-            for h in range(2):
-                o = 128 * h
-                gather(reg("PD", o, o + 128), Mo, reg("nbD", 8 * h, 8 * h + 8), "S")
-                turn(reg("PT", o, o + 128), reg("PD", o, o + 128))
-                copy(reg("EO", 4 * h, 4 * h + 4), reg("PT", o, o + 128, st=32))
-            payload01()
+            copy(reg("en", K * t, K * t + K), ps(7, 0, K), "S")
+            scatter(reg("E1", 0, 256), J, reg("en", K * t, K * t + K))
+            gather(EG, reg("E1", 0, 256), reg("nbK", 0, 4))
+            tt_by(z0, reg("E1", 0, 256), reg("nbK", 4, 8), EG, OP.add)
+            w = 256 // NP
+            for k in range(2):
+                gather(reg("LRo", 256 * k, 256 * k + 256), Mo, reg("nbG", 16 * k, 16 * k + 16), "S")
+                as_list("d_l%d" % (3 * t + k), "LIo", 32 * t + 16 * k, "LRo", 256 * k)
+                o = 48 * t + 16 * k
+                copy(reg("Lu", o, o + 16), reg("LIo", 32 * t + 16 * k, 32 * t + 16 * k + 16))
+                for h in range(NP):
+                    pick(PA, 256 * k + w * h, 256 * k + w * h + w, "W", w0 + K, reg("Lu", o + w // 16 * h, o + w // 16 * (h + 1)))
+                for b in range(4):
+                    mm(b, "Qa", 128 * b, PA, 256 * k, 256, k == 0, False)
             scatter(M, reg(SR, 0, 9), reg("ID", ARR[t], ARR[t] + 3 * K))
             gather(reg("PD", 256, 384), M, reg("nbD", 16, 24), "S")
             turn(reg("PT", 256, 384), reg("PD", 256, 384))
             ts(reg("EO", 8, 12), reg("PT", 256, 384, st=32), float(-FAR), OP.add)
-            payload2()
-            gather(EG, reg("E1", 0, FAR), reg("EO", 0, 4))
-            tt_by(z0, reg("E1", 0, FAR), reg("EO", 4, 8), EG, OP.add)
+            gather(reg("LRf", 0, 256), M, reg("nbG", 32, 48), "S")
+            as_list("d_l%d" % (3 * t + 2), "LIf", 16 * t, "LRf", 0)
+            o = 48 * t + 32
+            copy(reg("Lu", o, o + 16), reg("LIf", 16 * t, 16 * t + 16))
+            for h in range(NP):
+                pick(PA, 512 + w * h, 512 + w * h + w, "W", WEND[u], reg("Lu", o + w // 16 * h, o + w // 16 * (h + 1)))
+            for b in range(4):
+                mm(b, "Qa", 128 * b, PA, 512, 256, False, True)
+            for b in range(4):
+                act(reg("ST", 256 * b, 256 * b + 256), ps(b, 0, 256), AF.Copy, scale=C005)
         else:
-            for h in range(4):
-                o = 128 * h
-                gather(reg("FD", o, o + 128), Mo, reg("DL", 8 * h, 8 * h + 8), "S")
-                turn(reg("FT", o, o + 128), reg("FD", o, o + 128))
-                copy(reg("FO", 4 * h, 4 * h + 4), reg("FT", o, o + 128, st=32))
             for h in range(2):
                 pick("FIN", 128 * h, 128 * h + 128, "W", WC, reg("FO", 8 * h, 8 * h + 8))
-        copy(nf, reg("Ji", 0, 3))
+        copy(nf, Jn)
         for c in range(3):
             dma("Y", "d_nd", T.nd[t:t + 1, 16 * c:16 * c + 16], T.nf[0:16, 3 * t + c:3 * t + c + 1], [nf], [])
+        if t == 1:
+            for h in range(4):
+                gather(reg("MoD", 128 * h, 128 * h + 128), Mo, reg("DL", 8 * h, 8 * h + 8), "S")
         mm(4, "Qw", 0, "W", w0, 128)
         copy(reg("yn", K * t, K * t + K), ps(4, 0, K), "S")
         scatter(reg("ys", 0, 256), J, reg("yn", K * t, K * t + K))
-        if t == 0:
-            for h in range(2):
-                copy(reg("DL", h, 32, st=2), reg("IC", 0, 16))
 
     dma("Y", "d_out", T.oc[:, 0:1024], cb("FIN", 0, 256), [reg("FIN", 0, 256)], [])
     for k in range(4):
         dma("YYSS"[k], "d_out", T.osc[4 * k:4 * k + 4, 0:256], T.FINs[32 * k:32 * k + 4, 0:256], [reg("FINs", 0, 256)], [])
     for h in range(2):
         dma("YS"[h], "d_out", T.y[:, 128 * h:128 * h + 128], T.ys[:, 128 * h:128 * h + 128], [reg("ys", 128 * h, 128 * h + 128)], [])
-    plan()
-    for s in ("v", "s", "p", "gq", "d_q", "d_nd", "d_out", "loc"):
+    for i in ORDER:
+        calls[i]()
+    for s in ("v", "s", "p", "gq", "d_q", "d_g", "d_nd", "d_out", "loc"):
         if know["G"].get(s, 0) < count[s]:
             g.wait_ge(T.sem[s], count[s])

from concourse.bass import DstId, RemoteDMATransfer
from concourse.mybir import AluOpType as OP, AxisListType, ActivationFunctionType as AF, dt

P, K, R, LC = 256, 48, 3, 96
OWN = [P, P + K]
FAR = P + K + 128
ARR = [FAR + 3 * LC, FAR + 3 * LC + 3 * K]
OWN.append(ARR[1] + 3 * K)
WEND = [ARR[0], ARR[1], OWN[2]]
WC = OWN[2] + 128
PW = 2 * K + 128
TINY = 2.0 ** -122
PRED = 1.0 - 2.0 ** -24
STEP, MID = 2.0 ** 19, 2.0 ** 24
STEP1 = 512.0
UP = 2.0 ** 23
VPART = 128
NP = 2
INP = 2
SCN_S = 2
LEN_S = 3
ORDER = [int(_i) for _i in """
53 10 8 23 48 11 9 0 6 4 24 1 5 2 37 3 7 34 12 13 47 14 15 38 16 36 17 18 41 39 19 25 189 46 20 21 30 31 26 22 32 67 57 60 27 74 61 62 73 68 188 33 85 69 63 86 64 58 143 83 84 146 65 66 182 75 77 28 78 185 144 59 105 163 195 108 70 87 106 79 90 93 80 81 88 96 91 109 99 102 107 94 89 97 92 100 110 95 103 98 145 101 54 104 55 56 35 111 148 150 112 82 42 129 126 127 113 128 147 115 119 117 114 116 120 154 118 149 121 122 71 123 72 124 157 155 167 162 156 76 151 130 159 158 164 212 173 160 131 132 133 213 134 135 161 136 168 137 45 169 138 170 139 214 171 140 141 29 50 222 165 166 125 223 153 215 216 200 224 201 172 203 202 225 226 142 240 40 227 205 207 204 238 229 230 231 206 232 234 233 235 236 217 228 237 239 241 194 219 242 218 243 198 220 244 221 49 246 174 247 245 248 250 196 249 175 251 177 252 254 208 253 178 303 255 197 256 259 257 258 260 152 261 199 262 263 264 266 304 265 43 267 268 269 176 270 279 272 271 281 179 273 282 280 289 283 284 285 286 180 275 274 183 294 181 52 184 290 44 295 291 276 296 292 278 297 287 51 293 288 298 299 301 300 302 314 355 191 305 306 309 307 209 359 277 336 187 315 210 356 357 358 325 326 310 311 192 337 186 190 312 340 338 316 339 317 341 308 318 319 320 327 193 360 313 362 329 330 331 322 363 328 321 211 323 364 324 342 344 365 343 366 370 333 371 367 372 332 377 373 374 375 334 378 376 369 380 379 368 381 382 383 385 384 345 346 386 388 387 390 389 347 392 391 393 395 397 394 348 396 351 398 349 399 400 352 401 403 404 402 353 405 406 411 412 407 410 335 350 408 469 361 470 471 415 413 414 472 354 416 417 428 418 419 439 429 420 423 477 421 473 440 409 424 450 478 474 430 451 425 431 433 432 434 426 441 422 452 454 480 427 435 443 475 453 481 442 482 479 483 455 444 437 436 445 476 438 484 488 489 446 485 490 496 495 487 491 448 447 493 494 492 498 497 486 500 499 456 501 503 502 457 458 460 504 506 459 508 505 461 510 507 509 511 513 515 462 512 514 465 516 463 449 517 518 466 519 520 464 521 522 524 523 467 525 549 526 550 551 537 536 552 541 527 528 539 538 468 540 529 542 543 530 531 544 553 533 532 534 546 554 535 545 547 548 555 556 559 557 560 558 561 562
""".split()]

BUF = {
    "float32": "ID:%d JB:64 Fm:128 Ft:128 FRA:192 FRB:192 FR:192 SLf:256 LJ:768 SJ:256 Mo:256 MoD:512 LRo:512 LRf:256 LIo:64 LIf:32 en:96 G4:192 ST:1024 M:1024 ec:2 EM:768 E1:%d fb:64 PC:192 PAB:128 PAYT:128 PDn:384 PTn:384 PD:384 PT:384 EG:64 zK:64 z0:64 z1:64 z2:64 zr:64 ZT:64 zB:64 zr0:64 Zc:320 KB:192 KEY:192 DK:384 RS:128 nf:9 SU:768 FT:512 ys:256 yn:144" % (WC, OWN[2]),
    "bfloat16": "ZB:256 xt:1024 bt:1024 at:2048 wt:512 uvs:32 uvt:1024 bbT:1024 EQ:2048 SC:1024 PB:256 PR:256 SCN:256 LE:1536 LC2:768 MK:512 H:512",
    "int32": "pI:8 ti:24 nbI:12 nbP:24 Ne:28 Ri:6 Di:9 Ji:3 Dj:12",
    "uint16": "UL:8 DL:32 FN:512 nbG:48 Lu:96 JD:8 KDL:24 nbp:24 nbo:12 nbe:4 nbD:24 nbK:12 FA:256 LST:6 LA:18 LO:18 EO:12 PO:30 J:12 SL0:4 SL1:4 SR0:9 SR1:9 FO:16",
}
SMALL = "C12:12 tf:12 GCOL:8 IC:16 ICS:8 TB:4 CK:32 C1:32 PADD:4 LS:8 SS:8 VP:96 PAYJ:4 OFF:192 ZN:4 Rf:4 R0:8 R1:8"
PART = {}
_n = 0
for _b in SMALL.split():
    PART[_b.split(":")[0]] = _n
    _n += int(_b.split(":")[1])
QBUF = "Q0:256 Qb:256 Qa:512 Qw:128 UV2:256 SND:288 W:%d PK0:%d PA1:768 PA2:768 FIN:256" % (WC, PW)
SCRATCH = {"eld": ("dram", [3, 128, 2], "float32"), "ps": ("psum", [128, 4096], "float32"), "KC": ("sbuf", [128, _n], "float32")}
for _d, _s in BUF.items():
    for _b in _s.split():
        SCRATCH[_b.split(":")[0]] = ("sbuf", [128, int(_b.split(":")[1])], _d)
for _b in QBUF.split():
    SCRATCH[_b.split(":")[0]] = ("sbuf", [128, int(_b.split(":")[1])], "float8_e4m3fn_x4")
    SCRATCH[_b.split(":")[0] + "s"] = ("sbuf", [128, int(_b.split(":")[1])], "uint8")
SEMAPHORES = "v s p gq d_nb d_nc d_x d_y d_p d_uv d_bb d_a d_w d_q d_m d_e d_nd d_out d_g d_l0 d_l1 d_l2 d_l3 d_l4 d_l5 r_e r_l r_c r_s0 r_s1 r_n0 r_n1 loc".split()


def rank_program(g, core, T, topo):
    rank = T.rank_of(core)
    if rank is None:
        return
    V, S, PE, Y = g.vector, g.scalar, g.tensor, g.sync
    queue = {"V": V, "S": S, "P": PE, "G": g, "Y": Y}
    sem_of = {"V": "v", "S": "s", "P": "p", "G": "gq"}
    count = {s: 0 for s in SEMAPHORES}
    total = {s: 0 for s in SEMAPHORES}
    know = {q: {} for q in queue}
    snaps, touched, calls = {}, {}, []

    def reg(name, c0, c1, p0=0, p1=128, st=1):
        if name in PART:
            return ("KC", p0, p1, c0 + PART[name], c1 + PART[name], st)
        return (name, p0, p1, c0, c1, st)

    def ap(r):
        n, p0, p1, c0, c1, st = r
        return T[n][p0:p1, c0:c1:st] if st > 1 else T[n][p0:p1, c0:c1]

    def meet(a, b):
        if a[0] == "ps":
            return a[3] // 512 == b[3] // 512
        if a[2] <= b[1] or b[2] <= a[1] or a[4] <= b[3] or b[4] <= a[3]:
            return False
        return not (a[5] == b[5] > 1 and a[3] % a[5] != b[3] % b[5])

    def order(q, reads, writes, acc=False):
        want = {}
        for r, w in [(r, False) for r in reads] + [(r, True) for r in writes]:
            for (o, ow, oq, sem, val) in touched.get(r[0], []):
                if meet(r, o) and not (acc and oq == q and r[0] == "ps") and (ow or ((w or r[0] == "ps") and oq != q)):
                    if know[q].get(sem, 0) < val:
                        want[sem] = max(want.get(sem, 0), val)
        for s in sorted(want):
            if any(o != s and snaps.get((o, want[o]), {}).get(s, 0) >= want[s] for o in want):
                del want[s]
        for s, val in want.items():
            queue[q].wait_ge(T.sem[s], val)
            know[q][s] = max(know[q].get(s, 0), val)
            for k, x in snaps.get((s, val), {}).items():
                know[q][k] = max(know[q].get(k, 0), x)

    def note(reads, writes, q, sem, val):
        for r in reads:
            touched.setdefault(r[0], []).append((r, False, q, sem, val))
        for r in writes:
            touched.setdefault(r[0], []).append((r, True, q, sem, val))

    def op(q, fn, reads, writes, acc=False):
        s = sem_of[q]

        def emit():
            order(q, reads, writes, acc)
            count[s] += 1
            fn().then_inc(T.sem[s], 1)
            snaps[(s, count[s])] = dict(know[q])
            note(reads, writes, q, s, count[s])
        calls.append(emit)

    def dma(q, sem, out, in_, reads, writes):
        total[sem] += 16

        def emit():
            order(q, reads, writes)
            count[sem] += 16
            queue[q].dma_start(out, in_).then_inc(T.sem[sem], 16)
            note(reads, writes, "dma", sem, total[sem])
        calls.append(emit)

    def arrive(sem, n, *writes):
        calls.append(lambda: note([], writes, "far", sem, n))

    def sc(x):
        return ap(x) if isinstance(x, tuple) else x

    def act(out, in_, f, bias=None, scale=None, accum=None):
        kw = {}
        if bias is not None: kw["bias"] = sc(bias)
        if scale is not None: kw["scale"] = sc(scale)
        if accum is not None: kw["accum_out"] = ap(accum)
        op("S", lambda: S.activation(ap(out), ap(in_), f, **kw), [in_] + [x for x in (bias, scale) if isinstance(x, tuple)], [out] + ([accum] if accum else []))

    def copy(out, in_, q="V"):
        if q == "V":
            op("V", lambda: V.tensor_copy(ap(out), ap(in_)), [in_], [out])
        else:
            act(out, in_, AF.Copy)

    def ts(out, in_, s1, op0, s2=None, op1=None):
        rd = [in_] + [x for x in (s1, s2) if isinstance(x, tuple)]
        if op1 is None:
            op("V", lambda: V.tensor_scalar(ap(out), ap(in_), sc(s1), None, op0), rd, [out])
        else:
            op("V", lambda: V.tensor_scalar(ap(out), ap(in_), sc(s1), sc(s2), op0, op1), rd, [out])

    def tt(out, a, b, o):
        op("V", lambda: V.tensor_tensor(ap(out), ap(a), ap(b), o), [a, b], [out])

    def tt_by(out, win, off, b, o):
        op("V", lambda: V.tensor_tensor(ap(out), ap(win).indirect(ap(off)), ap(b), o), [win, off, b], [out])

    def scan(out, a, b):
        op("V", lambda: V.tensor_tensor_scan(ap(out), ap(a), ap(b), 0.0, OP.add, OP.add), [a, b], [out])

    def turn(out, in_):
        op("V", lambda: V.transpose(ap(out), ap(in_)), [in_], [out])

    def fill(out, x):
        op("V", lambda: V.memset(ap(out), x), [], [out])

    def least(o, i):
        op("V", lambda: V.tensor_reduce(ap(o), ap(i), AxisListType.X, OP.min, apply_absolute_value=True), [i], [o])

    def iota(out, pattern, base, mult=0):
        if SCRATCH[out[0]][2] == "int32":
            op("G", lambda: g.iota(ap(out), pattern, base, mult), [], [out])
        else:
            op("G", lambda: g.iota(ap(out), pattern, base, mult, allow_small_or_imprecise_dtypes=True), [], [out])

    def gather(out, win, off, q="V"):
        if q == "V":
            op("V", lambda: V.tensor_copy(ap(out), ap(win).indirect(ap(off))), [win, off], [out])
        else:
            op("S", lambda: S.activation(ap(out), ap(win).indirect(ap(off)), AF.Copy), [win, off], [out])

    def scatter(win, off, in_):
        op("V", lambda: V.tensor_copy(ap(win).indirect(ap(off)), ap(in_)), [in_, off], [win])

    def pick(dst, c0, c1, src, w1, off):
        a, b = reg(dst, c0, c1), reg(src, 0, w1)
        op("V", lambda: V.tensor_copy(ap(a).bitcast(dt.uint32), ap(b).bitcast(dt.uint32).indirect(ap(off))), [b, off], [a])
        gather(reg(dst + "s", c0, c1), reg(src + "s", 0, w1), off, "S")

    def both(q, c0, c1):
        return [reg(q, c0, c1), reg(q + "s", c0, c1)]

    def quant(q, c0, c1, t, e0=0):
        e1 = e0 + 4 * (c1 - c0)
        op("V", lambda: V.quantize_mx(T[q][:, c0:c1], T[q + "s"][:, c0:c1], T[t][:, e0:e1]), [reg(t, e0, e1)], both(q, c0, c1))

    def mm(bank, a, a0, b, b0, n, start=True, stop=True):
        o = reg("ps", 512 * bank, 512 * bank + n)
        op("P", lambda: PE.matmul_mx(ap(o), T[a][:, a0:a0 + 128], T[a + "s"][:, a0:a0 + 128], T[b][:, b0:b0 + n], T[b + "s"][:, b0:b0 + n], start, stop), both(a, a0, a0 + 128) + both(b, b0, b0 + n), [o], not start)

    def ps(bank, c0, c1, p0=0, p1=128):
        return reg("ps", 512 * bank + c0, 512 * bank + c1, p0, p1)

    def lanes(src):
        others = [c for c in T.cores if c != src]
        off = [c for c in others if topo.chip(c) != topo.chip(src)]
        on = [c for c in others if topo.chip(c) == topo.chip(src)]
        out = topo.engines(src, off[0])
        inn = [e for e in topo.engines(src, on[0]) if e not in out]
        m = {}
        for i, c in enumerate(off): m[c] = out[i * (len(out) // len(off)):(i + 1) * (len(out) // len(off))]
        for i, c in enumerate(on): m[c] = inn[i * (len(inn) // len(on)):(i + 1) * (len(inn) // len(on))]
        return m

    mine = lanes(core)
    sources = [T.cores[(rank + 1 + i) % 4] for i in range(3)]

    def slot(dst):
        return (rank - T.rank_of(dst) - 1) % 4

    def send(sem, pair, reads):
        def emit():
            order("G", reads, [])
            tr = []
            for c in mine:
                rid, pid, _ = topo.addr(c)
                s, d = pair(c)
                tr.append(RemoteDMATransfer(dst_ids=[DstId(rid=rid, pnc=pid)], dma_engine_mask=sum(1 << e for e in mine[c]), remote_sem=T.sem[sem], src=s, dst=d))
                count["loc"] += len(mine[c])
            g.remote_dma_fused(tr, local_sem=T.sem.loc)
        calls.append(emit)

    incoming = sum(len(lanes(c)[core]) for c in sources)

    def cb(name, c0, c1):
        return T[name][:, c0:c1].bitcast(dt.uint8)

    def ship(sem, q, s0, n, dst, c0, c1):
        send(sem, lambda c: (cb(q, s0(c), s0(c) + n), cb("W", dst(c), dst(c) + n)), [reg(q, c0, c1)])
        send(sem, lambda c: (T[q + "s"][:, s0(c):s0(c) + n], T.Ws[:, dst(c):dst(c) + n]), [reg(q + "s", c0, c1)])

    def as_list(sem, l, c, row, r0):
        dma("Y", sem, T[l][:, c:c + 16], T[row][0:128:16, r0:r0 + 256], [reg(row, r0, r0 + 256)], [reg(l, c, c + 16)])

    def ti(i):
        return reg("ti", i, i + 1)

    def tf(i):
        return reg("tf", i, i + 1)

    for h in range(2):
        for a in range(4):
            p0, b0 = 32 * a + 16 * h, 24 * (a // 2)
            dma("YS"[h], "d_nb", T.nbP[p0:p0 + 16, :], T.nb[:, b0:b0 + 24], [], [reg("nbP", 0, 24, p0, p0 + 16)])
    for h in range(2):
        dma("Y", ("d_x", "d_y")[h], T.xt[:, 512 * h:512 * h + 512], T.x[:, 512 * h:512 * h + 512], [], [reg("xt", 512 * h, 512 * h + 512)])
    dma("S", "d_uv", T.uvs[:, 0:4], T.u[:, 0:4], [], [reg("uvs", 0, 4)])
    dma("S", "d_uv", T.uvs[:, 16:20], T.v[:, 0:4], [], [reg("uvs", 16, 20)])
    for h in range(2):
        for a in range(4):
            p0 = 32 * a + 16 * h
            dma("Y", "d_nc", T.nbI[p0:p0 + 16, :], T.nb[:, 12 * a:12 * a + 12], [], [reg("nbI", 0, 12, p0, p0 + 16)])
    dma("Y", "d_bb", T.bt[:], T.bb[:], [], [reg("bt", 0, 1024)])
    dma("Y", "d_a", T.at[:], T.a[:], [], [reg("at", 0, 2048)])
    dma("Y", "d_w", T.wt[:], T.w[:], [], [reg("wt", 0, 512)])
    pI = reg("pI", 0, 1)
    iota(reg("pI", 0, 8), [[0, 8]], 0, 1)
    iota(reg("ID", 0, 256), [[1, 256]], 0)
    iota(reg("C12", 0, 12), [[1, 3], [48, 4]], 0)
    for q in range(3):
        iota(reg("EM", 256 * q, 256 * q + 256), [[0, 256]], 0)
    act(reg("M", 256 * rank, 256 * rank + 256), reg("ID", 0, 256), AF.Copy)
    for k, q in ((1, "V"), (2, "S"), (3, "V"), (4, "S")):
        n = min(256, WC - 256 * k)
        if q == "V":
            ts(reg("ID", 256 * k, 256 * k + n), reg("ID", 0, n), 256.0 * k, OP.add)
        else:
            act(reg("ID", 256 * k, 256 * k + n), reg("ID", 0, n), AF.Identity, bias=256.0 * k)
    ts(ti(0), pI, 96, OP.bitwise_and)
    ts(ti(1), pI, 31, OP.bitwise_and)
    ts(ti(2), pI, 15, OP.bitwise_and)
    ts(reg("ti", 8, 16), reg("pI", 0, 8), 3, OP.bitwise_and)
    ts(tf(4), ti(0), 7.0, OP.mult)
    copy(tf(3), ti(2))
    ts(tf(2), ti(0), 2048.0, OP.mult, -MID, OP.add)
    tt(tf(0), tf(4), pI, OP.add)
    copy(tf(5), ti(1))
    ts(tf(8), ti(0), 2.0, OP.mult)
    tt(tf(9), tf(8), ti(1), OP.add)
    ts(tf(6), ti(1), 32.0, OP.add)
    ts(tf(7), ti(2), 3.0, OP.mult)
    copy(reg("UL", 0, 8), reg("ti", 8, 16))
    fill(reg("ZB", 0, 256), 0.0)
    fill(reg("CK", 0, 32), STEP)
    fill(reg("C1", 0, 32), 1.0)
    fill(reg("H", 4 * K, 512), 0.0)
    fill(reg("E1", OWN[0] + 128, FAR), 0.0)
    for a in range(4):
        fill(reg("PADD", 0, 1, 32 * a, 32 * a + 32), float(FAR + LC * ((a - rank - 1) % 4 % 3) - 1))
    act(reg("GCOL", 0, 8), reg("ID", 0, 8), AF.Identity, scale=32.0, bias=tf(0))
    act(reg("IC", 0, 16), reg("ID", 0, 16), AF.Identity, scale=16.0, bias=tf(3))
    act(reg("ICS", 0, 8), reg("IC", 0, 8), AF.Identity, scale=-1.0, bias=-0.5)
    copy(reg("nbp", 0, 24), reg("nbP", 0, 24))
    gather(reg("FRA", 0, 192), reg("ID", 0, 1024), reg("nbp", 0, 12))
    gather(reg("FRB", 0, 192), reg("ID", 0, 1024), reg("nbp", 12, 24), "S")
    copy(reg("FA", 0, 64), reg("FRA", 2, 192, st=3))
    copy(reg("FA", 64, 128), reg("FRB", 2, 192, st=3))
    copy(reg("FA", 128, 256, 0, 64), reg("FA", 0, 128, 64, 128))
    copy(reg("FA", 128, 256, 64, 128), reg("FA", 0, 128, 0, 64))
    for k in range(2):
        o = 512 * k
        gather(reg("uvt", o, o + 128), reg("uvs", 16 * k, 16 * k + 4), reg("UL", 0, 8), "S")
        copy(reg("uvt", o + 128, o + 256), reg("uvt", o, o + 128), "S")
        copy(reg("uvt", o + 256, o + 512), reg("uvt", o, o + 256), "S")
    for h in range(2):
        quant("Q0", 128 * h, 128 * h + 128, "xt", 512 * h)
    quant("UV2", 0, 128, "uvt")
    quant("UV2", 128, 256, "uvt", 512)
    for c in range(2):
        mm(c, "Q0", 128 * c, "UV2", 0, 128)
    for c in range(2):
        copy(reg("ec", c, c + 1), ps(c, 0, 1), "S")
    send("r_e", lambda c: (T.ec[:, 0:2], T.eld[slot(c)]), [reg("ec", 0, 2)])
    arrive("r_e", incoming, reg("eld", 0, 3))
    dma("Y", "d_q", cb("W", 0, 256), cb("Q0", 0, 256), [reg("Q0", 0, 256)], [reg("W", 0, 256)])
    dma("Y", "d_q", T.Ws[:, 0:256], T.Q0s[:, 0:256], [reg("Q0s", 0, 256)], [reg("Ws", 0, 256)])
    dma("Y", "d_p", cb("PK0", 3 * K, PW), cb("Q0", 0, PW - 3 * K), [reg("Q0", 0, PW - 3 * K)], [reg("PK0", 3 * K, PW)])
    dma("Y", "d_p", T["PK0s"][:, 3 * K:PW], T.Q0s[:, 0:PW - 3 * K], [reg("Q0s", 0, PW - 3 * K)], [reg("PK0s", 3 * K, PW)])
    for c in range(8):
        eq = reg("EQ", 256 * c, 256 * c + 256)
        ts(eq, reg("FA", 0, 256), reg("GCOL", c, c + 1), OP.is_equal)
        if c < 8 - SCN_S:
            scan(reg("SC", 128 * c, 128 * c + 128), reg("EQ", 256 * c, 256 * c + 128), reg("EQ", 256 * c + 128, 256 * c + 256))
            n = reg("SC", 128 * c + 127, 128 * c + 128)
        else:
            n = reg("SS", c, c + 1)
            act(reg("SJ", 0, 256), eq, AF.Copy, accum=n)
        act(reg("PB", 32 * c, 32 * c + 32), reg("ZB", 0, 32), AF.Sign, bias=n)
    turn(reg("PR", 0, 256), reg("PB", 0, 256))
    scan(reg("SCN", 0, 256), reg("PR", 0, 256), reg("ZB", 0, 256))
    nv = 6 - LEN_S
    for c in range(nv):
        ts(reg("LE", 256 * c, 256 * c + 256), reg("SCN", 0, 256), reg("IC", c, c + 1), OP.is_le)
        scan(reg("LC2", 128 * c, 128 * c + 128), reg("LE", 256 * c, 256 * c + 128), reg("LE", 256 * c + 128, 256 * c + 256))
    for c in range(nv, 6):
        act(reg("LJ", 256 * (c % 3), 256 * (c % 3) + 255), reg("SCN", 0, 255), AF.Sign, bias=reg("ICS", c, c + 1), accum=reg("LS", c, c + 1))
    ts(reg("LST", 0, nv), reg("LC2", 127, 128 * nv, st=128), 255.0, OP.min)
    ts(reg("LST", nv, 6), reg("LS", nv, 6), -0.5, OP.mult, 127.5, OP.add)
    send("r_l", lambda c: (T.LST[:, 0:6], T.LA[:, 6 * slot(c):6 * slot(c) + 6]), [reg("LST", 0, 6)])
    arrive("r_l", incoming, reg("LA", 0, 18))
    for d in range(4):
        dma("Y", "d_e", T.EM[32 * d:32 * d + 1, 0:768], T.eld[0:3], [reg("eld", 0, 3)], [reg("EM", 0, 768, 32 * d, 32 * d + 1)])
    act(reg("SLf", 0, 256), reg("SCN", 0, 256), AF.Identity, bias=reg("PADD", 0, 1))
    for q in range(4):
        if q != rank:
            for d in range(4):
                dma("Y", "d_m", T.M[32 * d:32 * d + 32, 256 * q:256 * q + 256], T.SLf[32 * q:32 * q + 32, :], [reg("SLf", 0, 256, 32 * q, 32 * q + 32)], [reg("M", 256 * q, 256 * q + 256, 32 * d, 32 * d + 32)])
    copy(reg("nbo", 0, 12), reg("nbI", 0, 12))
    for h in range(2):
        ts(reg("KDL", h, 24, st=2), reg("C12", 0, 12), tf(7), OP.add)
    gather(reg("FR", 0, 192), reg("ID", 0, 1024), reg("nbo", 0, 12), "S")
    gather(reg("PDn", 0, 256), reg("FR", 0, 192), reg("KDL", 0, 16), "S")
    gather(reg("PDn", 256, 384), reg("FR", 0, 192), reg("KDL", 16, 24), "S")
    turn(reg("PTn", 0, 256), reg("PDn", 0, 256))
    turn(reg("PTn", 256, 384), reg("PDn", 256, 384))
    ts(reg("nbK", 0, 8), reg("PTn", 0, 256, st=32), float(-256 * rank), OP.add)
    copy(reg("nbD", 16, 24), reg("PTn", 256, 384, st=16))
    copy(reg("nbK", 8, 12), reg("PTn", 256, 384, st=32))
    m0, m1, n0, n1, n2, n3, n4 = [reg("Ne", 4 * i, 4 * i + 4) for i in range(7)]
    ts(m0, reg("PTn", 256, 384, st=32), float(1024 - 256 * (rank + 1)), OP.add)
    ts(m1, m0, 1023, OP.bitwise_and)
    ts(n0, m0, 127, OP.bitwise_and)
    ts(n1, m0, 7, OP.logical_shift_right, 1, OP.bitwise_and)
    tt(n2, n0, m1, OP.add)
    ts(n3, n1, -127.0, OP.mult)
    tt(n4, n2, n3, OP.add)
    copy(reg("nbe", 0, 4), n4)
    quant("Qb", 0, 256, "bt")
    mm(5, "UV2", 0, "Q0", 0, 256)
    mm(4, "UV2", 128, "Qb", 0, 256)
    for b in range(2):
        ts(reg("Ft", 64 * b, 64 * b + 64), reg("ID", 0, 64), tf(5 + b), OP.is_lt, 2.0 ** -24, OP.mult)
    copy(reg("E1", 0, 256), ps(5, 0, 256), "S")
    for a in range(4):
        copy(reg("fb", 0, 64, 32 * a, 32 * a + 32), ps(4, 64 * a, 64 * a + 64, 32 * a, 32 * a + 32), "S")
    act(reg("Fm", 0, 128), reg("Ft", 0, 128), AF.Identity, bias=PRED)
    copy(reg("Mo", 0, 256), reg("ID", 0, 256), "S")
    for k in range(2):
        for i in range(2):
            ts(reg("FN", 256 * k + 64 * i, 256 * k + 64 * i + 64), reg(("FRA", "FRB")[i], k, 192, st=3), float(-256 * rank), OP.add)
        copy(reg("FN", 256 * k + 128, 256 * k + 256, 0, 64), reg("FN", 256 * k, 256 * k + 128, 64, 128))
    for h in range(2):
        for k in range(3):
            f, o = ("FN", 256 * k) if k < 2 else ("FA", 0)
            dma("Y", "d_g", T.nbG[64 * h:64 * h + 64, 16 * k:16 * k + 16], T[f][0:64:16, o:o + 256], [reg(f, o, o + 256, 0, 64)], [reg("nbG", 16 * k, 16 * k + 16, 64 * h, 64 * h + 64)])
    for h in range(2):
        copy(reg("DL", h, 32, st=2), reg("IC", 0, 16))
    iota(reg("VP", 0, 96), [[0, 2], [1, 48]], OWN[2])
    iota(reg("OFF", 0, 96), [[-16, 3], [0, 2], [-1, 16]], 0)
    for k in range(2):
        ts(reg("PAYJ", k, k + 1), tf(9), 1.0 / STEP1, OP.mult, k * 32.0 / STEP1, OP.add)
    act(reg("OFF", 96, 192), reg("OFF", 0, 96), AF.Identity, bias=reg("PAYJ", 1, 2))
    act(reg("OFF", 0, 96), reg("OFF", 0, 96), AF.Identity, bias=reg("PAYJ", 0, 1))
    act(reg("JB", 0, 64), reg("ID", 0, 64), AF.Identity, scale=1024.0, bias=tf(2))
    act(reg("TB", 0, 4), reg("IC", 0, 4), AF.Identity, scale=-STEP, bias=MID)
    for t in range(4):
        copy(reg("bbT", 256 * t, 256 * t + 256), reg("bt", t, 1024, st=4), "S")
    for d in range(4):
        copy(reg("LO", 0, 18, 32 * d, 32 * d + 32), reg("LA", 0, 18, 32 * rank, 32 * rank + 32))
    pick("SND", 0, 288, "Q0", 256, reg("LO", 0, 18))
    ship("r_c", "SND", lambda c: LC * sources.index(c), LC, lambda c: FAR + LC * slot(c), 0, 3 * LC)
    arrive("r_c", 2 * incoming, *both("W", FAR, FAR + 3 * LC))

    z0, z1, z2, EG = reg("z0", 0, 64), reg("z1", 0, 64), reg("z2", 0, 64), reg("EG", 0, 64)
    M = reg("M", 0, 1024)
    Mo = reg("Mo", 0, 256)
    C005 = 13421773.0 * 2.0 ** -28

    def payload01():
        gather(reg("PC", 0, 128), Mo, reg("nbK", 0, 8), "S")
        act(reg("zK", 0, 64), reg("PC", 64, 128), AF.Identity, scale=512.0, bias=-MID)
        tt(reg("PAB", 0, 64), reg("zK", 0, 64), reg("PC", 0, 64), OP.add)
        turn(reg("PAYT", 0, 64), reg("PAB", 0, 64))

    def payload2():
        gather(reg("PC", 128, 192), M, reg("nbK", 8, 12), "S")
        tt(reg("PAB", 64, 128), reg("PC", 128, 192), reg("JB", 0, 64), OP.add)
        turn(reg("PAYT", 64, 128), reg("PAB", 64, 128))

    quant("Qw", 0, 128, "wt")
    mm(5, "Qw", 0, "Q0", 0, 256)
    copy(reg("ys", 0, 256), ps(5, 0, 256), "S")
    for t in range(R):
        SL, SR = "SL%d" % t, "SR%d" % t
        PO, J, nf = reg("PO", 10 * t, 10 * t + 9), reg("J", 4 * t, 4 * t + 3), reg("nf", 3 * t, 3 * t + 3)
        nk, Jn = (2, reg("Ji", 0, 3)) if t == 0 else (1, reg("Dj", 0, 3))
        wend, w0 = WEND[t], OWN[t]
        if t == 0:
            gather(EG, reg("E1", 0, 256), reg("nbK", 0, 4))
            tt_by(z0, reg("E1", 0, 256), reg("nbK", 4, 8), EG, OP.add)
            tt_by(z1, reg("EM", 0, 768), reg("nbe", 0, 4), z0, OP.add)
            payload01()
            payload2()
        else:
            a0 = ARR[t - 1]
            mm(6, "UV2", 0, "W", a0, 3 * K)
            copy(reg("E1", a0, a0 + 3 * K), ps(6, 0, 3 * K))
            tt_by(z1, reg("E1", FAR, wend), reg("EO", 8, 12), z0, OP.add)
        tt(z2, z1, reg("fb", 0, 64), OP.subtract)
        act(reg("zr", 0, 64), z2, AF.Abs, bias=TINY)
        turn(reg("ZT", 0, 64), reg("zr", 0, 64))
        zr, zs = "zr", "z2"
        if t == 0:
            for b in range(2):
                ts(reg("zB", 32 * b, 32 * b + 32), reg("C1", 0, 32), reg("ZT", 32 * b, 32 * b + 1), OP.mult)
            turn(reg("zr0", 0, 64), reg("zB", 0, 64))
            zr = zs = "zr0"
        for b in range(2):
            tt(reg("Zc", 256 * b, 256 * b + 64), reg(zr, 0, 64), reg("Fm", 64 * b, 64 * b + 64), OP.mult)
        for q, d, s, w, x in (("S", 0, 2, 2, 2), ("S", 2, 0, 2, 2), ("S", 0, 1, 1, 1), ("S", 1, 0, 1, 1), ("S", 2, 3, 1, 1), ("S", 3, 2, 1, 1), ("S", 0, 3, 1, 3), ("V", 3, 0, 1, 3), ("V", 1, 2, 1, 3), ("S", 2, 1, 1, 3)):
            o = reg("Zc", 64 * x, 64 * x + 64, 32 * d, 32 * d + 32 * w)
            i = reg(zs if q == "S" else zr, 0, 64, 32 * s, 32 * s + 32 * w)
            f = PRED if s > d else 1.0
            if q == "S":
                if t == 0:
                    act(o, i, AF.Copy, scale=f)
                else:
                    act(o, i, AF.Abs, scale=f, bias=TINY * f)
            elif s > d:
                ts(o, i, f, OP.mult)
            else:
                copy(o, i)
        ts(reg("ZN", 0, 1), reg("ZT", 32, 33), -UP, OP.mult)
        ts(reg("MK", 256, 256 + VPART), reg("Zc", 64, 64 + VPART), reg("ZT", 32, 33), OP.is_ge, 1.0, OP.subtract)
        act(reg("MK", 256 + VPART, 512), reg("Zc", 64 + VPART, 320), AF.Sign, scale=UP, bias=reg("ZN", 0, 1))
        for h in range(2):
            ts(reg("MK", 128 * h, 128 * h + 128), reg("Zc", 128 * h, 128 * h + 128), reg("ZT", 0, 1), OP.is_ge)
        act(reg("SJ", 0, 256), reg("MK", 256, 512), AF.Sign, bias=1.0, accum=reg("SS", 0, 1))
        scan(reg("RS", 0, 128), reg("MK", 0, 128), reg("MK", 128, 256))
        if t == 0:
            for k in range(2):
                o = 64 * k
                ts(reg("KB", o, o + 32), reg("CK", 0, 32), reg("RS", 127, 128), OP.mult, reg("PAYT", o, o + 1), OP.add)
                act(reg("KB", o + 32, o + 64), reg("CK", 0, 32), AF.Identity, scale=reg("SS", 0, 1), bias=reg("PAYT", o + 32, o + 33))
            turn(reg("KEY", 0, 128), reg("KB", 0, 128))
            for c in range(3):
                o, tb = reg("DK", 128 * c, 128 * c + 128), reg("TB", c, c + 1)
                if c == 2:
                    ts(o, reg("KEY", 0, 128), tb, OP.add)
                else:
                    act(o, reg("KEY", 0, 128), AF.Identity, bias=tb)
            for c in range(3):
                for k in range(2):
                    least(reg("R0", 3 * k + c, 3 * k + c + 1), reg("DK", 128 * c + 64 * k, 128 * c + 64 * k + 64))
        else:
            for c in range(3):
                o = 64 * c
                ts(reg("KB", o, o + 32), reg("OFF", 32 * c, 32 * c + 32), reg("RS", 127, 128), OP.add)
                act(reg("KB", o + 32, o + 64), reg("OFF", 96 + 32 * c, 128 + 32 * c), AF.Identity, bias=reg("SS", 0, 1))
            for c in range(3):
                o = 64 * c
                turn(reg("KEY", o, o + 64), reg("KB", o, o + 64))
                least(reg("R0", c, c + 1), reg("KEY", o, o + 64))
        n3 = 3 * nk
        for d in range(2):
            tt(reg("R1", 0, n3, 64 * d, 64 * d + 64), reg("R0", 0, n3, 64 * d, 64 * d + 64), reg("R0", 0, n3, 64 - 64 * d, 128 - 64 * d), OP.min)
        Rd = "Ri" if t == 0 else "Rf"
        for d in range(4):
            s = d ^ 1
            tt(reg(Rd, 0, n3, 32 * d, 32 * d + 32), reg("R1", 0, n3, 32 * d, 32 * d + 32), reg("R1", 0, n3, 32 * s, 32 * s + 32), OP.min)
        if t == 0:
            ts(reg("Di", 0, 3), reg("Ri", 0, 3), 511, OP.bitwise_and)
            ts(reg("Di", 3, 6), reg("Ri", 0, 3), 9, OP.logical_shift_right)
            ts(reg("Di", 6, 9), reg("Ri", 3, 6), 1023, OP.bitwise_and)
            copy(PO, reg("Di", 0, 9))
            pick("PK0", 0, 144, "W", wend, PO)
            ts(Jn, reg("Ri", 3, 6), 10, OP.logical_shift_right)
            copy(J, Jn)
        else:
            ts(J, reg("Rf", 0, 3), STEP1, OP.mult)
            ts(Jn, reg("Rf", 0, 3), STEP1, OP.mult)
        if t < 2:
            ts(reg(SL, 0, 3), Jn, float(256 * rank), OP.add)
            send("r_s%d" % t, lambda c, SL=SL, SR=SR: (T[SL][:, 0:3], T[SR][:, 3 * slot(c):3 * slot(c) + 3]), [reg(SL, 0, 3)])
            arrive("r_s%d" % t, incoming, reg(SR, 0, 9))
        if t < 2:
            scatter(Mo, J, reg("ID", w0, w0 + K))
        else:
            ts(reg("Dj", 8, 11), Jn, 240, OP.bitwise_and)
            tt(reg("Dj", 4, 7), Jn, reg("Dj", 8, 11), OP.add)
            copy(reg("JD", 0, 3), reg("Dj", 4, 7))
            ts(reg("JD", 3, 6), reg("Dj", 4, 7), 16.0, OP.add)
            scatter(reg("MoD", 0, 512), reg("JD", 0, 6), reg("VP", 0, 96))
            for h in range(4):
                turn(reg("FT", 128 * h, 128 * h + 128), reg("MoD", 128 * h, 128 * h + 128))
            for h in range(2):
                copy(reg("FO", 8 * h, 8 * h + 8), reg("FT", 256 * h, 256 * h + 256, st=32))
        if t == 0:
            quant("Qa", 0, 256, "at")
            quant("Qa", 256, 512, "at", 1024)
            for b in range(4 - INP):
                mm(b, "Qa", 128 * b, "PK0", 0, 3 * K)
            for b in range(4 - INP, 4):
                for k in range(3):
                    mm(b, "Qa", 128 * b, "PK0", K * k, 128, k == 0, k == 2)
            for b in range(4):
                s0, s1, s2, s3 = [reg("SU", 192 * k + K * b, 192 * k + K * b + K) for k in range(4)]
                if b < 4 - INP:
                    copy(s0, ps(b, 0, K), "S")
                    tt(s1, ps(b, K, 2 * K), s0, OP.add)
                    tt(s2, ps(b, 2 * K, 3 * K), s1, OP.add)
                else:
                    s2 = ps(b, 0, K)
                act(s3, s2, AF.Copy, scale=C005)
                tt_by(reg("H", b, 4 * K, st=4), reg("bbT", 256 * b, 256 * b + 256), J, s3, OP.add)
        else:
            for b in range(4):
                gather(reg("G4", K * b, K * b + K), reg("bbT", 256 * b, 256 * b + 256), J, "S")
            for b in range(4):
                tt_by(reg("H", b, 4 * K, st=4), reg("ST", 256 * b, 256 * b + 256), J, reg("G4", K * b, K * b + K), OP.add)
        if t == 0:
            mm(7, "UV2", 0, "W", FAR, 3 * LC)
            copy(reg("E1", FAR, FAR + 3 * LC), ps(7, 0, 3 * LC), "S")
        quant("W", w0, w0 + 128, "H")
        if t < 2:
            ship("r_n%d" % t, "W", lambda c, w0=w0: w0, K, lambda c, t=t: ARR[t] + K * slot(c), w0, w0 + K)
            arrive("r_n%d" % t, 2 * incoming, *both("W", ARR[t], ARR[t] + 3 * K))
            u = t + 1
            PA = "PA%d" % u
            mm(7, "UV2", 0, "W", w0, 128)
            copy(reg("en", K * t, K * t + K), ps(7, 0, K), "S")
            scatter(reg("E1", 0, 256), J, reg("en", K * t, K * t + K))
            gather(EG, reg("E1", 0, 256), reg("nbK", 0, 4))
            tt_by(z0, reg("E1", 0, 256), reg("nbK", 4, 8), EG, OP.add)
            w = 256 // NP
            for k in range(2):
                gather(reg("LRo", 256 * k, 256 * k + 256), Mo, reg("nbG", 16 * k, 16 * k + 16), "S")
                as_list("d_l%d" % (3 * t + k), "LIo", 32 * t + 16 * k, "LRo", 256 * k)
                o = 48 * t + 16 * k
                copy(reg("Lu", o, o + 16), reg("LIo", 32 * t + 16 * k, 32 * t + 16 * k + 16))
                for h in range(NP):
                    pick(PA, 256 * k + w * h, 256 * k + w * h + w, "W", w0 + K, reg("Lu", o + w // 16 * h, o + w // 16 * (h + 1)))
                for b in range(4):
                    mm(b, "Qa", 128 * b, PA, 256 * k, 256, k == 0, False)
            scatter(M, reg(SR, 0, 9), reg("ID", ARR[t], ARR[t] + 3 * K))
            gather(reg("PD", 256, 384), M, reg("nbD", 16, 24), "S")
            turn(reg("PT", 256, 384), reg("PD", 256, 384))
            ts(reg("EO", 8, 12), reg("PT", 256, 384, st=32), float(-FAR), OP.add)
            gather(reg("LRf", 0, 256), M, reg("nbG", 32, 48), "S")
            as_list("d_l%d" % (3 * t + 2), "LIf", 16 * t, "LRf", 0)
            o = 48 * t + 32
            copy(reg("Lu", o, o + 16), reg("LIf", 16 * t, 16 * t + 16))
            for h in range(NP):
                pick(PA, 512 + w * h, 512 + w * h + w, "W", WEND[u], reg("Lu", o + w // 16 * h, o + w // 16 * (h + 1)))
            for b in range(4):
                mm(b, "Qa", 128 * b, PA, 512, 256, False, True)
            for b in range(4):
                act(reg("ST", 256 * b, 256 * b + 256), ps(b, 0, 256), AF.Copy, scale=C005)
        else:
            for h in range(2):
                pick("FIN", 128 * h, 128 * h + 128, "W", WC, reg("FO", 8 * h, 8 * h + 8))
        copy(nf, Jn)
        for c in range(3):
            dma("Y", "d_nd", T.nd[t:t + 1, 16 * c:16 * c + 16], T.nf[0:16, 3 * t + c:3 * t + c + 1], [nf], [])
        if t == 1:
            for h in range(4):
                gather(reg("MoD", 128 * h, 128 * h + 128), Mo, reg("DL", 8 * h, 8 * h + 8), "S")
        mm(4, "Qw", 0, "W", w0, 128)
        copy(reg("yn", K * t, K * t + K), ps(4, 0, K), "S")
        scatter(reg("ys", 0, 256), J, reg("yn", K * t, K * t + K))

    dma("Y", "d_out", T.oc[:, 0:1024], cb("FIN", 0, 256), [reg("FIN", 0, 256)], [])
    for k in range(4):
        dma("YYSS"[k], "d_out", T.osc[4 * k:4 * k + 4, 0:256], T.FINs[32 * k:32 * k + 4, 0:256], [reg("FINs", 0, 256)], [])
    for h in range(2):
        dma("YS"[h], "d_out", T.y[:, 128 * h:128 * h + 128], T.ys[:, 128 * h:128 * h + 128], [reg("ys", 128 * h, 128 * h + 128)], [])
    for i in ORDER:
        calls[i]()
    for s in ("v", "s", "p", "gq", "d_q", "d_g", "d_nd", "d_out", "loc"):
        if know["G"].get(s, 0) < count[s]:
            g.wait_ge(T.sem[s], count[s])
